import numpy as np, ml_dtypes
CORES = [9,25,41,57]
N = 4
BF = ml_dtypes.bfloat16
B, LE, LP, M, ST, RO, TH = 2112, 176, 80, 160, 2, 2, 65536
E = RO * LE + LP
W = B + RO * ST * M
def parts(rng):
    c = (65536 * rng.random((N, 8, 16, B)) * np.exp2(-1.0 * rng.integers(0, 7, (N, 8, 1, B)))).astype(np.int64)
    return c, rng.integers(0, B, (N, 8, 16, B))
def starts(rng, c, share):
    e = np.where(rng.random((N, 8, 1, E)) < share, rng.integers(0, 3, (N, 8, 1, E)), rng.integers(4, 9, (N, 8, 1, E)))
    c[..., B - E:] = (65536 * rng.random((N, 8, 16, E)) * np.exp2(-1.0 * e)).astype(np.int64)
    return c
def pack(c, s):
    return {"c0": np.ascontiguousarray(c.reshape(N, 128, B)).astype(np.int32), "s0": np.ascontiguousarray(s.reshape(N, 128, B)).astype(np.int32)}
def setup_inputs(rng):
    c, s = parts(rng)
    return pack(starts(rng, c, rng.choice(np.array([0.4, 0.7, 0.9, 1.0]), (N, 8, 1, 1))), s)
def setup_inputs_room(rng):
    c, s = parts(rng); c = starts(rng, c, 0.8)
    for q in range(N):
        for g in range(8):
            n = int(rng.choice(np.array([0, 1, M - 1, M, M + 1, LE]))); z = int(rng.choice(np.array([0, 1, LP - 1, LP, LP + 1, M])))
            if q == 0: n = (M, M + 1, LE, M - 1, M, 1, 0, M)[g]; z = (LP, LP + 1, M, LP - 1, 0, 1, 0, 1)[g]
            live = min(n, M); z = min(z, live)
            pool = rng.permutation(B - E); ch = pool[:ST * LE].reshape(ST, LE); nil = pool[ST * LE:ST * LE + 64]; ent = B - E + np.arange(LE)
            who = np.sort(rng.permutation(LE)[:n]); drop = np.delete(who[:M], rng.permutation(live)[:z])
            c[q, g][:, ent] = 0; c[q, g][:, ent[who]] = rng.integers(30000, 65536, (16, n))
            c[q, g][:, ch.reshape(-1)] = rng.integers(20000, 65536, (16, ST * LE)); c[q, g][:, nil] = 0
            c[q, g][:, ch[ST - 1][drop]] = 0
            prev = ent
            for st in range(ST):
                own = np.where(rng.random((16, LE)) < 0.4, ch[st][None, :], rng.choice(nil, (16, LE)))
                own[rng.integers(0, 16, LE), np.arange(LE)] = ch[st]
                s[q, g][:, prev] = own; prev = ch[st]
    return pack(c, s)
def setup_inputs_ties(rng):
    c, s = parts(rng); u = TH // 16
    one = (np.arange(16).reshape(1, 1, 16, 1) == rng.integers(0, 16, (N, 8, 1, B))).astype(np.int64)
    full = rng.random((N, 8, 1, B)) < np.array([0.05, 0.1, 0.2, 0.5, 0.05, 0.1, 0.2, 0.5]).reshape(1, 8, 1, 1)
    c = np.where(full, u, u - one); c = np.where(rng.random((N, 8, 1, B)) < 0.1, 0, c)
    big = rng.random((N, 8, 1, B)) < 0.1; big[:, :4] = False; c = np.where(big, 65535, c)
    c[..., B - E:] = np.where(rng.random((N, 8, 1, E)) < 0.7, 65535, u - one[..., B - E:] * rng.integers(0, 2, (N, 8, 1, E)))
    s[:, :4] = rng.integers(0, B - E, (N, 4, 16, B))
    return pack(c, s)
def setup_inputs_alike(rng):
    c, s = parts(rng); c = starts(rng, c, 0.85)
    for q in range(N):
        for g in range(8):
            h = (1, 2, 17, 64, 160, 300, B // 4, B)[(g + q) % 8]
            s[q, g] = rng.permutation(B)[:h][rng.integers(0, h, (16, B))]
    s = np.where(rng.random(s.shape) < 0.1, np.arange(B), s)
    ends = rng.random(s.shape) < 0.05; ends[:, ::2] = False
    s = np.where(ends, rng.choice(np.array([0, B - 1]), s.shape), s); c[:, 1::2, :, 0] = 65535; c[:, 1::2, :, B - 1] = 65535
    return pack(c, s)
def setup_inputs_links(rng):
    c, s = parts(rng); c = c >> 3; c = starts(rng, c, 0.9)
    near = rng.random(s.shape) < 0.5; near[:, ::2] = True
    return pack(c, np.where(near, rng.integers(B - E, B, s.shape), s))
def setup_inputs_spread(rng):
    c, s = parts(rng); lo = rng.choice(np.array([0.0, 6.0, 10.0]), (N, 8, 1, 1))
    c = np.minimum((np.exp2(lo + (16.0 - lo) * rng.random((N, 8, 1, B))) * rng.random((N, 8, 16, B))).astype(np.int64), 65535)
    c[:, :, :, B - E::7] = rng.integers(0, 65536, c[:, :, :, B - E::7].shape)
    v = rng.random((N, 4, 16, B)); s[:, 1::2] = np.minimum((B * v * v).astype(np.int64), B - 1)
    return pack(c, s)
def check_inputs(d):
    bad = []
    for k, hi in (("c0", 65535), ("s0", B - 1)):
        if np.min(d[k]) < 0 or np.max(d[k]) > hi: bad.append("range of " + k)
    return bad
def reference(c0, s0):
    C = np.zeros((N, 8, 16, W), np.int64); S = np.zeros((N, 8, 16, W), np.int64)
    C[..., :B] = c0.reshape(N, 8, 16, B); S[..., :B] = s0.reshape(N, 8, 16, B)
    port = np.zeros((N, 8, 16, LP), np.int64)
    for rnd in range(RO):
        x = np.concatenate([B - E + rnd * LE + np.arange(LE), B - LP + np.arange(LP)])
        c = np.concatenate([C[..., x[:LE]], port], axis=3)
        for st in range(ST):
            b = B + (rnd * ST + st) * M
            sx = S[..., x]
            score = np.stack([np.add.reduce(np.minimum(c, np.take_along_axis(C, sx[:, :, i][:, :, None, :], 3)), axis=2) for i in range(16)], axis=2)
            k = np.argmax(score, axis=2); best = np.max(score, axis=2)
            y = np.take_along_axis(sx, k[:, :, None, :], 2)[:, :, 0]
            for a in range(N):
                for g in range(8):
                    l = np.flatnonzero(best[a, g] >= TH)
                    l = l[np.sort(np.unique(y[a, g, l], return_index=True)[1])][:M]
                    n = b + np.arange(l.size); yy = y[a, g, l]
                    m = np.minimum(c[a, g][:, l], C[a, g][:, yy]); old = S[a, g][:, yy]
                    C[a, g][:, yy] -= m
                    C[a, g][:, n] = m; S[a, g][:, n] = old
                    S[a, g][k[a, g, l], x[l]] = n
            x = b + np.arange(M); c = np.array(C[..., b:b + M])
        port = np.roll(c[..., :LP], 1, axis=0)
    return {"yc": C.reshape(N, 128, W).astype(np.float32), "ys": np.ascontiguousarray(S[..., B - E:]).reshape(N, 128, W - B + E).astype(np.float32)}

@@ -1,0 +1,474 @@
+from concourse.mybir import AluOpType, ActivationFunctionType
+
+B, LE, LP, M = 2112, 176, 80, 160
+W = B + 4 * M
+E = W + 256
+LANES = (176, 160, 256, 160)
+XCOL = (1680, B, 1856, B + 2 * M)
+WIDE = (B, B, B, B + 2 * M)
+CHUNKS = ((112, 64), (32, 128), (128, 128), (32, 128))
+SHARE = ((32, 0), (16, 32), (48, 12), (0, 16))
+BEST = ((11, 13), (0, 15), (0, 5), (0, 5))
+
+SCRATCH = {}
+PSUM = ("pK0", "pK1", "pC0", "pC1", "pO0", "pO1", "pY", "pW")
+for _names, _w, _t in (
+        ("CI SI", B, "int32"), ("PI PA", 1, "int32"), ("C S", E, "float32"),
+        ("G MN", 4096, "float32"), ("EQ", 4096, "bfloat16"), ("DEAD ONEB", 256, "bfloat16"), ("land", LP, "float32"),
+        ("PMX0 PMX1 SEG", 136, "float32"), ("BIAS", 136, "bfloat16"), ("OH0 OH1 IDB BBIG WGT", 128, "bfloat16"),
+        ("OS CY SY0 SY1 DD REST TQ EA EA2 THA THB THR SV0 SV1 SV3", 256, "float32"), ("PR YR EV2 SV2", 256, "float16"),
+        ("RS", 512, "float16"), ("BB1", 128, "float16"), ("BSEL", 2048, "float16"), ("RSEL", 2048, "bfloat16"),
+        ("YO YF YD DX D16 F S2 U16 WN WY LFN LFY QO I16 IDP TR TRX TRM TB", 16, "float32"),
+        ("QH QL", 16, "bfloat16"), ("YG LN LY", 16, "uint16"), ("SX0 SX1 SX2 SX3", 256, "uint16"),
+        ("T16", B // 16, "float32"), ("IDL", B // 16, "uint16"),
+        ("ONEF BH BONES IDN NEG DG SUM", 128, "float32"), ("KEY8", 8, "float32"), ("PF", 1, "float32")):
+    for _n in _names.split():
+        SCRATCH[_n] = ("sbuf", [128, _w], _t)
+for _n in PSUM:
+    SCRATCH[_n] = ("psum", [128, 512], "float32")
+NDMA = 13
+SEMAPHORES = ["qV", "qA", "qP", "qG", "snt", "arr"] + ["d%d" % _i for _i in range(NDMA)]
+
+
+def R(name, lo, hi, step=1, p=128):
+    return (name, lo, hi, step, p)
+
+
+def IND(win, off):
+    return ("@", win, off)
+
+
+def machine(g, T):
+    queue = {"V": g.vector, "A": g.scalar, "P": g.tensor, "G": g, "S": g.sync}
+    count = {"V": 0, "A": 0, "P": 0, "G": 0}
+    known = {"V": {}, "A": {}, "P": {}, "G": {}, "S": {}}
+    clock = {}
+    log = {}
+    ndma = [0]
+
+    def ap(r):
+        if r[0] == "@":
+            return ap(r[1]).indirect(ap(r[2]))
+        name, lo, hi, step, p = r
+        if step == 1:
+            return T[name][0:p, lo:hi]
+        return T[name][0:p, lo:hi:step]
+
+    def spread(items):
+        out = []
+        for r in items:
+            if not isinstance(r, tuple):
+                continue
+            if r[0] == "@":
+                out.append(r[1])
+                out.append(r[2])
+            else:
+                out.append(r)
+        return out
+
+    def needs(q, reads, writes, compute):
+        need = {}
+        for kind, items in (("r", reads), ("w", writes)):
+            for r in items:
+                name, lo, hi = r[0], r[1], r[2]
+                psum = name in PSUM
+                for (l2, h2, k2, ch, val, q2, c2) in log.get(name, []):
+                    same = q2 == q and c2 and compute
+                    over = lo < h2 and l2 < hi
+                    if psum and not same:
+                        hit = True
+                    elif not over or (kind == "r" and k2 == "r"):
+                        hit = False
+                    elif same:
+                        hit = k2 == "w" and q != "P"
+                    else:
+                        hit = True
+                    if hit:
+                        need[ch] = max(need.get(ch, 0), val)
+        return need
+
+    def wait(q, need):
+        todo = {ch: v for ch, v in need.items() if known[q].get(ch, 0) < v}
+        for ch, v in todo.items():
+            if not any(c2 != ch and clock[(c2, v2)].get(ch, 0) >= v for c2, v2 in todo.items()):
+                queue[q].wait_ge(T.sem[ch], v)
+        for ch, v in todo.items():
+            for c2, v2 in clock[(ch, v)].items():
+                if known[q].get(c2, 0) < v2:
+                    known[q][c2] = v2
+
+    def record(q, ch, val, reads, writes, compute):
+        snap = dict(known[q])
+        if compute:
+            for c2, v2 in clock.get((ch, val - 1), {}).items():
+                if snap.get(c2, 0) < v2:
+                    snap[c2] = v2
+        snap[ch] = val
+        clock[(ch, val)] = snap
+        for kind, items in (("r", reads), ("w", writes)):
+            for r in items:
+                name, lo, hi, full = r[0], r[1], r[2], r[3] == 1 and r[4] == 128
+                old = log.get(name, [])
+                if name in PSUM:
+                    old = [a for a in old if a[5] == q]
+                if kind == "w" and full:
+                    old = [a for a in old if not (lo <= a[0] and a[1] <= hi)]
+                log[name] = old + [(lo, hi, kind, ch, val, q, compute)]
+
+    def op(q, call, out, reads):
+        rd = spread(reads)
+        wr = [out]
+        if out[0] == "@":
+            wr = [(out[1][0], out[1][1], out[1][2], 2, 128)]
+            rd.append(out[2])
+        wait(q, needs(q, rd, wr, True))
+        count[q] += 1
+        ch = "q" + q
+        call(queue[q]).then_inc(T.sem[ch], 1)
+        record(q, ch, count[q], rd, wr, True)
+
+    def dma(q, out, in_, reads, writes):
+        wait(q, needs(q, reads, writes, False))
+        ch = "d%d" % ndma[0]
+        ndma[0] += 1
+        queue[q].dma_start(out, in_).then_inc(T.sem[ch], 16)
+        record(q, ch, 16, reads, writes, False)
+
+    m = {"ap": ap, "dma": dma}
+    m["cp"] = lambda out, a: op("V", lambda e: e.tensor_copy(ap(out), ap(a)), out, [a])
+    m["tt"] = lambda out, a, b, o: op("V", lambda e: e.tensor_tensor(ap(out), ap(a), ap(b), o), out, [a, b])
+
+    def ts(out, a, s1, o0, s2=None, o1=None):
+        x1 = ap(s1) if isinstance(s1, tuple) else s1
+        if o1 is None:
+            op("V", lambda e: e.tensor_scalar(ap(out), ap(a), x1, None, o0), out, [a, s1])
+        else:
+            op("V", lambda e: e.tensor_scalar(ap(out), ap(a), x1, s2, o0, o1), out, [a, s1])
+    m["ts"] = ts
+    m["fill"] = lambda out, c: op("V", lambda e: e.memset(ap(out), c), out, [])
+    m["scan"] = lambda out, a, b, i, o0, o1: op(
+        "V", lambda e: e.tensor_tensor_scan(ap(out), ap(a), ap(b), i, o0, o1), out, [a, b])
+    m["iota"] = lambda out, pat, base, cm, small: op(
+        "G", (lambda e: e.iota(ap(out), pat, base, cm, allow_small_or_imprecise_dtypes=True)) if small else
+        (lambda e: e.iota(ap(out), pat, base, cm)), out, [])
+    m["keep"] = lambda out, a, pat, cond, base, cm: op(
+        "G", lambda e: e.affine_select(ap(out), ap(a), pat, cond, 0.0, base, cm), out, [a])
+    m["mm"] = lambda out, l, r, start, stop: op(
+        "P", lambda e: e.matmul(ap(out), ap(l), ap(r), start, stop), out, [l, r])
+
+    def act(out, a, func, scale=1.0, bias=0.0):
+        x = ap(scale) if isinstance(scale, tuple) else scale
+        op("A", lambda e: e.activation(ap(out), ap(a), func, bias=bias, scale=x), out, [a, scale])
+    m["act"] = act
+
+    def remote(call, reads, local, n):
+        wait("G", needs("G", reads, [], False))
+        call()
+        record("G", local, n, reads, [], False)
+    m["remote"] = remote
+
+    def landed(name, lo, hi, ch, n):
+        clock[(ch, n)] = {ch: n}
+        log[name] = [(lo, hi, "w", ch, n, "far", False)]
+    m["landed"] = landed
+
+    def finish(n):
+        need = {"q" + q: count[q] for q in count}
+        for i in range(ndma[0]):
+            need["d%d" % i] = 16
+        need["snt"] = n
+        for ch, v in need.items():
+            if known["G"].get(ch, 0) < v:
+                g.wait_ge(T.sem[ch], v)
+    m["finish"] = finish
+    return m
+
+
+def rank_program(g, core, T, topo):
+    rank = T.rank_of(core)
+    if rank is None:
+        return
+    O, AF = AluOpType, ActivationFunctionType
+    m = machine(g, T)
+    cp, tt, ts, fill, scan, mm, act, dma, ap, iota, keep = (
+        m["cp"], m["tt"], m["ts"], m["fill"], m["scan"], m["mm"], m["act"], m["dma"], m["ap"], m["iota"], m["keep"])
+    n = len(T.cores)
+    nxt, prv = T.cores[(rank + 1) % n], T.cores[(rank - 1) % n]
+    sent = len(topo.engines(core, nxt))
+    m["landed"]("land", 0, LP, "arr", len(topo.engines(prv, core)))
+
+    def load(q, to, src, lo, hi):
+        dma(q, T[to][:, lo:hi], T[src][:, lo:hi], [], [R(to, lo, hi)])
+    cut = (0, 960, 1680, B)
+    load("S", "SI", "s0", 1680, 1856)
+    load("A", "CI", "c0", cut[0], cut[1])
+    load("S", "CI", "c0", cut[1], cut[2])
+    load("A", "CI", "c0", cut[2], cut[3])
+    load("S", "SI", "s0", 1856, B)
+    load("A", "SI", "s0", 0, 1680)
+
+    fill(R("ONEF", 0, 128), 1.0)
+    iota(R("PI", 0, 1), [[0, 1]], 0, 1, False)
+    iota(R("T16", 0, B // 16), [[16, B // 16]], 0, 0, True)
+    iota(R("I16", 0, 16), [[1, 16]], 0, 0, True)
+    keep(R("BH", 0, 128), R("ONEF", 0, 128), [[-16, 8], [0, 16]], O.is_ge, 0, 1)
+    keep(R("BONES", 0, 128), R("BH", 0, 128), [[16, 8], [0, 16]], O.is_ge, 15, -1)
+    keep(R("IDN", 0, 128), R("ONEF", 0, 128), [[-1, 128]], O.is_equal, 0, 1)
+    iota(R("BIAS", 0, 136), [[0, 8], [-1, 17]], 15, 0, True)
+    iota(R("ONEB", 0, 256), [[0, 256]], 1, 0, True)
+    iota(R("C", B, W), [[0, W - B]], 0, 0, True)
+    iota(R("S", B, W), [[0, W - B]], 0, 0, True)
+    fill(R("SEG", 0, 136), 1.0)
+    fill(R("THA", 0, 256), 0.5)
+    fill(R("THB", 0, 256), 0.0)
+    fill(R("SEG", 0, 136, 17), 0.0)
+    fill(R("THA", 0, 256, 16), 0.0)
+    fill(R("THB", 0, 256, 16), 65536.0)
+    ts(R("PA", 0, 1), R("PI", 0, 1), 15, O.bitwise_and)
+    scan(R("THR", 0, 256), R("THA", 0, 256), R("THB", 0, 256), 0.0, O.mult, O.add)
+    cp(R("PF", 0, 1), R("PA", 0, 1))
+    ts(R("IDP", 0, 16), R("I16", 0, 16), R("PF", 0, 1), O.is_equal)
+    fill(R("BSEL", 0, 2048), 0.0)
+    ts(R("TR", 0, 16), R("T16", 0, 16), R("PF", 0, 1), O.add, float(W), O.add)
+    ts(R("IDL", 0, B // 16), R("T16", 0, B // 16), R("PF", 0, 1), O.add)
+    ts(R("KEY8", 0, 8), R("BONES", 0, 128, 16), 16.0, O.mult)
+    cp(R("BB1", 0, 128), R("BONES", 0, 128))
+    for i in range(8):
+        cp(R("BSEL", 16 * i, 16 * i + 129 * 15 + 1, 129), R("BONES", 16 * i, 16 * i + 16))
+    fill(R("BIAS", 16, 136, 17), 1048576.0)
+    act(R("IDB", 0, 128), R("IDN", 0, 128), AF.Copy)
+    act(R("BBIG", 0, 128), R("BONES", 0, 128), AF.Copy, 65536.0)
+    act(R("NEG", 0, 128), R("IDN", 0, 128), AF.Copy, -1.0)
+    for i in range(16):
+        act(R("RSEL", 128 * i, 128 * i + 128), R("BONES", 0, 128), AF.Copy, R("IDP", i, i + 1))
+    tt(R("DG", 0, 128), R("IDN", 0, 128), R("THR", 0, 128), O.mult)
+    scan(R("SUM", 0, 128), R("ONEF", 0, 128), R("DG", 0, 128), 0.0, O.mult, O.add)
+    ts(R("WGT", 0, 128), R("BONES", 0, 128), R("SUM", 127, 128), O.mult, 0.5, O.mult)
+
+    def high(u, to):
+        ts(R(to, 0, LANES[u]), R("S", XCOL[u], XCOL[u] + LANES[u]), 2047.5, O.is_gt, -4096.0, O.mult)
+
+    def lists(u):
+        cp(R("SX%d" % u, 0, LANES[u]), R("S", XCOL[u], XCOL[u] + LANES[u]))
+
+    def convert(to, src, lo, hi):
+        cp(R(to, lo, hi), R(src, lo, hi))
+
+    convert("S", "SI", 1680, 1856)
+    lists(0)
+    high(0, "EA")
+    convert("C", "CI", cut[0], cut[1])
+    convert("C", "CI", cut[1], cut[2])
+
+    def new_counts(u):
+        tt(IND(R("C", B + M * u, E), R("LN", 0, LANES[u] // 16)), R("CY", 0, LANES[u]), R("REST", 0, LANES[u]), O.subtract)
+
+    def new_links(u):
+        cp(IND(R("S", B + M * u, E), R("LN", 0, LANES[u] // 16)), R("SY%d" % (u % 2), 0, LANES[u]))
+
+    def changes(u):
+        nt = LANES[u] // 16
+        tt(R("QO", 0, nt), R("LFN", 0, nt), R("LFY", 0, nt), O.subtract)
+        cp(R("QH", 0, nt), R("QO", 0, nt))
+        tt(R("QL", 0, nt), R("QO", 0, nt), R("QH", 0, nt), O.subtract)
+        for i in range(16):
+            mm(R("pW", i, LANES[u], 16), R("RSEL", 128 * i, 128 * i + 128), R("QH", 0, nt), True, False)
+            mm(R("pW", i, LANES[u], 16), R("RSEL", 128 * i, 128 * i + 128), R("QL", 0, nt), False, True)
+
+    def link_changes(u):
+        tt(R("TQ", 0, LANES[u]), R("OS", 0, LANES[u]), R("pW", 0, LANES[u]), O.mult)
+
+    def add_links(u):
+        L, x = LANES[u], XCOL[u]
+        if u == 3:
+            tt(R("S", x, x + L), R("S", x, x + L), R("TQ", 0, L), O.add)
+        else:
+            mm(R("pW", 0, L), R("IDN", 0, 128), R("S", x, x + L), True, False)
+            mm(R("pW", 0, L), R("IDN", 0, 128), R("TQ", 0, L), False, True)
+            act(R("S", x, x + L), R("pW", 0, L), AF.Copy)
+
+    def send():
+        rid, pid = topo.addr(nxt)[:2]
+        src = B + M
+        m["remote"](lambda: g.remote_dma(out_ap=T.land[:], in_ap=T.C[:, src:src + LP], remote_sem=T.sem.arr,
+                                         local_sem=T.sem.snt, pid=pid, routing_id=rid, dma_engine_mask=topo.mask(core, nxt)),
+                    [R("C", src, src + LP)], "snt", sent)
+
+    def store_links(q, lo, hi):
+        dma(q, T.ys[:, lo - 1680:hi - 1680], T.S[:, lo:hi], [R("S", lo, hi)], [])
+
+    def store_counts(q, lo, hi):
+        dma(q, T.yc[:, lo:hi], T.C[:, lo:hi], [R("C", lo, hi)], [])
+
+    for u in range(4):
+        L, x, wide = LANES[u], XCOL[u], WIDE[u]
+        nt = L // 16
+        n0, n1 = CHUNKS[u]
+        h0, h1 = SHARE[u]
+        win = R("C" if u else "CI", 0, wide)
+        SX, SV, SY = "SX%d" % u, "SV%d" % u, "SY%d" % (u % 2)
+
+        def gather(q, lo, hi):
+            if lo < hi and q == "A":
+                act(R("G", 16 * lo, 16 * hi), IND(win, R(SX, lo, hi)), AF.Copy)
+            elif lo < hi:
+                cp(R("G", 16 * lo, 16 * hi), IND(win, R(SX, lo, hi)))
+
+        def own(b, lo, hi, src):
+            mm(R("pC%d" % b, lo, hi), R("IDN", 0, 128), src, True, True)
+
+        gather("A", 0, n0 - h0)
+        gather("A", n0, L - h1)
+        if u == 0:
+            convert("C", "CI", cut[2], cut[3])
+        else:
+            changes(u - 1)
+            if u % 2:
+                high(u, "EA")
+            new_counts(u - 1)
+            if u == 2:
+                send()
+            if u == 3:
+                store_links("S", B, B + 2 * M)
+                store_counts("S", B + 2 * M, W - M)
+        own(0, 0, n0, R("C", x, x + n0))
+        if u == 2:
+            own(1, 0, LE - n0, R("C", x + n0, x + LE))
+            act(R("pC1", LE - n0, n1), R("land", 0, LP), AF.Copy)
+        else:
+            own(1, 0, n1, R("C", x + n0, x + L))
+            mm(R("pY", 0, L), R("IDN", 0, 128), R("S", x, x + L), True, False)
+            mm(R("pY", 0, L), R("IDN", 0, 128), R("EA", 0, L), False, True)
+            act(R(SV, 0, L), R("pY", 0, L), AF.Identity, 1.0, 1.0)
+        gather("V", n0 - h0, n0)
+        if u == 0:
+            ts(R("TRX", 0, 16), R("TR", 0, 16), 1.0, O.add)
+            ts(R("TRM", 0, 16), R("TR", 0, 16), -16.0, O.mult)
+            act(R("S", 1856, B), IND(R("SI", 0, B), R("IDL", 1856 // 16, B // 16)), AF.Copy)
+            act(R("S", 0, 1680), IND(R("SI", 0, B), R("IDL", 0, 1680 // 16)), AF.Copy)
+        if u == 2:
+            link_changes(1)
+
+        def keys(b, k):
+            nl, l0 = CHUNKS[u][b], b * n0
+            tt(R("MN", 16 * l0 + k * nl, 16 * l0 + (k + 1) * nl), R("G", 16 * l0 + k, 16 * (l0 + nl), 16),
+               R("pC%d" % b, 0, nl), O.min)
+            if k == 0:
+                mm(R("pK%d" % b, 0, 136, 1, nl), R("ONEB", 0, nl, 1, 1), R("BIAS", 0, 136, 1, 1), True, False)
+            mm(R("pK%d" % b, k, 136, 17, nl), R("MN", 16 * l0 + k * nl, 16 * l0 + (k + 1) * nl), R("KEY8", 0, 8),
+               False, k == 15)
+
+        def best(b):
+            nl = CHUNKS[u][b]
+            K, X = "pK%d" % b, "PMX%d" % b
+            scan(R(X, 0, 136, 1, nl), R("SEG", 0, 136, 1, nl), R(K, 0, 136, 1, nl), 0.0, O.mult, O.max)
+            for j in range(8):
+                ts(R("OH%d" % b, 16 * j, 16 * j + 16, 1, nl), R(K, 17 * j, 17 * j + 16, 1, nl),
+                   R(X, 17 * j + 16, 17 * j + 17, 1, nl), O.is_equal)
+            mm(R("pO%d" % b, 0, nl), R("OH%d" % b, 0, 128, 1, nl), R("IDB", 0, nl, 1, nl), True, True)
+
+        def pick(b):
+            nl, l0 = CHUNKS[u][b], b * n0
+            tt(R("PR", l0, l0 + nl), R("pO%d" % b, 0, nl), R(SV, l0, l0 + nl), O.mult)
+            act(R("OS", l0, l0 + nl), R("pO%d" % b, 0, nl), AF.Copy)
+
+        for k in range(16):
+            keys(0, k)
+        if u == 2:
+            add_links(1)
+        if u % 2:
+            lo, hi = ((1680, 1856), (1856, B))[u // 2]
+            link_changes(u - 1)
+            add_links(u - 1)
+            store_links("S", lo, hi)
+        gather("V", L - h1, L)
+        for k in range(16):
+            if k == BEST[u][0]:
+                best(0)
+            keys(1, k)
+            if k == BEST[u][1]:
+                pick(0)
+        ts(R("TB", 0, 16), R("TRM", 0, 16), 16.0 * (B + M * u - 1), O.add)
+        best(1)
+        pick(1)
+        mm(R("pY", 0, L), R("BB1", 0, 128), R("PR", 0, L), True, True)
+        for i in range(16):
+            mm(R("pK0", 256, 256 + nt), R("BSEL", 128 * i, 128 * i + 128), R("PR", i, L, 16), i == 0, i == 15)
+        cp(R("YR", 0, L), R("pY", 0, L))
+        ts(R("DEAD", 0, L), R("YR", 0, L), 0.0, O.is_equal)
+        mm(R("pW", 0, L), R("BBIG", 0, 128), R("DEAD", 0, L), True, False)
+        cp(R("YO", 0, nt), R("pK0", 256, 256 + nt))
+        ts(R("YF", 0, nt), R("YO", 0, nt), 0.0, O.is_lt, 4096.0, O.mult)
+
+        def same(t):
+            o = 256 * t
+            ts(R("EQ", o + 16 * t, o + L), R("YR", 16 * t, L), R("YO", t, t + 1), O.is_equal)
+            mm(R("pW", 16 * t, 16 * t + 16), R("WGT", 0, 128), R("EQ", o + 16 * t, o + 16 * t + 16), False, t == nt - 1)
+            if t < nt - 1:
+                mm(R("pW", 16 * t + 16, L), R("BBIG", 0, 128), R("EQ", o + 16 * t + 16, o + L), False, False)
+        same(0)
+        tt(R("YD", 0, nt), R("YF", 0, nt), R("YO", 0, nt), O.add)
+        same(1)
+        ts(R("YG", 0, nt), R("YD", 0, nt), -1.0, O.add, 0.0, O.max)
+        act(R("CY", 0, L), IND(win, R("YG", 0, nt)), AF.Copy)
+        act(R(SY, 0, L), IND(R("S" if u else "SI", 0, wide), R("YG", 0, nt)), AF.Copy)
+        for t in range(2, nt):
+            same(t)
+        tt(R("DX", 0, nt), R("YD", 0, nt), R("TRX", 0, nt), O.subtract)
+        if u % 2:
+            l0 = 0
+            for b, nl in enumerate(CHUNKS[u]):
+                tt(R("DD", l0, l0 + nl), R("CY", l0, l0 + nl), R("pC%d" % b, 0, nl), O.subtract)
+                l0 += nl
+            act(R("REST", 0, L), R("DD", 0, L), AF.Relu)
+        ts(R("D16", 0, nt), R("DX", 0, nt), 16.0, O.mult)
+        tt(R("RS", L, 2 * L), R("pW", 0, L), R("THR", 0, L), O.is_lt)
+        scan(R("RS", 0, L), R("ONEB", 0, L), R("RS", L, 2 * L), 0.0, O.mult, O.add)
+        for i in range(16):
+            mm(R("pK1", 256, 256 + 2 * nt), R("BSEL", 128 * i, 128 * i + 128), R("RS", i, 2 * L, 16), i == 0, i == 15)
+        if u == 0:
+            lists(2)
+            high(2, "EA2")
+        if u == 1:
+            tt(R("EV2", 0, LANES[2]), R("EA2", 0, LANES[2]), R("S", XCOL[2], XCOL[2] + LANES[2]), O.add)
+            ts(R("SV2", 0, LANES[2]), R("EV2", 0, LANES[2]), 1.0, O.add)
+        if u == 2:
+            new_links(1)
+        if u % 2 == 0:
+            ent = min(L, LE)
+            mm(R("pY", 0, L), R("IDN", 0, 128), R("CY", 0, L), True, False)
+            mm(R("pY", 0, ent), R("NEG", 0, 128), R("C", x, x + ent), False, ent == L)
+            if ent < L:
+                mm(R("pY", ent, L), R("NEG", 0, 128), R("land", 0, LP), False, True)
+            act(R("REST", 0, L), R("pY", 0, L), AF.Relu)
+
+        if L > M:
+            ts(R("F", 0, nt), R("pK1", 256, 256 + nt), 16.0 * M + 0.5, O.is_le, 1.0 / 256, O.mult)
+            tt(R("U16", 0, nt), R("pK1", 256, 256 + nt), R("TB", 0, nt), O.add)
+            tt(R("S2", 0, nt), R("F", 0, nt), R("pK1", 256 + nt, 256 + 2 * nt), O.mult)
+        else:
+            ts(R("S2", 0, nt), R("pK1", 256 + nt, 256 + 2 * nt), 1.0 / 256, O.mult)
+            tt(R("U16", 0, nt), R("pK1", 256, 256 + nt), R("TB", 0, nt), O.add)
+        tt(R("WY", 0, nt), R("D16", 0, nt), R("S2", 0, nt), O.mult)
+        tt(R("WN", 0, nt), R("U16", 0, nt), R("S2", 0, nt), O.mult)
+        tt(R("LFY", 0, nt), R("WY", 0, nt), R("TR", 0, nt), O.add)
+        if u % 2:
+            cp(R("LY", 0, nt), R("LFY", 0, nt))
+            cp(IND(R("C", 0, E), R("LY", 0, nt)), R("REST", 0, L))
+        tt(R("LFN", 0, nt), R("WN", 0, nt), R("TR", 0, nt), O.add)
+        ts(R("LN", 0, nt), R("LFN", 0, nt), -float(B + M * u), O.add)
+        if u % 2 == 0:
+            cp(R("LY", 0, nt), R("LFY", 0, nt))
+            new_links(u)
+            lists(u + 1)
+            cp(IND(R("C", 0, E), R("LY", 0, nt)), R("REST", 0, L))
+
+    store_counts("S", 0, B + 2 * M)
+    changes(3)
+    new_counts(3)
+    store_counts("A", W - M, W)
+    new_links(3)
+    link_changes(3)
+    add_links(3)
+    store_links("S", B + 2 * M, W)
+    m["finish"](sent)

@@ -1,32 +1,37 @@
-from concourse.mybir import AluOpType, ActivationFunctionType
+from concourse.mybir import AluOpType, ActivationFunctionType, AxisListType
 
 B, LE, LP, M = 2112, 176, 80, 160
 W = B + 4 * M
-E = W + 256
-LANES = (176, 160, 256, 160)
-XCOL = (1680, B, 1856, B + 2 * M)
-WIDE = (B, B, B, B + 2 * M)
-CHUNKS = ((112, 64), (32, 128), (128, 128), (32, 128))
-SHARE = ((32, 0), (16, 32), (48, 12), (0, 16))
-BEST = ((11, 13), (0, 15), (0, 5), (0, 5))
+TOP = B + M
+SPARE = TOP + 256
+HALF = 1376.0
+LANES = (176, 176, 256, 160)
+WIDE = (B, B, B, TOP)
+CHUNKS = ((48, 128), (48, 128), (128, 128), (32, 128))
+TWICE = (1, 1, 1, 2)
+SHARE = ((32, 32), (32, 32), (48, 16), (0, 16))
+BEST = ((0, 2, 4, 12), (2, 4, 6, 10), (0, 2, 4, 12), (4, 7, 10, 14))
 
 SCRATCH = {}
-PSUM = ("pK0", "pK1", "pC0", "pC1", "pO0", "pO1", "pY", "pW")
+PSUM = ("pK0", "pK1", "pC0", "pC1", "pO", "pX", "pW", "pN")
 for _names, _w, _t in (
-        ("CI SI", B, "int32"), ("PI PA", 1, "int32"), ("C S", E, "float32"),
-        ("G MN", 4096, "float32"), ("EQ", 4096, "bfloat16"), ("DEAD ONEB", 256, "bfloat16"), ("land", LP, "float32"),
-        ("PMX0 PMX1 SEG", 136, "float32"), ("BIAS", 136, "bfloat16"), ("OH0 OH1 IDB BBIG WGT", 128, "bfloat16"),
-        ("OS CY SY0 SY1 DD REST TQ EA EA2 THA THB THR SV0 SV1 SV3", 256, "float32"), ("PR YR EV2 SV2", 256, "float16"),
-        ("RS", 512, "float16"), ("BB1", 128, "float16"), ("BSEL", 2048, "float16"), ("RSEL", 2048, "bfloat16"),
-        ("YO YF YD DX D16 F S2 U16 WN WY LFN LFY QO I16 IDP TR TRX TRM TB", 16, "float32"),
-        ("QH QL", 16, "bfloat16"), ("YG LN LY", 16, "uint16"), ("SX0 SX1 SX2 SX3", 256, "uint16"),
-        ("T16", B // 16, "float32"), ("IDL", B // 16, "uint16"),
-        ("ONEF BH BONES IDN NEG DG SUM", 128, "float32"), ("KEY8", 8, "float32"), ("PF", 1, "float32")):
+        ("CI", B, "int32"), ("SI", B + SPARE, "int32"), ("C", B + SPARE, "float32"), ("PI PA", 1, "int32"),
+        ("CN1 CN2 CN3 SN1 SN2 SN3", SPARE, "float32"), ("SO", TOP - 1680, "float32"),
+        ("G MN", 4096, "float32"), ("EQ", 4096, "bfloat16"), ("land", LP, "float32"),
+        ("DEAD ONEB FM MASKC", 256, "bfloat16"), ("RS", 272, "bfloat16"),
+        ("CY0 CY1 CY2 CY3 SY0 SY1 SY2 SY3 RE0 RE1 RE2 RE3 YX THR DM I256 SEGY RA RB RW", 256, "float32"),
+        ("PR YR SV0 SV1 SV2 SV3", 256, "float16"), ("SX0 SX1 SX2 SX3", 256, "uint16"),
+        ("OH0 OH1 IDB ID4 IDH BONB BIAS L1A L2A L1N L2N", 128, "bfloat16"), ("BB1", 128, "float16"),
+        ("ROWS", 640, "bfloat16"), ("CU", 32, "bfloat16"), ("RSEL", 2048, "bfloat16"),
+        ("XB0 XB1 SEGK ONEF BH BONES B4 LA LB IDN NEG", 128, "float32"),
+        ("YF Z KR I16 IDP TR WT WA WH WD", 16, "float32"), ("KILL Q", 16, "bfloat16"),
+        ("YG LY LN0 LN1 LN2 LN3", 16, "uint16"), ("T16", B // 16, "float32"), ("IDL", B // 16, "uint16"),
+        ("KEY8", 8, "float32"), ("PF W0 W1 ZERO", 1, "float32")):
     for _n in _names.split():
         SCRATCH[_n] = ("sbuf", [128, _w], _t)
 for _n in PSUM:
     SCRATCH[_n] = ("psum", [128, 512], "float32")
-NDMA = 13
+NDMA = 16
 SEMAPHORES = ["qV", "qA", "qP", "qG", "snt", "arr"] + ["d%d" % _i for _i in range(NDMA)]
 
 
@@ -47,9 +52,13 @@ def machine(g, T):
     ndma = [0]
 
     def ap(r):
+        if not isinstance(r, tuple):
+            return r
         if r[0] == "@":
             return ap(r[1]).indirect(ap(r[2]))
         name, lo, hi, step, p = r
+        if step == -1:
+            return T[name][0:p, hi - 1::-1] if lo == 0 else T[name][0:p, hi - 1:lo - 1:-1]
         if step == 1:
             return T[name][0:p, lo:hi]
         return T[name][0:p, lo:hi:step]
@@ -107,7 +116,7 @@ def machine(g, T):
         clock[(ch, val)] = snap
         for kind, items in (("r", reads), ("w", writes)):
             for r in items:
-                name, lo, hi, full = r[0], r[1], r[2], r[3] == 1 and r[4] == 128
+                name, lo, hi, full = r[0], r[1], r[2], abs(r[3]) == 1 and r[4] == 128
                 old = log.get(name, [])
                 if name in PSUM:
                     old = [a for a in old if a[5] == q]
@@ -139,27 +148,25 @@ def machine(g, T):
     m["tt"] = lambda out, a, b, o: op("V", lambda e: e.tensor_tensor(ap(out), ap(a), ap(b), o), out, [a, b])
 
     def ts(out, a, s1, o0, s2=None, o1=None):
-        x1 = ap(s1) if isinstance(s1, tuple) else s1
         if o1 is None:
-            op("V", lambda e: e.tensor_scalar(ap(out), ap(a), x1, None, o0), out, [a, s1])
+            op("V", lambda e: e.tensor_scalar(ap(out), ap(a), ap(s1), None, o0), out, [a, s1])
         else:
-            op("V", lambda e: e.tensor_scalar(ap(out), ap(a), x1, s2, o0, o1), out, [a, s1])
+            op("V", lambda e: e.tensor_scalar(ap(out), ap(a), ap(s1), ap(s2), o0, o1), out, [a, s1, s2])
     m["ts"] = ts
     m["fill"] = lambda out, c: op("V", lambda e: e.memset(ap(out), c), out, [])
+    m["top"] = lambda out, a: op(
+        "V", lambda e: e.tensor_reduce(ap(out), ap(a), AxisListType.X, AluOpType.max), out, [a])
     m["scan"] = lambda out, a, b, i, o0, o1: op(
-        "V", lambda e: e.tensor_tensor_scan(ap(out), ap(a), ap(b), i, o0, o1), out, [a, b])
+        "V", lambda e: e.tensor_tensor_scan(ap(out), ap(a), ap(b), ap(i), o0, o1), out, [a, b, i])
     m["iota"] = lambda out, pat, base, cm, small: op(
         "G", (lambda e: e.iota(ap(out), pat, base, cm, allow_small_or_imprecise_dtypes=True)) if small else
         (lambda e: e.iota(ap(out), pat, base, cm)), out, [])
-    m["keep"] = lambda out, a, pat, cond, base, cm: op(
-        "G", lambda e: e.affine_select(ap(out), ap(a), pat, cond, 0.0, base, cm), out, [a])
+    m["keep"] = lambda out, a, pat, cond, other, base, cm: op(
+        "G", lambda e: e.affine_select(ap(out), ap(a), pat, cond, other, base, cm), out, [a])
     m["mm"] = lambda out, l, r, start, stop: op(
         "P", lambda e: e.matmul(ap(out), ap(l), ap(r), start, stop), out, [l, r])
-
-    def act(out, a, func, scale=1.0, bias=0.0):
-        x = ap(scale) if isinstance(scale, tuple) else scale
-        op("A", lambda e: e.activation(ap(out), ap(a), func, bias=bias, scale=x), out, [a, scale])
-    m["act"] = act
+    m["act"] = lambda out, a, func, scale=1.0, bias=0.0: op(
+        "A", lambda e: e.activation(ap(out), ap(a), func, bias=bias, scale=ap(scale)), out, [a, scale])
 
     def remote(call, reads, local, n):
         wait("G", needs("G", reads, [], False))
@@ -190,123 +197,143 @@ def rank_program(g, core, T, topo):
         return
     O, AF = AluOpType, ActivationFunctionType
     m = machine(g, T)
-    cp, tt, ts, fill, scan, mm, act, dma, ap, iota, keep = (
-        m["cp"], m["tt"], m["ts"], m["fill"], m["scan"], m["mm"], m["act"], m["dma"], m["ap"], m["iota"], m["keep"])
+    cp, tt, ts, fill, scan, mm, act, dma, iota, keep, top = (
+        m["cp"], m["tt"], m["ts"], m["fill"], m["scan"], m["mm"], m["act"], m["dma"], m["iota"], m["keep"], m["top"])
     n = len(T.cores)
     nxt, prv = T.cores[(rank + 1) % n], T.cores[(rank - 1) % n]
     sent = len(topo.engines(core, nxt))
     m["landed"]("land", 0, LP, "arr", len(topo.engines(prv, core)))
 
-    def load(q, to, src, lo, hi):
-        dma(q, T[to][:, lo:hi], T[src][:, lo:hi], [], [R(to, lo, hi)])
-    cut = (0, 960, 1680, B)
-    load("S", "SI", "s0", 1680, 1856)
-    load("A", "CI", "c0", cut[0], cut[1])
-    load("S", "CI", "c0", cut[1], cut[2])
-    load("A", "CI", "c0", cut[2], cut[3])
-    load("S", "SI", "s0", 1856, B)
-    load("A", "SI", "s0", 0, 1680)
+    def load(q, to, src, lo, hi, after=()):
+        dma(q, T[to][:, lo:hi], T[src][:, lo:hi], list(after), [R(to, lo, hi)])
+    load("A", "SI", "s0", 1680, 1856)
+    load("S", "CI", "c0", 0, B)
+    load("S", "SI", "s0", 1856, B, [R("CI", 0, B)])
+    load("S", "SI", "s0", 0, 1680)
 
+    big = float(2 ** 60)
     fill(R("ONEF", 0, 128), 1.0)
     iota(R("PI", 0, 1), [[0, 1]], 0, 1, False)
+    keep(R("IDN", 0, 128), R("ONEF", 0, 128), [[-1, 128]], O.is_equal, 0.0, 0, 1)
+    keep(R("BH", 0, 128), R("ONEF", 0, 128), [[-16, 8], [0, 16]], O.is_ge, 0.0, 0, 1)
+    keep(R("BONES", 0, 128), R("BH", 0, 128), [[16, 8], [0, 16]], O.is_ge, 0.0, 15, -1)
+    iota(R("BIAS", 0, 128), [[0, 8], [-1, 16]], 15, 0, True)
     iota(R("T16", 0, B // 16), [[16, B // 16]], 0, 0, True)
-    iota(R("I16", 0, 16), [[1, 16]], 0, 0, True)
-    keep(R("BH", 0, 128), R("ONEF", 0, 128), [[-16, 8], [0, 16]], O.is_ge, 0, 1)
-    keep(R("BONES", 0, 128), R("BH", 0, 128), [[16, 8], [0, 16]], O.is_ge, 15, -1)
-    keep(R("IDN", 0, 128), R("ONEF", 0, 128), [[-1, 128]], O.is_equal, 0, 1)
-    iota(R("BIAS", 0, 136), [[0, 8], [-1, 17]], 15, 0, True)
-    iota(R("ONEB", 0, 256), [[0, 256]], 1, 0, True)
-    iota(R("C", B, W), [[0, W - B]], 0, 0, True)
-    iota(R("S", B, W), [[0, W - B]], 0, 0, True)
-    fill(R("SEG", 0, 136), 1.0)
-    fill(R("THA", 0, 256), 0.5)
-    fill(R("THB", 0, 256), 0.0)
-    fill(R("SEG", 0, 136, 17), 0.0)
-    fill(R("THA", 0, 256, 16), 0.0)
-    fill(R("THB", 0, 256, 16), 65536.0)
+    iota(R("I256", 0, 256), [[0, 16], [1, 16]], 0, 0, True)
+    fill(R("ONEB", 0, 256), 1.0)
+    fill(R("SEGK", 0, 128), big)
+    fill(R("SEGY", 0, 256), big)
+    fill(R("RA", 0, 256), 0.5)
+    fill(R("RB", 0, 256), 0.0)
+    fill(R("RS", 0, 16), 0.0)
+    fill(R("W0", 0, 1), 2.0 * big)
+    fill(R("CU", 0, 16), 4096.0 * (255 - M + 1))
+    fill(R("CU", 16, 32), 0.0)
+    fill(R("ROWS", 0, 128), -2048.0)
+    for u in range(4):
+        fill(R("ROWS", 128 * u + 128, 128 * u + 256), float(B + M * u - 4096))
+    fill(R("SEGK", 0, 128, 16), 1048575.5)
+    fill(R("SEGY", 0, 256, 16), -2047.5)
+    fill(R("RA", 0, 256, 16), 1.0)
+    ts(R("W1", 0, 1), R("W0", 0, 1), big, O.mult)
     ts(R("PA", 0, 1), R("PI", 0, 1), 15, O.bitwise_and)
-    scan(R("THR", 0, 256), R("THA", 0, 256), R("THB", 0, 256), 0.0, O.mult, O.add)
+    scan(R("RW", 0, 256), R("RA", 0, 256), R("RB", 0, 256), R("W1", 0, 1), O.mult, O.add)
     cp(R("PF", 0, 1), R("PA", 0, 1))
-    ts(R("IDP", 0, 16), R("I16", 0, 16), R("PF", 0, 1), O.is_equal)
-    fill(R("BSEL", 0, 2048), 0.0)
-    ts(R("TR", 0, 16), R("T16", 0, 16), R("PF", 0, 1), O.add, float(W), O.add)
-    ts(R("IDL", 0, B // 16), R("T16", 0, B // 16), R("PF", 0, 1), O.add)
     ts(R("KEY8", 0, 8), R("BONES", 0, 128, 16), 16.0, O.mult)
-    cp(R("BB1", 0, 128), R("BONES", 0, 128))
-    for i in range(8):
-        cp(R("BSEL", 16 * i, 16 * i + 129 * 15 + 1, 129), R("BONES", 16 * i, 16 * i + 16))
-    fill(R("BIAS", 16, 136, 17), 1048576.0)
+    ts(R("TR", 0, 16), R("T16", 0, 16), R("PF", 0, 1), O.add, float(TOP), O.add)
+    ts(R("IDL", 0, B // 16), R("T16", 0, B // 16), R("PF", 0, 1), O.add)
+    ts(R("DM", 0, 256), R("I256", 0, 256), R("PF", 0, 1), O.is_equal)
+    cp(R("SX0", 0, LE), R("SI", 1680, 1856))
+    tt(R("THR", 0, 256), R("DM", 0, 256), R("RW", 0, 256), O.mult)
+    ts(R("SV0", 0, LE), R("SI", 1680, 1856), -HALF, O.add)
+    top(R("WD", 0, 1), R("THR", 0, 16))
+    ts(R("WH", 0, 1), R("WD", 0, 1), 1.0 / big, O.mult, 0.25 / big, O.mult)
+    ts(R("WT", 0, 16), R("RW", 0, 256, 16), R("WH", 0, 1), O.mult)
+    act(R("ID4", 0, 128), R("IDN", 0, 128), AF.Copy, 4096.0)
     act(R("IDB", 0, 128), R("IDN", 0, 128), AF.Copy)
-    act(R("BBIG", 0, 128), R("BONES", 0, 128), AF.Copy, 65536.0)
+    act(R("IDH", 0, 128), R("IDN", 0, 128), AF.Copy, 2.0 * big)
     act(R("NEG", 0, 128), R("IDN", 0, 128), AF.Copy, -1.0)
+    act(R("BB1", 0, 128), R("BONES", 0, 128), AF.Copy)
+    act(R("BONB", 0, 128), R("BONES", 0, 128), AF.Copy)
+    act(R("B4", 0, 128), R("BONES", 0, 128), AF.Copy, 4096.0)
+    act(R("MASKC", 0, 256), R("DM", 0, 256), AF.Copy, 30720.0)
     for i in range(16):
-        act(R("RSEL", 128 * i, 128 * i + 128), R("BONES", 0, 128), AF.Copy, R("IDP", i, i + 1))
-    tt(R("DG", 0, 128), R("IDN", 0, 128), R("THR", 0, 128), O.mult)
-    scan(R("SUM", 0, 128), R("ONEF", 0, 128), R("DG", 0, 128), 0.0, O.mult, O.add)
-    ts(R("WGT", 0, 128), R("BONES", 0, 128), R("SUM", 127, 128), O.mult, 0.5, O.mult)
+        act(R("RSEL", 128 * i, 128 * i + 128), R("BONES", 0, 128), AF.Copy, R("DM", i, i + 1))
+    keep(R("L1N", 0, 128), R("BONES", 0, 128), [[1, 128]], O.is_gt, 0.0, 0, -1)
+    keep(R("L2N", 0, 128), R("BONES", 0, 128), [[-1, 128]], O.is_ge, 0.0, 0, 1)
+    keep(R("LA", 0, 128), R("B4", 0, 128), [[1, 128]], O.is_gt, 0.0, 0, -1)
+    keep(R("LB", 0, 128), R("B4", 0, 128), [[-1, 128]], O.is_ge, 0.0, 0, 1)
+    keep(R("L1A", 0, 128), R("LA", 0, 128), [[-1, 128]], O.not_equal, -255.0 * 4096, 0, 1)
+    keep(R("L2A", 0, 128), R("LB", 0, 128), [[-1, 128]], O.not_equal, 256.0 * 4096, 0, 1)
+    iota(R("SI", B, TOP), [[0, M]], 0, 0, False)
+    for r in (R("C", B, TOP), R("CN1", 0, M), R("CN2", 0, M), R("SN2", 0, M), R("SN1", 0, M), R("CN3", 0, M), R("SN3", 0, M)):
+        iota(r, [[0, M]], 0, 0, True)
+    cp(R("C", 1680, 1856), R("CI", 1680, 1856))
 
-    def high(u, to):
-        ts(R(to, 0, LANES[u]), R("S", XCOL[u], XCOL[u] + LANES[u]), 2047.5, O.is_gt, -4096.0, O.mult)
+    NEWC = (R("C", B, B + SPARE), R("CN1", 0, SPARE), R("CN2", 0, SPARE), R("CN3", 0, SPARE))
+    NEWS = (R("SI", B, B + SPARE), R("SN1", 0, SPARE), R("SN2", 0, SPARE), R("SN3", 0, SPARE))
+    OLDS = (R("SI", 1680, 1856), R("SY0", 0, LE), R("SI", 1856, B), R("SN2", 0, M))
 
-    def lists(u):
-        cp(R("SX%d" % u, 0, LANES[u]), R("S", XCOL[u], XCOL[u] + LANES[u]))
+    def new_counts(u, lo=0, hi=16):
+        hi = min(hi, LANES[u] // 16)
+        tt(IND(NEWC[u], R("LN%d" % u, lo, hi)), R("CY%d" % u, 16 * lo, 16 * hi), R("RE%d" % u, 16 * lo, 16 * hi), O.subtract)
 
-    def convert(to, src, lo, hi):
-        cp(R(to, lo, hi), R(src, lo, hi))
+    def new_links(u, lo=0, hi=16):
+        hi = min(hi, LANES[u] // 16)
+        cp(IND(NEWS[u], R("LN%d" % u, lo, hi)), R("SY%d" % u, 16 * lo, 16 * hi))
 
-    convert("S", "SI", 1680, 1856)
-    lists(0)
-    high(0, "EA")
-    convert("C", "CI", cut[0], cut[1])
-    convert("C", "CI", cut[1], cut[2])
-
-    def new_counts(u):
-        tt(IND(R("C", B + M * u, E), R("LN", 0, LANES[u] // 16)), R("CY", 0, LANES[u]), R("REST", 0, LANES[u]), O.subtract)
-
-    def new_links(u):
-        cp(IND(R("S", B + M * u, E), R("LN", 0, LANES[u] // 16)), R("SY%d" % (u % 2), 0, LANES[u]))
-
-    def changes(u):
+    def number(u):
         nt = LANES[u] // 16
-        tt(R("QO", 0, nt), R("LFN", 0, nt), R("LFY", 0, nt), O.subtract)
-        cp(R("QH", 0, nt), R("QO", 0, nt))
-        tt(R("QL", 0, nt), R("QO", 0, nt), R("QH", 0, nt), O.subtract)
+        tt(R("Q", 0, nt), R("pK1", 272, 272 + nt), R("KILL", 0, nt), O.add)
+
+    def spread_numbers(u):
         for i in range(16):
-            mm(R("pW", i, LANES[u], 16), R("RSEL", 128 * i, 128 * i + 128), R("QH", 0, nt), True, False)
-            mm(R("pW", i, LANES[u], 16), R("RSEL", 128 * i, 128 * i + 128), R("QL", 0, nt), False, True)
+            mm(R("pN", i, LANES[u], 16), R("RSEL", 128 * i, 128 * i + 128), R("Q", 0, LANES[u] // 16), False, i == 15)
 
-    def link_changes(u):
-        tt(R("TQ", 0, LANES[u]), R("OS", 0, LANES[u]), R("pW", 0, LANES[u]), O.mult)
+    def change_links(u):
+        tt(OLDS[u], OLDS[u], R("pN", 0, LANES[u]), O.max)
 
-    def add_links(u):
-        L, x = LANES[u], XCOL[u]
-        if u == 3:
-            tt(R("S", x, x + L), R("S", x, x + L), R("TQ", 0, L), O.add)
-        else:
-            mm(R("pW", 0, L), R("IDN", 0, 128), R("S", x, x + L), True, False)
-            mm(R("pW", 0, L), R("IDN", 0, 128), R("TQ", 0, L), False, True)
-            act(R("S", x, x + L), R("pW", 0, L), AF.Copy)
+    def convert(to, at, src, lo, hi):
+        act(R(to, at, at + hi - lo), IND(R(src, lo, hi), R("IDL", 0, (hi - lo) // 16)), AF.Copy)
 
     def send():
         rid, pid = topo.addr(nxt)[:2]
-        src = B + M
-        m["remote"](lambda: g.remote_dma(out_ap=T.land[:], in_ap=T.C[:, src:src + LP], remote_sem=T.sem.arr,
+        m["remote"](lambda: g.remote_dma(out_ap=T.land[:], in_ap=T.CN1[:, 0:LP], remote_sem=T.sem.arr,
                                          local_sem=T.sem.snt, pid=pid, routing_id=rid, dma_engine_mask=topo.mask(core, nxt)),
-                    [R("C", src, src + LP)], "snt", sent)
+                    [R("CN1", 0, LP)], "snt", sent)
 
-    def store_links(q, lo, hi):
-        dma(q, T.ys[:, lo - 1680:hi - 1680], T.S[:, lo:hi], [R("S", lo, hi)], [])
+    def store(q, to, at, src):
+        dma(q, T[to][:, at:at + src[2] - src[1]], T[src[0]][:, src[1]:src[2]], [src], [])
 
-    def store_counts(q, lo, hi):
-        dma(q, T.yc[:, lo:hi], T.C[:, lo:hi], [R("C", lo, hi)], [])
+    def old_links_out(lo, hi):
+        convert("SO", lo - 1680, "SI", lo, hi)
+        store("S", "ys", lo - 1680, R("SO", lo - 1680, hi - 1680))
+
+    LATER = {
+        0: {"F": [lambda: cp(R("SX2", 0, 256), R("SI", 1856, B))],
+            "O": [lambda: ts(R("SV2", 0, 256), R("SI", 1856, B), -HALF, O.add)]},
+        1: {"F": [lambda: new_counts(0, 0, 2)], "R": [lambda: new_counts(0, 2, 4)], "O": [lambda: new_counts(0, 4, 8)],
+            "P": [lambda: new_counts(0, 8, 11)]},
+        2: {"F": [lambda: new_links(0, 0, 2)], "R": [lambda: new_links(0, 2, 4)], "O": [lambda: new_links(0, 4, 8)],
+            "P": [lambda: new_links(0, 8, 11)]},
+        3: {"F": [lambda: new_links(1, 0, 2)], "R": [lambda: new_links(1, 2, 4)], "O": [lambda: new_links(1, 4, 8)],
+            "P": [lambda: new_links(1, 8, 11)]},
+    }
 
     for u in range(4):
-        L, x, wide = LANES[u], XCOL[u], WIDE[u]
+        L, wide = LANES[u], WIDE[u]
         nt = L // 16
         n0, n1 = CHUNKS[u]
         h0, h1 = SHARE[u]
+        rep = TWICE[u]
         win = R("C" if u else "CI", 0, wide)
-        SX, SV, SY = "SX%d" % u, "SV%d" % u, "SY%d" % (u % 2)
+        SX, SV, SY, CY, RE, LN = ("%s%d" % (a, u) for a in ("SX", "SV", "SY", "CY", "RE", "LN"))
+        own = (R("pC0", 0, rep * n0), R("pC1", 0, n1) if u == 2 else R("pC0", rep * n0, rep * n0 + n1))
+        pD = "pC0" if u == 2 else "pC1"
+
+        def later(place):
+            for call in LATER[u].get(place, []):
+                call()
 
         def gather(q, lo, hi):
             if lo < hi and q == "A":
@@ -314,161 +341,157 @@ def rank_program(g, core, T, topo):
             elif lo < hi:
                 cp(R("G", 16 * lo, 16 * hi), IND(win, R(SX, lo, hi)))
 
-        def own(b, lo, hi, src):
-            mm(R("pC%d" % b, lo, hi), R("IDN", 0, 128), src, True, True)
+        def minus_own():
+            if u == 1:
+                mm(R(pD, 0, L), R("NEG", 0, 128), R("CY0", 0, L), True, False)
+                mm(R(pD, 0, L), R("IDN", 0, 128), R("RE0", 0, L), False, False)
+            elif u == 2:
+                mm(R(pD, 0, LE), R("NEG", 0, 128), R("C", 1856, 1856 + LE), True, False)
+                mm(R(pD, LE, L), R("NEG", 0, 128), R("land", 0, LP), False, False)
+            else:
+                mm(R(pD, 0, L), R("NEG", 0, 128), R("CN2", 0, L) if u else R("C", 1680, 1856), True, False)
 
         gather("A", 0, n0 - h0)
         gather("A", n0, L - h1)
-        if u == 0:
-            convert("C", "CI", cut[2], cut[3])
-        else:
-            changes(u - 1)
-            if u % 2:
-                high(u, "EA")
-            new_counts(u - 1)
-            if u == 2:
-                send()
-            if u == 3:
-                store_links("S", B, B + 2 * M)
-                store_counts("S", B + 2 * M, W - M)
-        own(0, 0, n0, R("C", x, x + n0))
         if u == 2:
-            own(1, 0, LE - n0, R("C", x + n0, x + LE))
-            act(R("pC1", LE - n0, n1), R("land", 0, LP), AF.Copy)
+            new_counts(1)
+            send()
+        if u == 3:
+            new_counts(2)
+        if u:
+            number(u - 1)
+        if u == 1:
+            mm(R("pC0", 0, L), R("IDN", 0, 128), R("CY0", 0, L), True, False)
+            mm(R("pC0", 0, L), R("NEG", 0, 128), R("RE0", 0, L), False, False)
+            for i in range(16):
+                mm(R("pC0", i, L, 16), R("RSEL", 128 * i, 128 * i + 128), R("KILL", 0, nt), False, i == 15)
         else:
-            own(1, 0, n1, R("C", x + n0, x + L))
-            mm(R("pY", 0, L), R("IDN", 0, 128), R("S", x, x + L), True, False)
-            mm(R("pY", 0, L), R("IDN", 0, 128), R("EA", 0, L), False, True)
-            act(R(SV, 0, L), R("pY", 0, L), AF.Identity, 1.0, 1.0)
+            src, x = (("C", 1680), None, ("C", 1856), ("CN2", 0))[u]
+            for d in range(rep):
+                mm(R("pC0", d, rep * n0, rep), R("IDN", 0, 128), R(src, x, x + n0), True, True)
+            end = min(L, LE)
+            mm(R(own[1][0], own[1][1], own[1][1] + end - n0), R("IDN", 0, 128), R(src, x + n0, x + end), True, True)
+        if u:
+            spread_numbers(u - 1)
+        if u != 2:
+            minus_own()
+        mm(R("pX", 0, L), R("IDB", 0, 128), R("MASKC", 0, L), True, False)
+        mm(R("pO", 0, n0), R("ROWS", 0, 128, 1, 1), R("ONEB", 0, n0, 1, 1), True, False)
         gather("V", n0 - h0, n0)
+        if u:
+            change_links(u - 1)
         if u == 0:
-            ts(R("TRX", 0, 16), R("TR", 0, 16), 1.0, O.add)
-            ts(R("TRM", 0, 16), R("TR", 0, 16), -16.0, O.mult)
-            act(R("S", 1856, B), IND(R("SI", 0, B), R("IDL", 1856 // 16, B // 16)), AF.Copy)
-            act(R("S", 0, 1680), IND(R("SI", 0, B), R("IDL", 0, 1680 // 16)), AF.Copy)
+            convert("C", 0, "CI", 0, 1680)
+            convert("C", 1856, "CI", 1856, B)
+        if u == 1:
+            old_links_out(1680, 1856)
         if u == 2:
-            link_changes(1)
+            store("S", "yc", TOP, R("CN1", 0, M))
+        if u == 3:
+            old_links_out(1856, TOP)
+            store("S", "yc", TOP + M, R("CN2", 0, M))
 
         def keys(b, k):
-            nl, l0 = CHUNKS[u][b], b * n0
-            tt(R("MN", 16 * l0 + k * nl, 16 * l0 + (k + 1) * nl), R("G", 16 * l0 + k, 16 * (l0 + nl), 16),
-               R("pC%d" % b, 0, nl), O.min)
+            nl, l0, r = CHUNKS[u][b], b * n0, (rep, 1)[b]
+            a = 16 * l0 + k * r * nl
+            tt(R("MN", a, a + r * nl), R("G", 16 * l0 + k, 16 * (l0 + nl), 16 // r), own[b], O.min)
             if k == 0:
-                mm(R("pK%d" % b, 0, 136, 1, nl), R("ONEB", 0, nl, 1, 1), R("BIAS", 0, 136, 1, 1), True, False)
-            mm(R("pK%d" % b, k, 136, 17, nl), R("MN", 16 * l0 + k * nl, 16 * l0 + (k + 1) * nl), R("KEY8", 0, 8),
-               False, k == 15)
+                mm(R("pK%d" % b, 0, 128, 1, nl), R("ONEB", 0, nl, 1, 1), R("BIAS", 0, 128, 1, 1), True, False)
+            for d in range(r):
+                mm(R("pK%d" % b, k + d * 16 // r, 128, 16, nl), R("MN", a + d, a + r * nl, r), R("KEY8", 0, 8),
+                   False, k == 16 // r - 1 and d == r - 1)
 
-        def best(b):
-            nl = CHUNKS[u][b]
-            K, X = "pK%d" % b, "PMX%d" % b
-            scan(R(X, 0, 136, 1, nl), R("SEG", 0, 136, 1, nl), R(K, 0, 136, 1, nl), 0.0, O.mult, O.max)
-            for j in range(8):
-                ts(R("OH%d" % b, 16 * j, 16 * j + 16, 1, nl), R(K, 17 * j, 17 * j + 16, 1, nl),
-                   R(X, 17 * j + 16, 17 * j + 17, 1, nl), O.is_equal)
-            mm(R("pO%d" % b, 0, nl), R("OH%d" % b, 0, 128, 1, nl), R("IDB", 0, nl, 1, nl), True, True)
-
-        def pick(b):
+        def best(b, part):
             nl, l0 = CHUNKS[u][b], b * n0
-            tt(R("PR", l0, l0 + nl), R("pO%d" % b, 0, nl), R(SV, l0, l0 + nl), O.mult)
-            act(R("OS", l0, l0 + nl), R("pO%d" % b, 0, nl), AF.Copy)
+            K, X, H = "pK%d" % b, R("XB%d" % b, 0, 128, 1, nl), R("OH%d" % b, 0, 128, 1, nl)
+            if part == 0:
+                scan(R(K, 128, 256, 1, nl), R("SEGK", 0, 128, 1, nl), R(K, 0, 128, 1, nl), big, O.min, O.max)
+            elif part == 1:
+                scan(R(X[0], 0, 128, -1, nl), R("SEGK", 0, 128, 1, nl), R(K, 128, 256, -1, nl), big, O.min, O.max)
+            elif part == 2:
+                tt(H, R(K, 0, 128, 1, nl), X, O.is_equal)
+                if b == 0:
+                    mm(R("pN", 0, L), R("ROWS", 128 * u + 128, 128 * u + 256, 1, 1), R("ONEB", 0, L, 1, 1), True, False)
+                mm(R("pO", l0, l0 + nl), H, R("ID4", 0, nl, 1, nl), False, True)
+                mm(R("pN", l0, l0 + nl), H, R("ID4", 0, nl, 1, nl), False, False)
+            else:
+                tt(R("PR", l0, l0 + nl), R("pO", l0, l0 + nl), R(SV, l0, l0 + nl), O.min)
+                if b == 0:
+                    mm(R("pO", n0, L), R("ROWS", 0, 128, 1, 1), R("ONEB", 0, n1, 1, 1), True, False)
 
-        for k in range(16):
+        for k in range(16 // rep):
             keys(0, k)
         if u == 2:
-            add_links(1)
-        if u % 2:
-            lo, hi = ((1680, 1856), (1856, B))[u // 2]
-            link_changes(u - 1)
-            add_links(u - 1)
-            store_links("S", lo, hi)
+            mm(R("pC1", LE - n0, n1), R("IDN", 0, 128), R("land", 0, LP), True, True)
         gather("V", L - h1, L)
         for k in range(16):
-            if k == BEST[u][0]:
-                best(0)
+            for part in range(4):
+                if BEST[u][part] == k:
+                    best(0, part)
             keys(1, k)
-            if k == BEST[u][1]:
-                pick(0)
-        ts(R("TB", 0, 16), R("TRM", 0, 16), 16.0 * (B + M * u - 1), O.add)
-        best(1)
-        pick(1)
-        mm(R("pY", 0, L), R("BB1", 0, 128), R("PR", 0, L), True, True)
-        for i in range(16):
-            mm(R("pK0", 256, 256 + nt), R("BSEL", 128 * i, 128 * i + 128), R("PR", i, L, 16), i == 0, i == 15)
-        cp(R("YR", 0, L), R("pY", 0, L))
-        ts(R("DEAD", 0, L), R("YR", 0, L), 0.0, O.is_equal)
-        mm(R("pW", 0, L), R("BBIG", 0, 128), R("DEAD", 0, L), True, False)
-        cp(R("YO", 0, nt), R("pK0", 256, 256 + nt))
-        ts(R("YF", 0, nt), R("YO", 0, nt), 0.0, O.is_lt, 4096.0, O.mult)
-
-        def same(t):
-            o = 256 * t
-            ts(R("EQ", o + 16 * t, o + L), R("YR", 16 * t, L), R("YO", t, t + 1), O.is_equal)
-            mm(R("pW", 16 * t, 16 * t + 16), R("WGT", 0, 128), R("EQ", o + 16 * t, o + 16 * t + 16), False, t == nt - 1)
-            if t < nt - 1:
-                mm(R("pW", 16 * t + 16, L), R("BBIG", 0, 128), R("EQ", o + 16 * t + 16, o + L), False, False)
-        same(0)
-        tt(R("YD", 0, nt), R("YF", 0, nt), R("YO", 0, nt), O.add)
-        same(1)
-        ts(R("YG", 0, nt), R("YD", 0, nt), -1.0, O.add, 0.0, O.max)
-        act(R("CY", 0, L), IND(win, R("YG", 0, nt)), AF.Copy)
-        act(R(SY, 0, L), IND(R("S" if u else "SI", 0, wide), R("YG", 0, nt)), AF.Copy)
-        for t in range(2, nt):
-            same(t)
-        tt(R("DX", 0, nt), R("YD", 0, nt), R("TRX", 0, nt), O.subtract)
-        if u % 2:
-            l0 = 0
-            for b, nl in enumerate(CHUNKS[u]):
-                tt(R("DD", l0, l0 + nl), R("CY", l0, l0 + nl), R("pC%d" % b, 0, nl), O.subtract)
-                l0 += nl
-            act(R("REST", 0, L), R("DD", 0, L), AF.Relu)
-        ts(R("D16", 0, nt), R("DX", 0, nt), 16.0, O.mult)
-        tt(R("RS", L, 2 * L), R("pW", 0, L), R("THR", 0, L), O.is_lt)
-        scan(R("RS", 0, L), R("ONEB", 0, L), R("RS", L, 2 * L), 0.0, O.mult, O.add)
-        for i in range(16):
-            mm(R("pK1", 256, 256 + 2 * nt), R("BSEL", 128 * i, 128 * i + 128), R("RS", i, 2 * L, 16), i == 0, i == 15)
-        if u == 0:
-            lists(2)
-            high(2, "EA2")
-        if u == 1:
-            tt(R("EV2", 0, LANES[2]), R("EA2", 0, LANES[2]), R("S", XCOL[2], XCOL[2] + LANES[2]), O.add)
-            ts(R("SV2", 0, LANES[2]), R("EV2", 0, LANES[2]), 1.0, O.add)
         if u == 2:
-            new_links(1)
-        if u % 2 == 0:
-            ent = min(L, LE)
-            mm(R("pY", 0, L), R("IDN", 0, 128), R("CY", 0, L), True, False)
-            mm(R("pY", 0, ent), R("NEG", 0, 128), R("C", x, x + ent), False, ent == L)
-            if ent < L:
-                mm(R("pY", ent, L), R("NEG", 0, 128), R("land", 0, LP), False, True)
-            act(R("REST", 0, L), R("pY", 0, L), AF.Relu)
+            minus_own()
+        for part, place in enumerate("FROP"):
+            best(1, part)
+            if part == 2:
+                mm(R("pK1", 256, 288), R("ONEB", 0, 128, 1, 1), R("CU", 0, 32, 1, 1), True, False)
+            if part == 3:
+                mm(R("pX", 0, L), R("BB1", 0, 128), R("PR", 0, L), False, True)
+                mm(R("pK0", 256, 256 + L), R("BB1", 0, 128), R("PR", 0, L), True, True)
+            later(place)
+        act(R("YR", 0, L), R("pK0", 256, 256 + L), AF.Identity, 1.0, 30720.0)
+        act(R("DEAD", 0, L), R("pK0", 256, 256 + L), AF.Relu, -big, -32767.0 * big)
+        scan(R("YX", 0, L), R("SEGY", 0, L), R("pX", 0, L), big, O.min, O.max)
+        later("Y")
+        act(R("YG", 0, nt), R("YX", 15, L, 16), AF.Relu, 1.0, HALF)
+        act(R("YF", 0, nt), R("YX", 15, L, 16), AF.Relu, 1.0, HALF)
+        act(R(CY, 0, L), IND(win, R("YG", 0, nt)), AF.Copy)
+        act(R(SY, 0, L), IND(R("SI", 0, wide), R("YG", 0, nt)), AF.Copy)
+        if u == 0:
+            act(R("SX1", 0, L), R(SY, 0, L), AF.Copy)
+            act(R("SV1", 0, L), R(SY, 0, L), AF.Identity, 1.0, -HALF)
 
-        if L > M:
-            ts(R("F", 0, nt), R("pK1", 256, 256 + nt), 16.0 * M + 0.5, O.is_le, 1.0 / 256, O.mult)
-            tt(R("U16", 0, nt), R("pK1", 256, 256 + nt), R("TB", 0, nt), O.add)
-            tt(R("S2", 0, nt), R("F", 0, nt), R("pK1", 256 + nt, 256 + 2 * nt), O.mult)
+        for t in range(nt):
+            o = 256 * t
+            ts(R("EQ", o + 16 * t, o + L), R("YR", 16 * t, L), R("YX", 16 * t + 15, 16 * t + 16), O.is_equal,
+               R("WT", t, t + 1), O.mult)
+            if t == nt - 1:
+                mm(R("pW", 0, L), R("IDH", 0, 128), R("DEAD", 0, L), False, False)
+            mm(R("pW", 16 * t, L), R("BONB", 0, 128), R("EQ", o + 16 * t, o + L), t == 0, t == nt - 1)
+        mm(R(pD, 0, L), R("IDN", 0, 128), R(CY, 0, L), False, True)
+        act(R(RE, 0, L), R(pD, 0, L), AF.Relu)
+        later("E")
+        tt(R("FM", 0, L), R("pW", 0, L), R("THR", 0, L), O.is_lt)
+        later("L")
+        scan(R("RS", 16, 16 + L), R("ONEB", 0, L), R("FM", 0, L), 0.0, O.mult, O.add)
+        for at, l1, l2 in ((256, "L1A", "L2A"), (272, "L1N", "L2N")):
+            mm(R("pK1", at, at + nt), R(l1, 0, 128), R("RS", 31, 16 + L, 16), False, False)
+            mm(R("pK1", at, at + nt), R(l2, 0, 128), R("RS", 15, L, 16), False, at == 272)
+        later("S")
+
+        tt(R("Z", 0, nt), R("pK1", 256, 256 + nt), R("TR", 0, nt), O.min)
+        later("Z")
+        act(R("KR", 0, nt), R("Z", 0, nt), AF.Relu)
+        act(R("KILL", 0, nt), R("KR", 0, nt), AF.Copy, -32.0)
+        if u == 2:
+            tt(R(LN, 0, nt), R("pK1", 272, 272 + nt), R("Z", 0, nt), O.max)
+            tt(R("LY", 0, nt), R("YF", 0, nt), R("Z", 0, nt), O.max)
+            new_links(2)
+            act(R("SX3", 0, M), R("SN2", 0, M), AF.Copy)
+            act(R("SV3", 0, M), R("SN2", 0, M), AF.Identity, 1.0, -HALF)
         else:
-            ts(R("S2", 0, nt), R("pK1", 256 + nt, 256 + 2 * nt), 1.0 / 256, O.mult)
-            tt(R("U16", 0, nt), R("pK1", 256, 256 + nt), R("TB", 0, nt), O.add)
-        tt(R("WY", 0, nt), R("D16", 0, nt), R("S2", 0, nt), O.mult)
-        tt(R("WN", 0, nt), R("U16", 0, nt), R("S2", 0, nt), O.mult)
-        tt(R("LFY", 0, nt), R("WY", 0, nt), R("TR", 0, nt), O.add)
-        if u % 2:
-            cp(R("LY", 0, nt), R("LFY", 0, nt))
-            cp(IND(R("C", 0, E), R("LY", 0, nt)), R("REST", 0, L))
-        tt(R("LFN", 0, nt), R("WN", 0, nt), R("TR", 0, nt), O.add)
-        ts(R("LN", 0, nt), R("LFN", 0, nt), -float(B + M * u), O.add)
-        if u % 2 == 0:
-            cp(R("LY", 0, nt), R("LFY", 0, nt))
-            new_links(u)
-            lists(u + 1)
-            cp(IND(R("C", 0, E), R("LY", 0, nt)), R("REST", 0, L))
+            tt(R("LY", 0, nt), R("YF", 0, nt), R("Z", 0, nt), O.max)
+            tt(R(LN, 0, nt), R("pK1", 272, 272 + nt), R("Z", 0, nt), O.max)
+        cp(IND(R("C", 0, SPARE), R("LY", 0, nt)), R(RE, 0, L))
 
-    store_counts("S", 0, B + 2 * M)
-    changes(3)
+    store("S", "yc", 0, R("C", 0, TOP))
+    store("A", "ys", TOP - 1680, R("SN1", 0, M))
+    number(3)
+    spread_numbers(3)
     new_counts(3)
-    store_counts("A", W - M, W)
+    store("A", "yc", TOP + 2 * M, R("CN3", 0, M))
+    change_links(3)
+    store("A", "ys", TOP + M - 1680, R("SN2", 0, M))
     new_links(3)
-    link_changes(3)
-    add_links(3)
-    store_links("S", B + 2 * M, W)
+    store("A", "ys", TOP + 2 * M - 1680, R("SN3", 0, M))
     m["finish"](sent)

@@ -8,20 +8,22 @@ HALF = 1376.0
 LANES = (176, 176, 256, 160)
 WIDE = (B, B, B, TOP)
 CHUNKS = ((48, 128), (48, 128), (128, 128), (32, 128))
-TWICE = (1, 1, 1, 2)
-SHARE = ((32, 32), (32, 32), (48, 16), (0, 16))
-BEST = ((0, 2, 4, 12), (2, 4, 6, 10), (0, 2, 4, 12), (4, 7, 10, 14))
+TWICE = (2, 1, 1, 2)
+SHARE = ((24, 32, 16), (24, 32, 16), (56, 8, 8), (16, 16, 24))
+BEST = ((16, 17, 18), (16, 17, 18), (16, 17, 18), (16, 17, 18))
+MID = (5, 10, 15, 5)
+PORTS = 12
 
 SCRATCH = {}
 PSUM = ("pK0", "pK1", "pC0", "pC1", "pO", "pX", "pW", "pN")
 for _names, _w, _t in (
         ("CI", B, "int32"), ("SI", B + SPARE, "int32"), ("C", B + SPARE, "float32"), ("PI PA", 1, "int32"),
-        ("CN1 CN2 CN3 SN1 SN2 SN3", SPARE, "float32"), ("SO", TOP - 1680, "float32"),
+        ("CN1 CN2 CN3 SN1", SPARE, "float32"), ("SN2", M + SPARE, "float32"), ("SO", TOP - 1680, "float32"),
         ("G MN", 4096, "float32"), ("EQ", 4096, "bfloat16"), ("land", LP, "float32"),
         ("DEAD ONEB FM MASKC", 256, "bfloat16"), ("RS", 272, "bfloat16"),
         ("CY0 CY1 CY2 CY3 SY0 SY1 SY2 SY3 RE0 RE1 RE2 RE3 YX THR DM I256 SEGY RA RB RW", 256, "float32"),
         ("PR YR SV0 SV1 SV2 SV3", 256, "float16"), ("SX0 SX1 SX2 SX3", 256, "uint16"),
-        ("OH0 OH1 IDB ID4 IDH BONB BIAS L1A L2A L1N L2N", 128, "bfloat16"), ("BB1", 128, "float16"),
+        ("OH0 OH1 IDB ID4 NE4 IDH BONB BIAS L1A L2A L1N L2N", 128, "bfloat16"), ("BB1", 128, "float16"),
         ("ROWS", 640, "bfloat16"), ("CU", 32, "bfloat16"), ("RSEL", 2048, "bfloat16"),
         ("XB0 XB1 SEGK ONEF BH BONES B4 LA LB IDN NEG", 128, "float32"),
         ("YF Z KR I16 IDP TR WT WA WH WD", 16, "float32"), ("KILL Q", 16, "bfloat16"),
@@ -250,6 +252,7 @@ def rank_program(g, core, T, topo):
     ts(R("WH", 0, 1), R("WD", 0, 1), 1.0 / big, O.mult, 0.25 / big, O.mult)
     ts(R("WT", 0, 16), R("RW", 0, 256, 16), R("WH", 0, 1), O.mult)
     act(R("ID4", 0, 128), R("IDN", 0, 128), AF.Copy, 4096.0)
+    act(R("NE4", 0, 128), R("IDN", 0, 128), AF.Copy, -4096.0)
     act(R("IDB", 0, 128), R("IDN", 0, 128), AF.Copy)
     act(R("IDH", 0, 128), R("IDN", 0, 128), AF.Copy, 2.0 * big)
     act(R("NEG", 0, 128), R("IDN", 0, 128), AF.Copy, -1.0)
@@ -266,12 +269,12 @@ def rank_program(g, core, T, topo):
     keep(R("L1A", 0, 128), R("LA", 0, 128), [[-1, 128]], O.not_equal, -255.0 * 4096, 0, 1)
     keep(R("L2A", 0, 128), R("LB", 0, 128), [[-1, 128]], O.not_equal, 256.0 * 4096, 0, 1)
     iota(R("SI", B, TOP), [[0, M]], 0, 0, False)
-    for r in (R("C", B, TOP), R("CN1", 0, M), R("CN2", 0, M), R("SN2", 0, M), R("SN1", 0, M), R("CN3", 0, M), R("SN3", 0, M)):
-        iota(r, [[0, M]], 0, 0, True)
+    for r in (R("C", B, TOP), R("CN1", 0, M), R("CN2", 0, M), R("SN2", 0, 2 * M), R("SN1", 0, M), R("CN3", 0, M)):
+        iota(r, [[0, r[2] - r[1]]], 0, 0, True)
     cp(R("C", 1680, 1856), R("CI", 1680, 1856))
 
     NEWC = (R("C", B, B + SPARE), R("CN1", 0, SPARE), R("CN2", 0, SPARE), R("CN3", 0, SPARE))
-    NEWS = (R("SI", B, B + SPARE), R("SN1", 0, SPARE), R("SN2", 0, SPARE), R("SN3", 0, SPARE))
+    NEWS = (R("SI", B, B + SPARE), R("SN1", 0, SPARE), R("SN2", 0, SPARE), R("SN2", M, M + SPARE))
     OLDS = (R("SI", 1680, 1856), R("SY0", 0, LE), R("SI", 1856, B), R("SN2", 0, M))
 
     def new_counts(u, lo=0, hi=16):
@@ -310,26 +313,28 @@ def rank_program(g, core, T, topo):
         store("S", "ys", lo - 1680, R("SO", lo - 1680, hi - 1680))
 
     LATER = {
-        0: {"F": [lambda: cp(R("SX2", 0, 256), R("SI", 1856, B))],
+        0: {"K": [lambda: cp(R("SX2", 0, 256), R("SI", 1856, B))],
             "O": [lambda: ts(R("SV2", 0, 256), R("SI", 1856, B), -HALF, O.add)]},
-        1: {"F": [lambda: new_counts(0, 0, 2)], "R": [lambda: new_counts(0, 2, 4)], "O": [lambda: new_counts(0, 4, 8)],
-            "P": [lambda: new_counts(0, 8, 11)]},
-        2: {"F": [lambda: new_links(0, 0, 2)], "R": [lambda: new_links(0, 2, 4)], "O": [lambda: new_links(0, 4, 8)],
-            "P": [lambda: new_links(0, 8, 11)]},
-        3: {"F": [lambda: new_links(1, 0, 2)], "R": [lambda: new_links(1, 2, 4)], "O": [lambda: new_links(1, 4, 8)],
-            "P": [lambda: new_links(1, 8, 11)]},
+        1: {"K": [lambda: change_links(0), lambda: old_links_out(1680, 1856)], "O": [lambda: new_counts(0, 0, 4)],
+            "P": [lambda: new_counts(0, 4, 8)], "E": [lambda: new_counts(0, 8, 11)]},
+        2: {"K": [lambda: change_links(1)],
+            "O": [lambda: new_links(0, 0, 4)], "P": [lambda: new_links(0, 4, 8)], "Y": [lambda: new_links(1, 0, 2)],
+            "E": [lambda: new_links(0, 8, 11), lambda: old_links_out(B, TOP), lambda: new_links(1, 2, 4)],
+            "L": [lambda: new_links(1, 4, 6)],
+            "S": [lambda: new_links(1, 6, 11), lambda: store("S", "ys", TOP - 1680, R("SN1", 0, M))]},
+        3: {"K": [lambda: change_links(2), lambda: old_links_out(1856, B)]},
     }
 
     for u in range(4):
         L, wide = LANES[u], WIDE[u]
         nt = L // 16
         n0, n1 = CHUNKS[u]
-        h0, h1 = SHARE[u]
+        h0, h1, h2 = SHARE[u]
         rep = TWICE[u]
         win = R("C" if u else "CI", 0, wide)
         SX, SV, SY, CY, RE, LN = ("%s%d" % (a, u) for a in ("SX", "SV", "SY", "CY", "RE", "LN"))
-        own = (R("pC0", 0, rep * n0), R("pC1", 0, n1) if u == 2 else R("pC0", rep * n0, rep * n0 + n1))
-        pD = "pC0" if u == 2 else "pC1"
+        own = (R("pC0", 0, rep * n0), R("pC0", n0, L) if u == 1 else R("pC1", 0, n1))
+        pD = "pC1" if u == 1 else "pC0"
 
         def later(place):
             for call in LATER[u].get(place, []):
@@ -352,51 +357,43 @@ def rank_program(g, core, T, topo):
                 mm(R(pD, 0, L), R("NEG", 0, 128), R("CN2", 0, L) if u else R("C", 1680, 1856), True, False)
 
         gather("A", 0, n0 - h0)
-        gather("A", n0, L - h1)
+        gather("A", n0, L - h2 - h1)
         if u == 2:
             new_counts(1)
             send()
+            number(1)
         if u == 3:
             new_counts(2)
-        if u:
-            number(u - 1)
+        for b, nl in enumerate(CHUNKS[u]):
+            mm(R("pK%d" % b, 0, 128, 1, nl), R("ONEB", 0, nl, 1, 1), R("BIAS", 0, 128, 1, 1), True, False)
         if u == 1:
             mm(R("pC0", 0, L), R("IDN", 0, 128), R("CY0", 0, L), True, False)
             mm(R("pC0", 0, L), R("NEG", 0, 128), R("RE0", 0, L), False, False)
             for i in range(16):
                 mm(R("pC0", i, L, 16), R("RSEL", 128 * i, 128 * i + 128), R("KILL", 0, nt), False, i == 15)
+            spread_numbers(0)
         else:
             src, x = (("C", 1680), None, ("C", 1856), ("CN2", 0))[u]
             for d in range(rep):
                 mm(R("pC0", d, rep * n0, rep), R("IDN", 0, 128), R(src, x, x + n0), True, True)
             end = min(L, LE)
             mm(R(own[1][0], own[1][1], own[1][1] + end - n0), R("IDN", 0, 128), R(src, x + n0, x + end), True, True)
-        if u:
-            spread_numbers(u - 1)
-        if u != 2:
-            minus_own()
-        mm(R("pX", 0, L), R("IDB", 0, 128), R("MASKC", 0, L), True, False)
-        mm(R("pO", 0, n0), R("ROWS", 0, 128, 1, 1), R("ONEB", 0, n0, 1, 1), True, False)
+        if u == 2:
+            spread_numbers(1)
         gather("V", n0 - h0, n0)
-        if u:
-            change_links(u - 1)
+        gather("V", L - h2, L)
         if u == 0:
             convert("C", 0, "CI", 0, 1680)
             convert("C", 1856, "CI", 1856, B)
-        if u == 1:
-            old_links_out(1680, 1856)
         if u == 2:
             store("S", "yc", TOP, R("CN1", 0, M))
         if u == 3:
-            old_links_out(1856, TOP)
             store("S", "yc", TOP + M, R("CN2", 0, M))
 
         def keys(b, k):
             nl, l0, r = CHUNKS[u][b], b * n0, (rep, 1)[b]
             a = 16 * l0 + k * r * nl
             tt(R("MN", a, a + r * nl), R("G", 16 * l0 + k, 16 * (l0 + nl), 16 // r), own[b], O.min)
-            if k == 0:
-                mm(R("pK%d" % b, 0, 128, 1, nl), R("ONEB", 0, nl, 1, 1), R("BIAS", 0, 128, 1, 1), True, False)
             for d in range(r):
                 mm(R("pK%d" % b, k + d * 16 // r, 128, 16, nl), R("MN", a + d, a + r * nl, r), R("KEY8", 0, 8),
                    False, k == 16 // r - 1 and d == r - 1)
@@ -408,37 +405,51 @@ def rank_program(g, core, T, topo):
                 scan(R(K, 128, 256, 1, nl), R("SEGK", 0, 128, 1, nl), R(K, 0, 128, 1, nl), big, O.min, O.max)
             elif part == 1:
                 scan(R(X[0], 0, 128, -1, nl), R("SEGK", 0, 128, 1, nl), R(K, 128, 256, -1, nl), big, O.min, O.max)
-            elif part == 2:
-                tt(H, R(K, 0, 128, 1, nl), X, O.is_equal)
-                if b == 0:
-                    mm(R("pN", 0, L), R("ROWS", 128 * u + 128, 128 * u + 256, 1, 1), R("ONEB", 0, L, 1, 1), True, False)
-                mm(R("pO", l0, l0 + nl), H, R("ID4", 0, nl, 1, nl), False, True)
-                mm(R("pN", l0, l0 + nl), H, R("ID4", 0, nl, 1, nl), False, False)
             else:
-                tt(R("PR", l0, l0 + nl), R("pO", l0, l0 + nl), R(SV, l0, l0 + nl), O.min)
-                if b == 0:
-                    mm(R("pO", n0, L), R("ROWS", 0, 128, 1, 1), R("ONEB", 0, n1, 1, 1), True, False)
+                tt(H, R(K, 0, 128, 1, nl), X, O.is_equal)
+
+        def turn(to, b, stop):
+            nl, l0 = CHUNKS[u][b], b * n0
+            mm(R(to, l0, l0 + nl), R("OH%d" % b, 0, 128, 1, nl), R("ID4", 0, nl, 1, nl), False, stop)
+
+        def row(to, i):
+            mm(R(to, 0, L), R("ROWS", 128 * i, 128 * i + 128, 1, 1), R("ONEB", 0, L, 1, 1), True, False)
 
         for k in range(16 // rep):
             keys(0, k)
-        if u == 2:
-            mm(R("pC1", LE - n0, n1), R("IDN", 0, 128), R("land", 0, LP), True, True)
-        gather("V", L - h1, L)
+            if k == MID[u]:
+                gather("V", L - h2 - h1, L - h2)
+            if u == 2 and k == PORTS:
+                mm(R("pC1", LE - n0, n1), R("IDN", 0, 128), R("land", 0, LP), True, True)
         for k in range(16):
-            for part in range(4):
+            for part in range(3):
                 if BEST[u][part] == k:
                     best(0, part)
             keys(1, k)
-        if u == 2:
-            minus_own()
-        for part, place in enumerate("FROP"):
-            best(1, part)
-            if part == 2:
-                mm(R("pK1", 256, 288), R("ONEB", 0, 128, 1, 1), R("CU", 0, 32, 1, 1), True, False)
-            if part == 3:
-                mm(R("pX", 0, L), R("BB1", 0, 128), R("PR", 0, L), False, True)
-                mm(R("pK0", 256, 256 + L), R("BB1", 0, 128), R("PR", 0, L), True, True)
+        row("pO", 0)
+        mm(R("pX", 0, L), R("IDB", 0, 128), R("MASKC", 0, L), True, False)
+        minus_own()
+        for i, place in enumerate("KFR"):
+            for part in range(3):
+                if BEST[u][part] == 16 + i:
+                    best(0, part)
             later(place)
+            if i == 2:
+                turn("pO", 0, False)
+            best(1, i)
+        turn("pO", 1, True)
+        row("pN", u + 1)
+        turn("pN", 0, False)
+        turn("pN", 1, False)
+        if u % 2:
+            mm(R("pK1", 256, 272), R("IDN", 0, 128), R("TR", 0, 16), True, False)
+        else:
+            mm(R("pK1", 256, 272), R("ONEB", 0, 128, 1, 1), R("CU", 0, 16, 1, 1), True, False)
+        later("O")
+        tt(R("PR", 0, L), R("pO", 0, L), R(SV, 0, L), O.min)
+        mm(R("pX", 0, L), R("BB1", 0, 128), R("PR", 0, L), False, True)
+        mm(R("pK0", 256, 256 + L), R("BB1", 0, 128), R("PR", 0, L), True, True)
+        later("P")
         act(R("YR", 0, L), R("pK0", 256, 256 + L), AF.Identity, 1.0, 30720.0)
         act(R("DEAD", 0, L), R("pK0", 256, 256 + L), AF.Relu, -big, -32767.0 * big)
         scan(R("YX", 0, L), R("SEGY", 0, L), R("pX", 0, L), big, O.min, O.max)
@@ -455,43 +466,47 @@ def rank_program(g, core, T, topo):
             o = 256 * t
             ts(R("EQ", o + 16 * t, o + L), R("YR", 16 * t, L), R("YX", 16 * t + 15, 16 * t + 16), O.is_equal,
                R("WT", t, t + 1), O.mult)
-            if t == nt - 1:
-                mm(R("pW", 0, L), R("IDH", 0, 128), R("DEAD", 0, L), False, False)
             mm(R("pW", 16 * t, L), R("BONB", 0, 128), R("EQ", o + 16 * t, o + L), t == 0, t == nt - 1)
+            if t == nt - 4:
+                mm(R("pW", 0, L), R("IDH", 0, 128), R("DEAD", 0, L), False, False)
         mm(R(pD, 0, L), R("IDN", 0, 128), R(CY, 0, L), False, True)
         act(R(RE, 0, L), R(pD, 0, L), AF.Relu)
         later("E")
         tt(R("FM", 0, L), R("pW", 0, L), R("THR", 0, L), O.is_lt)
         later("L")
         scan(R("RS", 16, 16 + L), R("ONEB", 0, L), R("FM", 0, L), 0.0, O.mult, O.add)
-        for at, l1, l2 in ((256, "L1A", "L2A"), (272, "L1N", "L2N")):
+        for at, l1, l2 in ((256, "NE4", "ID4") if u % 2 else (256, "L1A", "L2A"), (272, "L1N", "L2N")):
             mm(R("pK1", at, at + nt), R(l1, 0, 128), R("RS", 31, 16 + L, 16), False, False)
             mm(R("pK1", at, at + nt), R(l2, 0, 128), R("RS", 15, L, 16), False, at == 272)
         later("S")
 
-        tt(R("Z", 0, nt), R("pK1", 256, 256 + nt), R("TR", 0, nt), O.min)
-        later("Z")
-        act(R("KR", 0, nt), R("Z", 0, nt), AF.Relu)
-        act(R("KILL", 0, nt), R("KR", 0, nt), AF.Copy, -32.0)
-        if u == 2:
-            tt(R(LN, 0, nt), R("pK1", 272, 272 + nt), R("Z", 0, nt), O.max)
+        Z, count = R("pK1", 256, 256 + nt), R("pK1", 272, 272 + nt)
+        if u % 2:
+            cp(R("Z", 0, nt), Z)
+            tt(R("LY", 0, nt), Z, R("YF", 0, nt), O.max)
+        else:
+            tt(R("Z", 0, nt), Z, R("TR", 0, nt), O.min)
+        ts(R("KILL", 0, nt), Z, 0.5, O.is_gt, -65536.0, O.mult)
+        if u:
+            tt(R(LN, 0, nt), count, R("Z", 0, nt), O.max)
+        if u % 2 == 0:
             tt(R("LY", 0, nt), R("YF", 0, nt), R("Z", 0, nt), O.max)
+            number(u)
+        if u == 0:
+            tt(R(LN, 0, nt), count, R("Z", 0, nt), O.max)
+        if u == 2:
+            spread_numbers(u)
             new_links(2)
             act(R("SX3", 0, M), R("SN2", 0, M), AF.Copy)
             act(R("SV3", 0, M), R("SN2", 0, M), AF.Identity, 1.0, -HALF)
-        else:
-            tt(R("LY", 0, nt), R("YF", 0, nt), R("Z", 0, nt), O.max)
-            tt(R(LN, 0, nt), R("pK1", 272, 272 + nt), R("Z", 0, nt), O.max)
         cp(IND(R("C", 0, SPARE), R("LY", 0, nt)), R(RE, 0, L))
 
     store("S", "yc", 0, R("C", 0, TOP))
-    store("A", "ys", TOP - 1680, R("SN1", 0, M))
     number(3)
     spread_numbers(3)
     new_counts(3)
     store("A", "yc", TOP + 2 * M, R("CN3", 0, M))
-    change_links(3)
-    store("A", "ys", TOP + M - 1680, R("SN2", 0, M))
     new_links(3)
-    store("A", "ys", TOP + 2 * M - 1680, R("SN3", 0, M))
+    change_links(3)
+    store("A", "ys", TOP + M - 1680, R("SN2", 0, 2 * M))
     m["finish"](sent)

@@ -12,7 +12,6 @@ TWICE = (2, 1, 1, 2)
 SHARE = ((24, 32, 16), (24, 32, 16), (56, 8, 8), (16, 16, 24))
 BEST = ((16, 17, 18), (16, 17, 18), (16, 17, 18), (16, 17, 18))
 MID = (5, 10, 15, 5)
-PORTS = 12
 
 SCRATCH = {}
 PSUM = ("pK0", "pK1", "pC0", "pC1", "pO", "pX", "pW", "pN")
@@ -21,7 +20,7 @@ for _names, _w, _t in (
         ("CN1 CN2 CN3 SN1", SPARE, "float32"), ("SN2", M + SPARE, "float32"), ("SO", TOP - 1680, "float32"),
         ("G MN", 4096, "float32"), ("EQ", 4096, "bfloat16"), ("land", LP, "float32"),
         ("DEAD ONEB FM MASKC", 256, "bfloat16"), ("RS", 272, "bfloat16"),
-        ("CY0 CY1 CY2 CY3 SY0 SY1 SY2 SY3 RE0 RE1 RE2 RE3 YX THR DM I256 SEGY RA RB RW", 256, "float32"),
+        ("CY0 CY1 CY2 CY3 SY0 SY1 SY2 SY3 RE0 RE1 RE2 RE3 YX THR DM I256 SEGY RA RW WX", 256, "float32"),
         ("PR YR SV0 SV1 SV2 SV3", 256, "float16"), ("SX0 SX1 SX2 SX3", 256, "uint16"),
         ("OH0 OH1 IDB ID4 NE4 IDH BONB BIAS L1A L2A L1N L2N", 128, "bfloat16"), ("BB1", 128, "float16"),
         ("ROWS", 640, "bfloat16"), ("CU", 32, "bfloat16"), ("RSEL", 2048, "bfloat16"),
@@ -91,7 +90,7 @@ def machine(g, T):
                     elif not over or (kind == "r" and k2 == "r"):
                         hit = False
                     elif same:
-                        hit = k2 == "w" and q != "P"
+                        hit = q != "P"
                     else:
                         hit = True
                     if hit:
@@ -216,52 +215,48 @@ def rank_program(g, core, T, topo):
     big = float(2 ** 60)
     fill(R("ONEF", 0, 128), 1.0)
     iota(R("PI", 0, 1), [[0, 1]], 0, 1, False)
+    iota(R("I256", 0, 256), [[0, 16], [1, 16]], 0, 0, True)
     keep(R("IDN", 0, 128), R("ONEF", 0, 128), [[-1, 128]], O.is_equal, 0.0, 0, 1)
     keep(R("BH", 0, 128), R("ONEF", 0, 128), [[-16, 8], [0, 16]], O.is_ge, 0.0, 0, 1)
     keep(R("BONES", 0, 128), R("BH", 0, 128), [[16, 8], [0, 16]], O.is_ge, 0.0, 15, -1)
     iota(R("BIAS", 0, 128), [[0, 8], [-1, 16]], 15, 0, True)
     iota(R("T16", 0, B // 16), [[16, B // 16]], 0, 0, True)
-    iota(R("I256", 0, 256), [[0, 16], [1, 16]], 0, 0, True)
+    fill(R("RA", 0, 256), 0.5)
+    fill(R("W0", 0, 1), 2.0 * big)
+    fill(R("SN2", 0, 2 * M), 0.0)
+    ts(R("PA", 0, 1), R("PI", 0, 1), 15, O.bitwise_and)
+    fill(R("RA", 0, 256, 16), 1.0)
+    ts(R("W1", 0, 1), R("W0", 0, 1), big, O.mult)
+    fill(R("SEGY", 0, 256), big)
+    cp(R("PF", 0, 1), R("PA", 0, 1))
+    scan(R("RW", 0, 256), R("RA", 0, 256), R("SN2", 0, 256), R("W1", 0, 1), O.mult, O.add)
+    ts(R("DM", 0, 256), R("I256", 0, 256), R("PF", 0, 1), O.is_equal)
+    fill(R("SEGY", 0, 256, 16), -2047.5)
     fill(R("ONEB", 0, 256), 1.0)
     fill(R("SEGK", 0, 128), big)
-    fill(R("SEGY", 0, 256), big)
-    fill(R("RA", 0, 256), 0.5)
-    fill(R("RB", 0, 256), 0.0)
+    tt(R("THR", 0, 256), R("DM", 0, 256), R("RW", 0, 256), O.mult)
     fill(R("RS", 0, 16), 0.0)
-    fill(R("W0", 0, 1), 2.0 * big)
     fill(R("CU", 0, 16), 4096.0 * (255 - M + 1))
-    fill(R("CU", 16, 32), 0.0)
+    fill(R("SEGK", 0, 128, 16), 1048575.5)
+    ts(R("RA", 0, 256), R("I256", 0, 256), 0.5, O.is_gt)
+    cp(R("SX0", 0, LE), R("SI", 1680, 1856))
+    ts(R("KEY8", 0, 8), R("BONES", 0, 128, 16), 16.0, O.mult)
+    scan(R("WX", 0, 256), R("RA", 0, 256), R("THR", 0, 256), 0.0, O.mult, O.max)
     fill(R("ROWS", 0, 128), -2048.0)
     for u in range(4):
         fill(R("ROWS", 128 * u + 128, 128 * u + 256), float(B + M * u - 4096))
-    fill(R("SEGK", 0, 128, 16), 1048575.5)
-    fill(R("SEGY", 0, 256, 16), -2047.5)
-    fill(R("RA", 0, 256, 16), 1.0)
-    ts(R("W1", 0, 1), R("W0", 0, 1), big, O.mult)
-    ts(R("PA", 0, 1), R("PI", 0, 1), 15, O.bitwise_and)
-    scan(R("RW", 0, 256), R("RA", 0, 256), R("RB", 0, 256), R("W1", 0, 1), O.mult, O.add)
-    cp(R("PF", 0, 1), R("PA", 0, 1))
-    ts(R("KEY8", 0, 8), R("BONES", 0, 128, 16), 16.0, O.mult)
-    ts(R("TR", 0, 16), R("T16", 0, 16), R("PF", 0, 1), O.add, float(TOP), O.add)
-    ts(R("IDL", 0, B // 16), R("T16", 0, B // 16), R("PF", 0, 1), O.add)
-    ts(R("DM", 0, 256), R("I256", 0, 256), R("PF", 0, 1), O.is_equal)
-    cp(R("SX0", 0, LE), R("SI", 1680, 1856))
-    tt(R("THR", 0, 256), R("DM", 0, 256), R("RW", 0, 256), O.mult)
     ts(R("SV0", 0, LE), R("SI", 1680, 1856), -HALF, O.add)
-    top(R("WD", 0, 1), R("THR", 0, 16))
-    ts(R("WH", 0, 1), R("WD", 0, 1), 1.0 / big, O.mult, 0.25 / big, O.mult)
-    ts(R("WT", 0, 16), R("RW", 0, 256, 16), R("WH", 0, 1), O.mult)
+    ts(R("IDL", 0, B // 16), R("T16", 0, B // 16), R("PF", 0, 1), O.add)
+    ts(R("TR", 0, 16), R("T16", 0, 16), R("PF", 0, 1), O.add, float(TOP), O.add)
     act(R("ID4", 0, 128), R("IDN", 0, 128), AF.Copy, 4096.0)
     act(R("NE4", 0, 128), R("IDN", 0, 128), AF.Copy, -4096.0)
     act(R("IDB", 0, 128), R("IDN", 0, 128), AF.Copy)
     act(R("IDH", 0, 128), R("IDN", 0, 128), AF.Copy, 2.0 * big)
     act(R("NEG", 0, 128), R("IDN", 0, 128), AF.Copy, -1.0)
-    act(R("BB1", 0, 128), R("BONES", 0, 128), AF.Copy)
-    act(R("BONB", 0, 128), R("BONES", 0, 128), AF.Copy)
-    act(R("B4", 0, 128), R("BONES", 0, 128), AF.Copy, 4096.0)
     act(R("MASKC", 0, 256), R("DM", 0, 256), AF.Copy, 30720.0)
-    for i in range(16):
-        act(R("RSEL", 128 * i, 128 * i + 128), R("BONES", 0, 128), AF.Copy, R("DM", i, i + 1))
+    act(R("B4", 0, 128), R("BONES", 0, 128), AF.Copy, 4096.0)
+    act(R("BB1", 0, 128), R("BONES", 0, 128), AF.Copy)
+    act(R("BONB", 0, 128), R("BONES", 0, 128), AF.Copy, 0.5)
     keep(R("L1N", 0, 128), R("BONES", 0, 128), [[1, 128]], O.is_gt, 0.0, 0, -1)
     keep(R("L2N", 0, 128), R("BONES", 0, 128), [[-1, 128]], O.is_ge, 0.0, 0, 1)
     keep(R("LA", 0, 128), R("B4", 0, 128), [[1, 128]], O.is_gt, 0.0, 0, -1)
@@ -269,8 +264,11 @@ def rank_program(g, core, T, topo):
     keep(R("L1A", 0, 128), R("LA", 0, 128), [[-1, 128]], O.not_equal, -255.0 * 4096, 0, 1)
     keep(R("L2A", 0, 128), R("LB", 0, 128), [[-1, 128]], O.not_equal, 256.0 * 4096, 0, 1)
     iota(R("SI", B, TOP), [[0, M]], 0, 0, False)
-    for r in (R("C", B, TOP), R("CN1", 0, M), R("CN2", 0, M), R("SN2", 0, 2 * M), R("SN1", 0, M), R("CN3", 0, M)):
-        iota(r, [[0, r[2] - r[1]]], 0, 0, True)
+    iota(R("C", B, TOP), [[0, M]], 0, 0, True)
+    for i in range(16):
+        keep(R("RSEL", 128 * i, 128 * i + 128), R("ONEF", 0, 128), [[-16, 8], [0, 16]], O.is_equal, 0.0, -i, 1)
+    for name in ("CN1", "SN1", "CN2", "CN3"):
+        iota(R(name, 0, M), [[0, M]], 0, 0, True)
     cp(R("C", 1680, 1856), R("CI", 1680, 1856))
 
     NEWC = (R("C", B, B + SPARE), R("CN1", 0, SPARE), R("CN2", 0, SPARE), R("CN3", 0, SPARE))
@@ -379,6 +377,7 @@ def rank_program(g, core, T, topo):
             end = min(L, LE)
             mm(R(own[1][0], own[1][1], own[1][1] + end - n0), R("IDN", 0, 128), R(src, x + n0, x + end), True, True)
         if u == 2:
+            act(R("pC1", LE - n0, n1), R("land", 0, LP), AF.Copy)
             spread_numbers(1)
         gather("V", n0 - h0, n0)
         gather("V", L - h2, L)
@@ -419,8 +418,7 @@ def rank_program(g, core, T, topo):
             keys(0, k)
             if k == MID[u]:
                 gather("V", L - h2 - h1, L - h2)
-            if u == 2 and k == PORTS:
-                mm(R("pC1", LE - n0, n1), R("IDN", 0, 128), R("land", 0, LP), True, True)
+
         for k in range(16):
             for part in range(3):
                 if BEST[u][part] == k:
@@ -465,7 +463,7 @@ def rank_program(g, core, T, topo):
         for t in range(nt):
             o = 256 * t
             ts(R("EQ", o + 16 * t, o + L), R("YR", 16 * t, L), R("YX", 16 * t + 15, 16 * t + 16), O.is_equal,
-               R("WT", t, t + 1), O.mult)
+               R("WX", 16 * t + 15, 16 * t + 16), O.mult)
             mm(R("pW", 16 * t, L), R("BONB", 0, 128), R("EQ", o + 16 * t, o + L), t == 0, t == nt - 1)
             if t == nt - 4:
                 mm(R("pW", 0, L), R("IDH", 0, 128), R("DEAD", 0, L), False, False)

@@ -9,24 +9,24 @@ LANES = (176, 176, 256, 160)
 WIDE = (B, B, B, TOP)
 CHUNKS = ((48, 128), (48, 128), (128, 128), (32, 128))
 TWICE = (2, 1, 1, 2)
-SHARE = ((24, 32, 16), (24, 32, 16), (56, 8, 8), (16, 16, 24))
-BEST = ((16, 17, 18), (16, 17, 18), (16, 17, 18), (16, 17, 18))
-MID = (5, 10, 15, 5)
+SHARE = ((24, 32, 16), (24, 32, 16), (56, 8, 16), (16, 16, 24))
+EARLY = 3
+MID = (6, 12, 10, 5)
 
 SCRATCH = {}
 PSUM = ("pK0", "pK1", "pC0", "pC1", "pO", "pX", "pW", "pN")
 for _names, _w, _t in (
-        ("CI", B, "int32"), ("SI", B + SPARE, "int32"), ("C", B + SPARE, "float32"), ("PI PA", 1, "int32"),
-        ("CN1 CN2 CN3 SN1", SPARE, "float32"), ("SN2", M + SPARE, "float32"), ("SO", TOP - 1680, "float32"),
+        ("CI", B, "int32"), ("SI", TOP, "int32"), ("PI PA", 1, "int32"),
+        ("C CN1 CN2 CN3", SPARE, "float32"), ("SN1", M, "float32"), ("SN2", M + SPARE, "float32"), ("SO", TOP - 1680, "float32"),
         ("G MN", 4096, "float32"), ("EQ", 4096, "bfloat16"), ("land", LP, "float32"),
         ("DEAD ONEB FM MASKC", 256, "bfloat16"), ("RS", 272, "bfloat16"),
-        ("CY0 CY1 CY2 CY3 SY0 SY1 SY2 SY3 RE0 RE1 RE2 RE3 YX THR DM I256 SEGY RA RW WX", 256, "float32"),
+        ("CY0 CY1 CY2 CY3 SY0 SY1 SY2 SY3 RE0 RE1 RE2 RE3 YX THR DM I256 SEGY RA RB WX TS ZX M0", 256, "float32"),
         ("PR YR SV0 SV1 SV2 SV3", 256, "float16"), ("SX0 SX1 SX2 SX3", 256, "uint16"),
         ("OH0 OH1 IDB ID4 NE4 IDH BONB BIAS L1A L2A L1N L2N", 128, "bfloat16"), ("BB1", 128, "float16"),
         ("ROWS", 640, "bfloat16"), ("CU", 32, "bfloat16"), ("RSEL", 2048, "bfloat16"),
         ("XB0 XB1 SEGK ONEF BH BONES B4 LA LB IDN NEG", 128, "float32"),
-        ("YF Z KR I16 IDP TR WT WA WH WD", 16, "float32"), ("KILL Q", 16, "bfloat16"),
-        ("YG LY LN0 LN1 LN2 LN3", 16, "uint16"), ("T16", B // 16, "float32"), ("IDL", B // 16, "uint16"),
+        ("YF Z TR JB SUMS", 16, "float32"), ("KILL Q", 16, "bfloat16"),
+        ("YG LY LN1 LN2 LN3 FROM0 FROM1", 16, "uint16"), ("T16", B // 16, "float32"), ("IDL", B // 16, "uint16"),
         ("KEY8", 8, "float32"), ("PF W0 W1 ZERO", 1, "float32")):
     for _n in _names.split():
         SCRATCH[_n] = ("sbuf", [128, _w], _t)
@@ -125,9 +125,9 @@ def machine(g, T):
                     old = [a for a in old if not (lo <= a[0] and a[1] <= hi)]
                 log[name] = old + [(lo, hi, kind, ch, val, q, compute)]
 
-    def op(q, call, out, reads):
+    def op(q, call, out, reads, also=()):
         rd = spread(reads)
-        wr = [out]
+        wr = [out] + list(also)
         if out[0] == "@":
             wr = [(out[1][0], out[1][1], out[1][2], 2, 128)]
             rd.append(out[2])
@@ -168,6 +168,9 @@ def machine(g, T):
         "P", lambda e: e.matmul(ap(out), ap(l), ap(r), start, stop), out, [l, r])
     m["act"] = lambda out, a, func, scale=1.0, bias=0.0: op(
         "A", lambda e: e.activation(ap(out), ap(a), func, bias=bias, scale=ap(scale)), out, [a, scale])
+    m["signs"] = lambda total, out, a, bias: op(
+        "A", lambda e: e.activation(ap(out), ap(a), ActivationFunctionType.Sign, bias=ap(bias), scale=-2.0,
+                                    accum_out=ap(total)), out, [a, bias], [total])
 
     def remote(call, reads, local, n):
         wait("G", needs("G", reads, [], False))
@@ -223,31 +226,24 @@ def rank_program(g, core, T, topo):
     iota(R("T16", 0, B // 16), [[16, B // 16]], 0, 0, True)
     fill(R("RA", 0, 256), 0.5)
     fill(R("W0", 0, 1), 2.0 * big)
-    fill(R("SN2", 0, 2 * M), 0.0)
+    fill(R("ONEB", 0, 256), 1.0)
     ts(R("PA", 0, 1), R("PI", 0, 1), 15, O.bitwise_and)
     fill(R("RA", 0, 256, 16), 1.0)
     ts(R("W1", 0, 1), R("W0", 0, 1), big, O.mult)
-    fill(R("SEGY", 0, 256), big)
-    cp(R("PF", 0, 1), R("PA", 0, 1))
-    scan(R("RW", 0, 256), R("RA", 0, 256), R("SN2", 0, 256), R("W1", 0, 1), O.mult, O.add)
-    ts(R("DM", 0, 256), R("I256", 0, 256), R("PF", 0, 1), O.is_equal)
-    fill(R("SEGY", 0, 256, 16), -2047.5)
-    fill(R("ONEB", 0, 256), 1.0)
     fill(R("SEGK", 0, 128), big)
-    tt(R("THR", 0, 256), R("DM", 0, 256), R("RW", 0, 256), O.mult)
+    cp(R("PF", 0, 1), R("PA", 0, 1))
+    scan(R("pW", 256, 512), R("RA", 0, 256), R("ONEB", 0, 256), R("W1", 0, 1), O.mult, O.mult)
+    ts(R("DM", 0, 256), R("I256", 0, 256), R("PF", 0, 1), O.is_equal)
     fill(R("RS", 0, 16), 0.0)
     fill(R("CU", 0, 16), 4096.0 * (255 - M + 1))
+    fill(R("CU", 16, 32), 4096.0)
     fill(R("SEGK", 0, 128, 16), 1048575.5)
-    ts(R("RA", 0, 256), R("I256", 0, 256), 0.5, O.is_gt)
+    tt(R("THR", 0, 256), R("pW", 256, 512), R("DM", 0, 256), O.mult)
     cp(R("SX0", 0, LE), R("SI", 1680, 1856))
-    ts(R("KEY8", 0, 8), R("BONES", 0, 128, 16), 16.0, O.mult)
-    scan(R("WX", 0, 256), R("RA", 0, 256), R("THR", 0, 256), 0.0, O.mult, O.max)
-    fill(R("ROWS", 0, 128), -2048.0)
-    for u in range(4):
-        fill(R("ROWS", 128 * u + 128, 128 * u + 256), float(B + M * u - 4096))
-    ts(R("SV0", 0, LE), R("SI", 1680, 1856), -HALF, O.add)
-    ts(R("IDL", 0, B // 16), R("T16", 0, B // 16), R("PF", 0, 1), O.add)
-    ts(R("TR", 0, 16), R("T16", 0, 16), R("PF", 0, 1), O.add, float(TOP), O.add)
+    for i, value in enumerate([-2048] + [B + M * u - 4096 for u in range(4)]):
+        act(R("ROWS", 128 * i, 128 * i + 128), R("ONEF", 0, 128), AF.Copy, float(value))
+    act(R("RB", 0, 256), R("I256", 0, 256), AF.Sign)
+    act(R("SEGY", 0, 256), R("ONEB", 0, 256), AF.Copy, big)
     act(R("ID4", 0, 128), R("IDN", 0, 128), AF.Copy, 4096.0)
     act(R("NE4", 0, 128), R("IDN", 0, 128), AF.Copy, -4096.0)
     act(R("IDB", 0, 128), R("IDN", 0, 128), AF.Copy)
@@ -255,20 +251,22 @@ def rank_program(g, core, T, topo):
     act(R("NEG", 0, 128), R("IDN", 0, 128), AF.Copy, -1.0)
     act(R("MASKC", 0, 256), R("DM", 0, 256), AF.Copy, 30720.0)
     act(R("B4", 0, 128), R("BONES", 0, 128), AF.Copy, 4096.0)
-    act(R("BB1", 0, 128), R("BONES", 0, 128), AF.Copy)
-    act(R("BONB", 0, 128), R("BONES", 0, 128), AF.Copy, 0.5)
+    act(R("TS", 0, 256), R("ONEB", 0, 256), AF.Copy, 0.0)
+    scan(R("WX", 0, 256), R("RB", 0, 256), R("THR", 0, 256), 0.0, O.mult, O.max)
+    fill(R("SEGY", 0, 256, 16), -2047.5)
+    ts(R("KEY8", 0, 8), R("BONES", 0, 128, 16), 16.0, O.mult)
+    ts(R("IDL", 0, B // 16), R("T16", 0, B // 16), R("PF", 0, 1), O.add)
     keep(R("L1N", 0, 128), R("BONES", 0, 128), [[1, 128]], O.is_gt, 0.0, 0, -1)
     keep(R("L2N", 0, 128), R("BONES", 0, 128), [[-1, 128]], O.is_ge, 0.0, 0, 1)
     keep(R("LA", 0, 128), R("B4", 0, 128), [[1, 128]], O.is_gt, 0.0, 0, -1)
     keep(R("LB", 0, 128), R("B4", 0, 128), [[-1, 128]], O.is_ge, 0.0, 0, 1)
     keep(R("L1A", 0, 128), R("LA", 0, 128), [[-1, 128]], O.not_equal, -255.0 * 4096, 0, 1)
     keep(R("L2A", 0, 128), R("LB", 0, 128), [[-1, 128]], O.not_equal, 256.0 * 4096, 0, 1)
-    iota(R("SI", B, TOP), [[0, M]], 0, 0, False)
-    iota(R("C", B, TOP), [[0, M]], 0, 0, True)
     for i in range(16):
         keep(R("RSEL", 128 * i, 128 * i + 128), R("ONEF", 0, 128), [[-16, 8], [0, 16]], O.is_equal, 0.0, -i, 1)
-    for name in ("CN1", "SN1", "CN2", "CN3"):
-        iota(R(name, 0, M), [[0, M]], 0, 0, True)
+    for name, lo, hi in (("M0", LE, LE + 16), ("SY0", LE, LE + 16), ("SY1", LE, LE + 16), ("CN1", 0, M), ("CN2", 0, M),
+                         ("SN2", 0, 2 * M), ("CN3", 0, M)):
+        iota(R(name, lo, hi), [[0, hi - lo]], 0, 0, True)
     cp(R("C", 1680, 1856), R("CI", 1680, 1856))
 
     NEWC = (R("C", B, B + SPARE), R("CN1", 0, SPARE), R("CN2", 0, SPARE), R("CN3", 0, SPARE))
@@ -283,19 +281,38 @@ def rank_program(g, core, T, topo):
         hi = min(hi, LANES[u] // 16)
         cp(IND(NEWS[u], R("LN%d" % u, lo, hi)), R("SY%d" % u, 16 * lo, 16 * hi))
 
+    def sources(u):
+        for t in range(M // 16):
+            m["signs"](R("SUMS", t, t + 1), R("EQ", 256 * t, 256 * t + LE), R("pO", 0, LE), R("JB", t, t + 1))
+        act(R("FROM%d" % u, 0, M // 16), R("SUMS", 0, M // 16), AF.Identity, 0.5, LE / 2.0)
+
+    def fetch(to, src, u):
+        act(to, IND(R(src, 0, LE + 16), R("FROM%d" % u, 0, M // 16)), AF.Copy)
+
     def number(u):
         nt = LANES[u] // 16
-        tt(R("Q", 0, nt), R("pK1", 272, 272 + nt), R("KILL", 0, nt), O.add)
+        tt(R("Q", 0, nt), R("pX", 0, nt), R("KILL", 0, nt), O.add)
+
+    def turn(to, u, b, stop):
+        nl, l0 = CHUNKS[u][b], b * CHUNKS[u][0]
+        mm(R(to, l0, l0 + nl), R("OH%d" % b, 0, 128, 1, nl), R("ID4", 0, nl, 1, nl), False, stop)
+
+    def row(to, i, lo, hi):
+        mm(R(to, lo, hi), R("ROWS", 128 * i, 128 * i + 128, 1, 1), R("ONEB", lo, hi, 1, 1), True, False)
 
     def spread_numbers(u):
+        row("pN", u + 1, 0, LANES[u])
+        turn("pN", u, 0, False)
+        turn("pN", u, 1, False)
         for i in range(16):
             mm(R("pN", i, LANES[u], 16), R("RSEL", 128 * i, 128 * i + 128), R("Q", 0, LANES[u] // 16), False, i == 15)
 
     def change_links(u):
         tt(OLDS[u], OLDS[u], R("pN", 0, LANES[u]), O.max)
 
-    def convert(to, at, src, lo, hi):
-        act(R(to, at, at + hi - lo), IND(R(src, lo, hi), R("IDL", 0, (hi - lo) // 16)), AF.Copy)
+    def convert(to, at, src, lo, hi, plus=0.0):
+        act(R(to, at, at + hi - lo), IND(R(src, lo, hi), R("IDL", 0, (hi - lo) // 16)), AF.Identity if plus else AF.Copy,
+            1.0, plus)
 
     def send():
         rid, pid = topo.addr(nxt)[:2]
@@ -311,16 +328,15 @@ def rank_program(g, core, T, topo):
         store("S", "ys", lo - 1680, R("SO", lo - 1680, hi - 1680))
 
     LATER = {
-        0: {"K": [lambda: cp(R("SX2", 0, 256), R("SI", 1856, B))],
-            "O": [lambda: ts(R("SV2", 0, 256), R("SI", 1856, B), -HALF, O.add)]},
-        1: {"K": [lambda: change_links(0), lambda: old_links_out(1680, 1856)], "O": [lambda: new_counts(0, 0, 4)],
-            "P": [lambda: new_counts(0, 4, 8)], "E": [lambda: new_counts(0, 8, 11)]},
-        2: {"K": [lambda: change_links(1)],
-            "O": [lambda: new_links(0, 0, 4)], "P": [lambda: new_links(0, 4, 8)], "Y": [lambda: new_links(1, 0, 2)],
-            "E": [lambda: new_links(0, 8, 11), lambda: old_links_out(B, TOP), lambda: new_links(1, 2, 4)],
-            "L": [lambda: new_links(1, 4, 6)],
-            "S": [lambda: new_links(1, 6, 11), lambda: store("S", "ys", TOP - 1680, R("SN1", 0, M))]},
-        3: {"K": [lambda: change_links(2), lambda: old_links_out(1856, B)]},
+        0: {"K": [lambda: ts(R("SV0", 0, LE), R("SI", 1680, 1856), -HALF, O.add),
+                  lambda: ts(R("TR", 0, 16), R("T16", 0, 16), R("PF", 0, 1), O.add, float(TOP), O.add)],
+            "O": [lambda: ts(R("JB", 0, 16), R("T16", 0, 16), R("PF", 0, 1), O.add, 0.5, O.add)],
+            "S": [lambda: cp(R("TS", 0, 256, 16), R("TR", 0, 16))]},
+        1: {"K": [lambda: change_links(0), lambda: fetch(R("C", B, TOP), "M0", 0), lambda: old_links_out(1680, 1856)]},
+        2: {"K": [lambda: change_links(1), lambda: fetch(R("SI", B, TOP), "SY0", 0),
+                  lambda: fetch(R("SO", B - 1680, TOP - 1680), "SY0", 0),
+                  lambda: store("S", "ys", B - 1680, R("SO", B - 1680, TOP - 1680))]},
+        3: {"K": [lambda: change_links(2), lambda: old_links_out(1856, B)], "O": [lambda: fill(R("SN2", M, 256), 0.0)]},
     }
 
     for u in range(4):
@@ -344,15 +360,12 @@ def rank_program(g, core, T, topo):
             elif lo < hi:
                 cp(R("G", 16 * lo, 16 * hi), IND(win, R(SX, lo, hi)))
 
-        def minus_own():
-            if u == 1:
-                mm(R(pD, 0, L), R("NEG", 0, 128), R("CY0", 0, L), True, False)
-                mm(R(pD, 0, L), R("IDN", 0, 128), R("RE0", 0, L), False, False)
+        def minus_own(half):
+            if half == (u == 1):
+                c = (R("C", 1680, 1856), R("M0", 0, LE), R("C", 1856, 1856 + LE), R("CN2", 0, M))[u]
+                mm(R(pD, 0, c[2] - c[1]), R("NEG", 0, 128), c, True, False)
             elif u == 2:
-                mm(R(pD, 0, LE), R("NEG", 0, 128), R("C", 1856, 1856 + LE), True, False)
                 mm(R(pD, LE, L), R("NEG", 0, 128), R("land", 0, LP), False, False)
-            else:
-                mm(R(pD, 0, L), R("NEG", 0, 128), R("CN2", 0, L) if u else R("C", 1680, 1856), True, False)
 
         gather("A", 0, n0 - h0)
         gather("A", n0, L - h2 - h1)
@@ -382,10 +395,17 @@ def rank_program(g, core, T, topo):
         gather("V", n0 - h0, n0)
         gather("V", L - h2, L)
         if u == 0:
+            act(R("BB1", 0, 128), R("BONES", 0, 128), AF.Copy)
+            act(R("BONB", 0, 128), R("BONES", 0, 128), AF.Copy, 0.5)
             convert("C", 0, "CI", 0, 1680)
             convert("C", 1856, "CI", 1856, B)
+        if u == 1:
+            sources(0)
         if u == 2:
             store("S", "yc", TOP, R("CN1", 0, M))
+            sources(1)
+            fetch(R("SN1", 0, M), "SY1", 1)
+            store("S", "ys", TOP - 1680, R("SN1", 0, M))
         if u == 3:
             store("S", "yc", TOP + M, R("CN2", 0, M))
 
@@ -407,50 +427,53 @@ def rank_program(g, core, T, topo):
             else:
                 tt(H, R(K, 0, 128, 1, nl), X, O.is_equal)
 
-        def turn(to, b, stop):
-            nl, l0 = CHUNKS[u][b], b * n0
-            mm(R(to, l0, l0 + nl), R("OH%d" % b, 0, 128, 1, nl), R("ID4", 0, nl, 1, nl), False, stop)
-
-        def row(to, i):
-            mm(R(to, 0, L), R("ROWS", 128 * i, 128 * i + 128, 1, 1), R("ONEB", 0, L, 1, 1), True, False)
-
         for k in range(16 // rep):
             keys(0, k)
             if k == MID[u]:
                 gather("V", L - h2 - h1, L - h2)
 
         for k in range(16):
-            for part in range(3):
-                if BEST[u][part] == k:
-                    best(0, part)
             keys(1, k)
-        row("pO", 0)
-        mm(R("pX", 0, L), R("IDB", 0, 128), R("MASKC", 0, L), True, False)
-        minus_own()
+
+        part = ((0, n0), (n0, L))
+        pO, pX, pY = ("pW", "pO"), ("pC0" if u == 1 else "pC1", "pX"), ("pW", "pK0")
+
+        def pick(b):
+            lo, hi = part[b]
+            tt(R("PR", lo, hi), R(pO[b], lo, hi), R(SV, lo, hi), O.min)
+            mm(R(pX[b], lo, hi), R("BB1", 0, 128), R("PR", lo, hi), False, True)
+            mm(R(pY[b], 256 + lo, 256 + hi), R("BB1", 0, 128), R("PR", lo, hi), True, True)
+            act(R("YR", lo, hi), R(pY[b], 256 + lo, 256 + hi), AF.Identity, 1.0, 30720.0)
+
+        def listed(b):
+            lo, hi = part[b]
+            scan(R("YX", lo, hi), R("SEGY", lo, hi), R(pX[b], lo, hi), big, O.min, O.max)
+
+        if u == 1:
+            act(R("M0", 0, L), R("pC0", 0, L), AF.Copy)
+        minus_own(0)
+        for b, (lo, hi) in enumerate(part):
+            row(pO[b], 0, lo, hi)
+        for b in (1, 0):
+            mm(R(pX[b], *part[b]), R("IDB", 0, 128), R("MASKC", *part[b]), True, False)
+        minus_own(1)
         for i, place in enumerate("KFR"):
-            for part in range(3):
-                if BEST[u][part] == 16 + i:
-                    best(0, part)
+            best(0, i)
             later(place)
             if i == 2:
-                turn("pO", 0, False)
+                turn(pO[0], u, 0, True)
             best(1, i)
-        turn("pO", 1, True)
-        row("pN", u + 1)
-        turn("pN", 0, False)
-        turn("pN", 1, False)
-        if u % 2:
-            mm(R("pK1", 256, 272), R("IDN", 0, 128), R("TR", 0, 16), True, False)
-        else:
-            mm(R("pK1", 256, 272), R("ONEB", 0, 128, 1, 1), R("CU", 0, 16, 1, 1), True, False)
+        turn(pO[1], u, 1, True)
         later("O")
-        tt(R("PR", 0, L), R("pO", 0, L), R(SV, 0, L), O.min)
-        mm(R("pX", 0, L), R("BB1", 0, 128), R("PR", 0, L), False, True)
-        mm(R("pK0", 256, 256 + L), R("BB1", 0, 128), R("PR", 0, L), True, True)
+        pick(0)
+        pick(1)
+        if u % 2 == 0:
+            mm(R("pK1", 256, 272), R("ONEB", 0, 128, 1, 1), R("CU", 0, 16, 1, 1), True, False)
         later("P")
-        act(R("YR", 0, L), R("pK0", 256, 256 + L), AF.Identity, 1.0, 30720.0)
-        act(R("DEAD", 0, L), R("pK0", 256, 256 + L), AF.Relu, -big, -32767.0 * big)
-        scan(R("YX", 0, L), R("SEGY", 0, L), R("pX", 0, L), big, O.min, O.max)
+        listed(0)
+        listed(1)
+        for b, (lo, hi) in enumerate(part):
+            act(R("DEAD", lo, hi), R(pY[b], 256 + lo, 256 + hi), AF.Relu, -big, -32767.0 * big)
         later("Y")
         act(R("YG", 0, nt), R("YX", 15, L, 16), AF.Relu, 1.0, HALF)
         act(R("YF", 0, nt), R("YX", 15, L, 16), AF.Relu, 1.0, HALF)
@@ -459,44 +482,88 @@ def rank_program(g, core, T, topo):
         if u == 0:
             act(R("SX1", 0, L), R(SY, 0, L), AF.Copy)
             act(R("SV1", 0, L), R(SY, 0, L), AF.Identity, 1.0, -HALF)
+        if u == 1:
+            convert("SX2", 0, "SI", 1856, B)
 
-        for t in range(nt):
-            o = 256 * t
-            ts(R("EQ", o + 16 * t, o + L), R("YR", 16 * t, L), R("YX", 16 * t + 15, 16 * t + 16), O.is_equal,
+        early = min(n0 // 16, EARLY)
+        apart = early == n0 // 16
+        pW, pW1 = "pO", "pW" if apart else "pO"
+
+        def same(t, lo, hi, to, start, stop):
+            ts(R("EQ", 256 * t + lo, 256 * t + hi), R("YR", lo, hi), R("YX", 16 * t + 15, 16 * t + 16), O.is_equal,
                R("WX", 16 * t + 15, 16 * t + 16), O.mult)
-            mm(R("pW", 16 * t, L), R("BONB", 0, 128), R("EQ", o + 16 * t, o + L), t == 0, t == nt - 1)
-            if t == nt - 4:
-                mm(R("pW", 0, L), R("IDH", 0, 128), R("DEAD", 0, L), False, False)
+            mm(R(to, lo, hi), R("BONB", 0, 128), R("EQ", 256 * t + lo, 256 * t + hi), start, stop)
+
+        def dead(to, lo, hi, stop):
+            mm(R(to, lo, hi), R("IDH", 0, 128), R("DEAD", lo, hi), False, stop)
+
+        def first(to, lo, hi):
+            tt(R("FM", lo, hi), R(to, lo, hi), R("THR", lo, hi), O.is_ge)
+
+        def counted(lo, hi):
+            scan(R("RS", 16 + lo, 16 + hi), R("ONEB", lo, hi), R("FM", lo, hi), R("RS", 15 + lo, 16 + lo), O.add, O.subtract)
+            if u % 2:
+                scan(R("ZX", lo, hi), R("TS", lo, hi), R("FM", lo, hi), 0.0, O.max, O.mult)
+
+        for t in range(early):
+            same(t, 16 * t, n0, pW, t == 0, False)
+        dead(pW, 0, n0, apart)
+        for t in range(nt):
+            same(t, max(16 * t, n0 if t < early else 0), L, pW1, apart and t == 0, t == nt - 1)
+            if t == 1:
+                dead(pW1, n0, L, False)
+        mm(R("pX", 0, 16), R("ONEB", 0, 128, 1, 1), R("CU", 16, 32, 1, 1), True, False)
         mm(R(pD, 0, L), R("IDN", 0, 128), R(CY, 0, L), False, True)
         act(R(RE, 0, L), R(pD, 0, L), AF.Relu)
+        if u == 1:
+            convert("SV2", 0, "SI", 1856, B, -HALF)
+        if apart:
+            first(pW, 0, n0)
         later("E")
-        tt(R("FM", 0, L), R("pW", 0, L), R("THR", 0, L), O.is_lt)
+        if apart:
+            counted(0, n0)
+        first(pW1, n0 if apart else 0, L)
         later("L")
-        scan(R("RS", 16, 16 + L), R("ONEB", 0, L), R("FM", 0, L), 0.0, O.mult, O.add)
-        for at, l1, l2 in ((256, "NE4", "ID4") if u % 2 else (256, "L1A", "L2A"), (272, "L1N", "L2N")):
-            mm(R("pK1", at, at + nt), R(l1, 0, 128), R("RS", 31, 16 + L, 16), False, False)
-            mm(R("pK1", at, at + nt), R(l2, 0, 128), R("RS", 15, L, 16), False, at == 272)
+        counted(n0 if apart else 0, L)
+        Z, U = R("pK1", 256, 256 + nt), R("pX", 0, nt)
+        upto, before = R("RS", 31, 16 + L, 16), R("RS", 15, L, 16)
+
+        def ends():
+            mm(Z, R("L1A", 0, 128), upto, False, False)
+            mm(Z, R("L2A", 0, 128), before, False, True)
+
+        def numbers():
+            for l1, l2 in (("L1N", "L2N"), ("NE4", "ID4")):
+                mm(U, R(l1, 0, 128), upto, False, False)
+                mm(U, R(l2, 0, 128), before, False, l2 == "ID4")
+        for call in ((ends, numbers), (numbers,), (numbers, ends), (numbers,))[u]:
+            call()
+        if u < 2:
+            mm(R("pO", 0, L), R("BONB", 0, 128), R("RS", 16, 16 + L), True, True)
         later("S")
 
-        Z, count = R("pK1", 256, 256 + nt), R("pK1", 272, 272 + nt)
+        def new_places():
+            tt(R(LN, 0, nt), U, R("TR", 0, nt), O.min)
+        if u == 2:
+            new_places()
         if u % 2:
-            cp(R("Z", 0, nt), Z)
+            Z = R("ZX", 15, L, 16)
             tt(R("LY", 0, nt), Z, R("YF", 0, nt), O.max)
         else:
             tt(R("Z", 0, nt), Z, R("TR", 0, nt), O.min)
         ts(R("KILL", 0, nt), Z, 0.5, O.is_gt, -65536.0, O.mult)
-        if u:
-            tt(R(LN, 0, nt), count, R("Z", 0, nt), O.max)
         if u % 2 == 0:
             tt(R("LY", 0, nt), R("YF", 0, nt), R("Z", 0, nt), O.max)
-            number(u)
-        if u == 0:
-            tt(R(LN, 0, nt), count, R("Z", 0, nt), O.max)
         if u == 2:
-            spread_numbers(u)
             new_links(2)
             act(R("SX3", 0, M), R("SN2", 0, M), AF.Copy)
             act(R("SV3", 0, M), R("SN2", 0, M), AF.Identity, 1.0, -HALF)
+            number(u)
+            spread_numbers(u)
+        if u == 0:
+            number(u)
+        if u % 2:
+            new_places()
         cp(IND(R("C", 0, SPARE), R("LY", 0, nt)), R(RE, 0, L))
 
     store("S", "yc", 0, R("C", 0, TOP))

@@ -1,38 +1,40 @@
 from concourse.mybir import AluOpType, ActivationFunctionType, AxisListType
 
 B, LE, LP, M = 2112, 176, 80, 160
-W = B + 4 * M
 TOP = B + M
 SPARE = TOP + 256
 HALF = 1376.0
+LOW = HALF + 15 * 2048
 LANES = (176, 176, 256, 160)
 WIDE = (B, B, B, TOP)
 CHUNKS = ((48, 128), (48, 128), (128, 128), (32, 128))
-TWICE = (2, 1, 1, 2)
-SHARE = ((24, 32, 16), (24, 32, 16), (56, 8, 16), (16, 16, 24))
-EARLY = 3
-MID = (6, 12, 10, 5)
+WIDTH = ((176, 192), (176, 192), (176, 192), (160, 160))
+PP = 96
+ORDER = ("FFFFFmmmmFmmmmmm", "FFFFFmmmmFmmmmmm", "FFmmmmFFmmmFmmmm" + 4 * "f" + 12 * "p", "FFFFFmmmmFmmmmmm")
+CALLS = ((4, 3, 2, 1), (4, 3, 2, 1), (4, 3, 2, 2), (4, 3, 2, 1))
+PORT_CALLS = (6, 4, 2)
+AHEAD = (4, 4, 0, 4)
 
 SCRATCH = {}
 PSUM = ("pK0", "pK1", "pC0", "pC1", "pO", "pX", "pW", "pN")
 for _names, _w, _t in (
-        ("CI", B, "int32"), ("SI", TOP, "int32"), ("PI PA", 1, "int32"),
+        ("CI", B, "int32"), ("SI", TOP, "int32"), ("PI PA PB", 1, "int32"), ("CE", 192, "int32"), ("OW0 OW2", 192, "float32"),
         ("C CN1 CN2 CN3", SPARE, "float32"), ("SN1", M, "float32"), ("SN2", M + SPARE, "float32"), ("SO", TOP - 1680, "float32"),
-        ("G MN", 4096, "float32"), ("EQ", 4096, "bfloat16"), ("land", LP, "float32"),
-        ("DEAD ONEB FM MASKC", 256, "bfloat16"), ("RS", 272, "bfloat16"),
-        ("CY0 CY1 CY2 CY3 SY0 SY1 SY2 SY3 RE0 RE1 RE2 RE3 YX THR DM I256 SEGY RA RB WX TS ZX M0", 256, "float32"),
-        ("PR YR SV0 SV1 SV2 SV3", 256, "float16"), ("SX0 SX1 SX2 SX3", 256, "uint16"),
-        ("OH0 OH1 IDB ID4 NE4 IDH BONB BIAS L1A L2A L1N L2N", 128, "bfloat16"), ("BB1", 128, "float16"),
-        ("ROWS", 640, "bfloat16"), ("CU", 32, "bfloat16"), ("RSEL", 2048, "bfloat16"),
-        ("XB0 XB1 SEGK ONEF BH BONES B4 LA LB IDN NEG", 128, "float32"),
-        ("YF Z TR JB SUMS", 16, "float32"), ("KILL Q", 16, "bfloat16"),
-        ("YG LY LN1 LN2 LN3 FROM0 FROM1", 16, "uint16"), ("T16", B // 16, "float32"), ("IDL", B // 16, "uint16"),
-        ("KEY8", 8, "float32"), ("PF W0 W1 ZERO", 1, "float32")):
+        ("G", 16 * (192 + PP), "float32"), ("MN", 16 * (192 + 128), "float32"), ("EQ", 4096, "bfloat16"), ("land", LP, "float32"),
+        ("DEAD ONEB FM MASKC I256 CAP CNT", 256, "bfloat16"), ("JUNK", 10 * LE, "bfloat16"), ("RS", 272, "bfloat16"),
+        ("CY0 CY1 CY2 CY3 SY0 SY1 SY2 SY3 M0 M1 M2 M3 YX SEGK SEGY TS ZX", 256, "float32"),
+        ("PR YR OFFD SV0 SV1 SV2 SV3 XT0 XT1 XT2 XT3", 256, "float16"), ("LT0 LT1 LT2 LT3", 192 + PP, "uint16"), ("SW", 512, "float16"),
+        ("OH0 OH1 NO0 NO1 IDB ID4 NE4 BON1 NB8 NBK BIAS L1A L2A L1N L2N", 128, "bfloat16"), ("BB1 IDF", 128, "float16"),
+        ("ROWS", 768, "bfloat16"), ("CU", 32, "bfloat16"), ("IDW", 160, "float32"),
+        ("XB0 XB1 BH BONES B4 LA LB", 128, "float32"), ("ONEF", 160, "float32"),
+        ("YF Z TR JB SUMS FULL T16", 16, "float32"),
+        ("YG LY LN1 LN2 LN3 FROM0 FROM1", 16, "uint16"),
+        ("KEY8", 8, "float32"), ("PF H0 H1", 1, "float32")):
     for _n in _names.split():
         SCRATCH[_n] = ("sbuf", [128, _w], _t)
 for _n in PSUM:
     SCRATCH[_n] = ("psum", [128, 512], "float32")
-NDMA = 16
+NDMA = 18
 SEMAPHORES = ["qV", "qA", "qP", "qG", "snt", "arr"] + ["d%d" % _i for _i in range(NDMA)]
 
 
@@ -90,7 +92,7 @@ def machine(g, T):
                     elif not over or (kind == "r" and k2 == "r"):
                         hit = False
                     elif same:
-                        hit = q != "P"
+                        hit = q != "P" and k2 == "w"
                     else:
                         hit = True
                     if hit:
@@ -147,6 +149,7 @@ def machine(g, T):
     m = {"ap": ap, "dma": dma}
     m["cp"] = lambda out, a: op("V", lambda e: e.tensor_copy(ap(out), ap(a)), out, [a])
     m["tt"] = lambda out, a, b, o: op("V", lambda e: e.tensor_tensor(ap(out), ap(a), ap(b), o), out, [a, b])
+    m["blocks"] = lambda out, a: op("V", lambda e: e.transpose(ap(out), ap(a)), out, [a])
 
     def ts(out, a, s1, o0, s2=None, o1=None):
         if o1 is None:
@@ -155,8 +158,6 @@ def machine(g, T):
             op("V", lambda e: e.tensor_scalar(ap(out), ap(a), ap(s1), ap(s2), o0, o1), out, [a, s1, s2])
     m["ts"] = ts
     m["fill"] = lambda out, c: op("V", lambda e: e.memset(ap(out), c), out, [])
-    m["top"] = lambda out, a: op(
-        "V", lambda e: e.tensor_reduce(ap(out), ap(a), AxisListType.X, AluOpType.max), out, [a])
     m["scan"] = lambda out, a, b, i, o0, o1: op(
         "V", lambda e: e.tensor_tensor_scan(ap(out), ap(a), ap(b), ap(i), o0, o1), out, [a, b, i])
     m["iota"] = lambda out, pat, base, cm, small: op(
@@ -169,7 +170,7 @@ def machine(g, T):
     m["act"] = lambda out, a, func, scale=1.0, bias=0.0: op(
         "A", lambda e: e.activation(ap(out), ap(a), func, bias=bias, scale=ap(scale)), out, [a, scale])
     m["signs"] = lambda total, out, a, bias: op(
-        "A", lambda e: e.activation(ap(out), ap(a), ActivationFunctionType.Sign, bias=ap(bias), scale=-2.0,
+        "A", lambda e: e.activation(ap(out), ap(a), ActivationFunctionType.Sign, bias=ap(bias), scale=-1.0,
                                     accum_out=ap(total)), out, [a, bias], [total])
 
     def remote(call, reads, local, n):
@@ -201,118 +202,144 @@ def rank_program(g, core, T, topo):
         return
     O, AF = AluOpType, ActivationFunctionType
     m = machine(g, T)
-    cp, tt, ts, fill, scan, mm, act, dma, iota, keep, top = (
-        m["cp"], m["tt"], m["ts"], m["fill"], m["scan"], m["mm"], m["act"], m["dma"], m["iota"], m["keep"], m["top"])
+    cp, tt, ts, fill, scan, mm, act, dma, iota, keep, blocks = (
+        m["cp"], m["tt"], m["ts"], m["fill"], m["scan"], m["mm"], m["act"], m["dma"], m["iota"], m["keep"], m["blocks"])
     n = len(T.cores)
     nxt, prv = T.cores[(rank + 1) % n], T.cores[(rank - 1) % n]
     sent = len(topo.engines(core, nxt))
     m["landed"]("land", 0, LP, "arr", len(topo.engines(prv, core)))
+    IDN = R("IDW", 16, 144)
 
     def load(q, to, src, lo, hi, after=()):
         dma(q, T[to][:, lo:hi], T[src][:, lo:hi], list(after), [R(to, lo, hi)])
-    load("A", "SI", "s0", 1680, 1856)
+    load("A", "SI", "s0", 1680, 1872)
+    dma("S", T.CE[:, 0:192], T.c0[:, 1680:1872], [], [R("CE", 0, 192)])
     load("S", "CI", "c0", 0, B)
-    load("S", "SI", "s0", 1856, B, [R("CI", 0, B)])
+    load("S", "SI", "s0", 1872, B, [R("CI", 0, B)])
     load("S", "SI", "s0", 0, 1680)
 
+    def turned(u):
+        wide = max(WIDTH[u][1], LANES[u])
+        blocks(R("XT%d" % u, 0, wide), R("SV%d" % u, 0, wide))
+
+    def by_successor(u, lo=0, hi=None, ports=False):
+        bank, nb, t0 = ("pN", PP // 16, LE // 16) if ports else ("pK0", WIDTH[u][1] // 16, 0)
+        for i in range(nb)[lo:hi]:
+            t = min(t0 + i, 15)
+            for h in range(2):
+                a, s = 32 * (t // 2) + 16 * h, 256 * (t % 2) + 128 * h
+                mm(R(bank, i, 16 * nb, nb), R("SW", s, s + 128), R("XT%d" % u, a, a + 16), i == 0 and h == 0,
+                   h == 1 and i == nb - 1)
+
+    def listed_successors(u, ports=False):
+        bank, at, wide = ("pN", WIDTH[u][1], PP) if ports else ("pK0", 0, WIDTH[u][1])
+        act(R("LT%d" % u, at, at + wide), R(bank, 0, wide), AF.Identity, 1.0, HALF)
+
     big = float(2 ** 60)
-    fill(R("ONEF", 0, 128), 1.0)
+    fill(R("ONEF", 0, 160), 1.0)
     iota(R("PI", 0, 1), [[0, 1]], 0, 1, False)
-    iota(R("I256", 0, 256), [[0, 16], [1, 16]], 0, 0, True)
-    keep(R("IDN", 0, 128), R("ONEF", 0, 128), [[-1, 128]], O.is_equal, 0.0, 0, 1)
+    keep(R("IDW", 0, 160), R("ONEF", 0, 160), [[-1, 160]], O.is_equal, 0.0, 16, 1)
     keep(R("BH", 0, 128), R("ONEF", 0, 128), [[-16, 8], [0, 16]], O.is_ge, 0.0, 0, 1)
     keep(R("BONES", 0, 128), R("BH", 0, 128), [[16, 8], [0, 16]], O.is_ge, 0.0, 15, -1)
     iota(R("BIAS", 0, 128), [[0, 8], [-1, 16]], 15, 0, True)
-    iota(R("T16", 0, B // 16), [[16, B // 16]], 0, 0, True)
-    fill(R("RA", 0, 256), 0.5)
-    fill(R("W0", 0, 1), 2.0 * big)
+    iota(R("T16", 0, 16), [[16, 16]], 0, 0, True)
+    iota(R("I256", 0, 256), [[0, 16], [1, 16]], 0, 0, True)
+    fill(R("SEGK", 0, 256), big)
+    ts(R("PB", 0, 1), R("PI", 0, 1), 4, O.arith_shift_right, 1, O.bitwise_and)
+    fill(R("SEGY", 0, 256), -big)
+    cp(R("H1", 0, 1), R("PB", 0, 1))
     fill(R("ONEB", 0, 256), 1.0)
+    ts(R("H0", 0, 1), R("H1", 0, 1), -1.0, O.mult, 1.0, O.add)
+    for tth, (lo, half) in enumerate(((16, "H0"), (0, "H0"), (32, "H1"), (16, "H1"))):
+        act(R("SW", 128 * tth, 128 * tth + 128), R("IDW", lo, lo + 128), AF.Copy, R(half, 0, 1))
     ts(R("PA", 0, 1), R("PI", 0, 1), 15, O.bitwise_and)
-    fill(R("RA", 0, 256, 16), 1.0)
-    ts(R("W1", 0, 1), R("W0", 0, 1), big, O.mult)
-    fill(R("SEGK", 0, 128), big)
+    fill(R("SEGK", 0, 128, 16), 2 ** 20 - 0.5)
+    fill(R("SEGK", 128, 256, 16), 2 ** 20 - 0.25)
     cp(R("PF", 0, 1), R("PA", 0, 1))
-    scan(R("pW", 256, 512), R("RA", 0, 256), R("ONEB", 0, 256), R("W1", 0, 1), O.mult, O.mult)
-    ts(R("DM", 0, 256), R("I256", 0, 256), R("PF", 0, 1), O.is_equal)
+    ts(R("SV0", 0, 192), R("SI", 1680, 1872), -HALF, O.add)
+    fill(R("SEGY", 0, 256, 16), B - 0.75 - HALF)
+    turned(0)
+    by_successor(0, 0, 12)
+    fill(R("TS", 0, 256), 0.0)
     fill(R("RS", 0, 16), 0.0)
     fill(R("CU", 0, 16), 4096.0 * (255 - M + 1))
     fill(R("CU", 16, 32), 4096.0)
-    fill(R("SEGK", 0, 128, 16), 1048575.5)
-    tt(R("THR", 0, 256), R("pW", 256, 512), R("DM", 0, 256), O.mult)
-    cp(R("SX0", 0, LE), R("SI", 1680, 1856))
-    for i, value in enumerate([-2048] + [B + M * u - 4096 for u in range(4)]):
-        act(R("ROWS", 128 * i, 128 * i + 128), R("ONEF", 0, 128), AF.Copy, float(value))
-    act(R("RB", 0, 256), R("I256", 0, 256), AF.Sign)
-    act(R("SEGY", 0, 256), R("ONEB", 0, 256), AF.Copy, big)
-    act(R("ID4", 0, 128), R("IDN", 0, 128), AF.Copy, 4096.0)
-    act(R("NE4", 0, 128), R("IDN", 0, 128), AF.Copy, -4096.0)
-    act(R("IDB", 0, 128), R("IDN", 0, 128), AF.Copy)
-    act(R("IDH", 0, 128), R("IDN", 0, 128), AF.Copy, 2.0 * big)
-    act(R("NEG", 0, 128), R("IDN", 0, 128), AF.Copy, -1.0)
-    act(R("MASKC", 0, 256), R("DM", 0, 256), AF.Copy, 30720.0)
+    fill(R("ROWS", 0, 128), 2048.0)
+    fill(R("ROWS", 640, 768), 15.0 * 2 ** 25)
+    cp(R("SV1", LE, LE + 16), R("ONEB", 0, 16))
+    act(R("OW0", 0, 192), R("CE", 0, 192), AF.Copy)
+    act(R("NE4", 0, 128), IDN, AF.Copy, -4096.0)
+    act(R("IDB", 0, 128), IDN, AF.Copy)
+    listed_successors(0)
     act(R("B4", 0, 128), R("BONES", 0, 128), AF.Copy, 4096.0)
-    act(R("TS", 0, 256), R("ONEB", 0, 256), AF.Copy, 0.0)
-    scan(R("WX", 0, 256), R("RB", 0, 256), R("THR", 0, 256), 0.0, O.mult, O.max)
-    fill(R("SEGY", 0, 256, 16), -2047.5)
+    act(R("BB1", 0, 128), R("BONES", 0, 128), AF.Copy)
+    act(R("BON1", 0, 128), R("BONES", 0, 128), AF.Copy)
     ts(R("KEY8", 0, 8), R("BONES", 0, 128, 16), 16.0, O.mult)
-    ts(R("IDL", 0, B // 16), R("T16", 0, B // 16), R("PF", 0, 1), O.add)
+    ts(R("TR", 0, 16), R("T16", 0, 16), R("PF", 0, 1), O.add, float(TOP), O.add)
+    ts(R("JB", 0, 16), R("T16", 0, 16), R("PF", 0, 1), O.add, 0.5, O.add)
+    cp(R("TS", 0, 256, 16), R("TR", 0, 16))
+    ts(R("MASKC", 0, 256), R("I256", 0, 256), R("PF", 0, 1), O.is_equal, -30720.0, O.mult)
+    ts(R("CAP", 0, 256), R("I256", 0, 256), R("PF", 0, 1), O.not_equal, 4096.0, O.mult)
+    act(R("OFFD", 0, 256), R("CAP", 0, 256), AF.Identity, 1.0, HALF - 30720.0)
+    act(R("IDF", 0, 128), IDN, AF.Copy)
     keep(R("L1N", 0, 128), R("BONES", 0, 128), [[1, 128]], O.is_gt, 0.0, 0, -1)
-    keep(R("L2N", 0, 128), R("BONES", 0, 128), [[-1, 128]], O.is_ge, 0.0, 0, 1)
     keep(R("LA", 0, 128), R("B4", 0, 128), [[1, 128]], O.is_gt, 0.0, 0, -1)
+    keep(R("C", 0, B), R("CI", 0, B), [[0, B]], O.is_gt, 0.0, 1, 0)
     keep(R("LB", 0, 128), R("B4", 0, 128), [[-1, 128]], O.is_ge, 0.0, 0, 1)
     keep(R("L1A", 0, 128), R("LA", 0, 128), [[-1, 128]], O.not_equal, -255.0 * 4096, 0, 1)
     keep(R("L2A", 0, 128), R("LB", 0, 128), [[-1, 128]], O.not_equal, 256.0 * 4096, 0, 1)
-    for i in range(16):
-        keep(R("RSEL", 128 * i, 128 * i + 128), R("ONEF", 0, 128), [[-16, 8], [0, 16]], O.is_equal, 0.0, -i, 1)
-    for name, lo, hi in (("M0", LE, LE + 16), ("SY0", LE, LE + 16), ("SY1", LE, LE + 16), ("CN1", 0, M), ("CN2", 0, M),
-                         ("SN2", 0, 2 * M), ("CN3", 0, M)):
+    for name, lo, hi in (("M0", LE, LE + 16), ("SY0", LE, LE + 16), ("SY1", LE, LE + 16)):
         iota(R(name, lo, hi), [[0, hi - lo]], 0, 0, True)
-    cp(R("C", 1680, 1856), R("CI", 1680, 1856))
+    for u in range(4):
+        iota(R("ROWS", 128 * u + 128, 128 * u + 256, 1, 2), [[0, 128]], B + M * u - 4096, 15 * 8192 - (B + M * u - 4096), True)
+    keep(R("L2N", 0, 128), R("BONES", 0, 128), [[-1, 128]], O.is_ge, 0.0, 0, 1)
+    for name, lo, hi in (("CN1", 0, M), ("MN", 16 * 192, 16 * (192 + 128)), ("CN2", 0, M), ("SN2", 0, 2 * M), ("CN3", 0, M)):
+        iota(R(name, lo, hi), [[0, hi - lo]], 0, 0, True)
 
-    NEWC = (R("C", B, B + SPARE), R("CN1", 0, SPARE), R("CN2", 0, SPARE), R("CN3", 0, SPARE))
-    NEWS = (R("SI", B, B + SPARE), R("SN1", 0, SPARE), R("SN2", 0, SPARE), R("SN2", M, M + SPARE))
+    NEWC = (None, R("CN1", 0, SPARE), R("CN2", 0, SPARE), R("CN3", 0, SPARE))
+    NEWS = (None, None, R("SN2", 0, SPARE), R("SN2", M, M + SPARE))
     OLDS = (R("SI", 1680, 1856), R("SY0", 0, LE), R("SI", 1856, B), R("SN2", 0, M))
+    OWN = (("OW0", 0), ("M0", 0), ("OW2", 0), ("CN2", 0))
 
-    def new_counts(u, lo=0, hi=16):
-        hi = min(hi, LANES[u] // 16)
-        tt(IND(NEWC[u], R("LN%d" % u, lo, hi)), R("CY%d" % u, 16 * lo, 16 * hi), R("RE%d" % u, 16 * lo, 16 * hi), O.subtract)
+    def new_counts(u):
+        cp(IND(NEWC[u], R("LN%d" % u, 0, LANES[u] // 16)), R("M%d" % u, 0, LANES[u]))
 
-    def new_links(u, lo=0, hi=16):
-        hi = min(hi, LANES[u] // 16)
-        cp(IND(NEWS[u], R("LN%d" % u, lo, hi)), R("SY%d" % u, 16 * lo, 16 * hi))
+    def new_links(u):
+        cp(IND(NEWS[u], R("LN%d" % u, 0, LANES[u] // 16)), R("SY%d" % u, 0, LANES[u]))
 
-    def sources(u):
+    def sources():
+        act(R("CNT", 0, LE), R("pO", 0, LE), AF.Copy)
         for t in range(M // 16):
-            m["signs"](R("SUMS", t, t + 1), R("EQ", 256 * t, 256 * t + LE), R("pO", 0, LE), R("JB", t, t + 1))
-        act(R("FROM%d" % u, 0, M // 16), R("SUMS", 0, M // 16), AF.Identity, 0.5, LE / 2.0)
+            m["signs"](R("SUMS", t, t + 1), R("JUNK", LE * t + 16 * t, LE * t + LE), R("CNT", 16 * t, LE), R("JB", t, t + 1))
+
+    def sources_below():
+        tt(R("FULL", 0, M // 16), R("SUMS", 0, M // 16), R("T16", 0, M // 16), O.add)
+
+    def sources_listed(u):
+        act(R("FROM%d" % u, 0, M // 16), R("FULL", 0, M // 16), AF.Identity, 0.5, LE / 2.0)
 
     def fetch(to, src, u):
         act(to, IND(R(src, 0, LE + 16), R("FROM%d" % u, 0, M // 16)), AF.Copy)
 
-    def number(u):
-        nt = LANES[u] // 16
-        tt(R("Q", 0, nt), R("pX", 0, nt), R("KILL", 0, nt), O.add)
-
-    def turn(to, u, b, stop):
+    def turn(to, u, b, stop, by="ID4"):
         nl, l0 = CHUNKS[u][b], b * CHUNKS[u][0]
-        mm(R(to, l0, l0 + nl), R("OH%d" % b, 0, 128, 1, nl), R("ID4", 0, nl, 1, nl), False, stop)
+        mm(R(to, l0, l0 + nl), R("OH%d" % b, 0, 128, 1, nl), R(by, 0, nl, 1, nl), False, stop)
 
-    def row(to, i, lo, hi):
-        mm(R(to, lo, hi), R("ROWS", 128 * i, 128 * i + 128, 1, 1), R("ONEB", lo, hi, 1, 1), True, False)
+    def row(to, i, lo, hi, rows=1):
+        mm(R(to, lo, hi), R("ROWS", 128 * i, 128 * i + 128, 1, rows), R("ONEB", lo, hi, 1, rows), True, False)
 
     def spread_numbers(u):
-        row("pN", u + 1, 0, LANES[u])
+        L, n0 = LANES[u], CHUNKS[u][0]
+        row("pN", u + 1, 0, L, 2)
         turn("pN", u, 0, False)
         turn("pN", u, 1, False)
-        for i in range(16):
-            mm(R("pN", i, LANES[u], 16), R("RSEL", 128 * i, 128 * i + 128), R("Q", 0, LANES[u] // 16), False, i == 15)
+        if u % 2 == 0:
+            mm(R("pN", n0, L), R("NB8", 0, 128), R("CAP", n0, L), False, False)
+        mm(R("pN", 0, L), R("NB8", 0, 128), R("FM", 0, L), False, False)
+        mm(R("pN", 0, L), R("BON1", 0, 128), R("RS", 15, 15 + L), False, True)
 
     def change_links(u):
         tt(OLDS[u], OLDS[u], R("pN", 0, LANES[u]), O.max)
-
-    def convert(to, at, src, lo, hi, plus=0.0):
-        act(R(to, at, at + hi - lo), IND(R(src, lo, hi), R("IDL", 0, (hi - lo) // 16)), AF.Identity if plus else AF.Copy,
-            1.0, plus)
 
     def send():
         rid, pid = topo.addr(nxt)[:2]
@@ -320,211 +347,216 @@ def rank_program(g, core, T, topo):
                                          local_sem=T.sem.snt, pid=pid, routing_id=rid, dma_engine_mask=topo.mask(core, nxt)),
                     [R("CN1", 0, LP)], "snt", sent)
 
-    def store(q, to, at, src):
-        dma(q, T[to][:, at:at + src[2] - src[1]], T[src[0]][:, src[1]:src[2]], [src], [])
+    def store(q, to, at, src, after=None):
+        dma(q, T[to][:, at:at + src[2] - src[1]], T[src[0]][:, src[1]:src[2]], [src, after or src], [])
 
     def old_links_out(lo, hi):
-        convert("SO", lo - 1680, "SI", lo, hi)
+        keep(R("SO", lo - 1680, hi - 1680), R("SI", lo, hi), [[0, hi - lo]], O.is_gt, 0.0, 1, 0)
         store("S", "ys", lo - 1680, R("SO", lo - 1680, hi - 1680))
 
     LATER = {
-        0: {"K": [lambda: ts(R("SV0", 0, LE), R("SI", 1680, 1856), -HALF, O.add),
-                  lambda: ts(R("TR", 0, 16), R("T16", 0, 16), R("PF", 0, 1), O.add, float(TOP), O.add)],
-            "O": [lambda: ts(R("JB", 0, 16), R("T16", 0, 16), R("PF", 0, 1), O.add, 0.5, O.add)],
-            "S": [lambda: cp(R("TS", 0, 256, 16), R("TR", 0, 16))]},
-        1: {"K": [lambda: change_links(0), lambda: fetch(R("C", B, TOP), "M0", 0), lambda: old_links_out(1680, 1856)]},
-        2: {"K": [lambda: change_links(1), lambda: fetch(R("SI", B, TOP), "SY0", 0),
-                  lambda: fetch(R("SO", B - 1680, TOP - 1680), "SY0", 0),
-                  lambda: store("S", "ys", B - 1680, R("SO", B - 1680, TOP - 1680))]},
-        3: {"K": [lambda: change_links(2), lambda: old_links_out(1856, B)], "O": [lambda: fill(R("SN2", M, 256), 0.0)]},
+        0: {"G": [lambda: act(R("SV2", 0, 256), R("SI", 1856, B), AF.Identity, 1.0, -HALF),
+                  lambda: act(R("NBK", 0, 128), R("BONES", 0, 128), AF.Copy, -float(2 ** 25)),
+                  lambda: act(R("NB8", 0, 128), R("BONES", 0, 128), AF.Copy, -8192.0),
+                  lambda: act(R("ID4", 0, 128), IDN, AF.Copy, 4096.0)],
+            "K": [lambda: turned(2), lambda: by_successor(2, ports=True), lambda: listed_successors(2, True)]},
+        1: {"G": [sources],
+            "O": [lambda: change_links(0), lambda: old_links_out(1680, 1856)],
+            "P": [sources_below],
+            "Y": [lambda: sources_listed(0), lambda: fetch(R("C", B, TOP), "M0", 0)],
+            "E": [lambda: by_successor(2), lambda: listed_successors(2)]},
+        2: {"G": [lambda: act(R("SY0", 0, LE), R("SV1", 0, LE), AF.Identity, 1.0, HALF), sources], "O": [lambda: change_links(1)], "P": [sources_below],
+            "E": [lambda: store("S", "yc", TOP, R("CN1", 0, M), R("YG", 0, 16))]},
+        3: {"G": [lambda: fetch(R("SI", B, TOP), "SY0", 0), lambda: old_links_out(B, TOP),
+                  lambda: sources_listed(1), lambda: fetch(R("SN1", 0, M), "SY1", 1),
+                  lambda: store("S", "ys", TOP - 1680, R("SN1", 0, M))],
+            "K": [lambda: fill(R("SN2", M, 256), 0.0), lambda: fill(R("SEGY", 0, M, 16), TOP - 0.75 - HALF)],
+            "O": [lambda: change_links(2), lambda: old_links_out(1856, B)]},
     }
 
     for u in range(4):
         L, wide = LANES[u], WIDE[u]
         nt = L // 16
         n0, n1 = CHUNKS[u]
-        h0, h1, h2 = SHARE[u]
-        rep = TWICE[u]
         win = R("C" if u else "CI", 0, wide)
-        SX, SV, SY, CY, RE, LN = ("%s%d" % (a, u) for a in ("SX", "SV", "SY", "CY", "RE", "LN"))
-        own = (R("pC0", 0, rep * n0), R("pC0", n0, L) if u == 1 else R("pC1", 0, n1))
-        pD = "pC1" if u == 1 else "pC0"
+        LT, SV, SY, CY, MU, LN = ("%s%d" % (a, u) for a in ("LT", "SV", "SY", "CY", "M", "LN"))
+        pC, pD = "pC%d" % (u % 2), "pC%d" % (1 - u % 2)
+        src, x = OWN[u]
 
         def later(place):
             for call in LATER[u].get(place, []):
                 call()
 
-        def gather(q, lo, hi):
-            if lo < hi and q == "A":
-                act(R("G", 16 * lo, 16 * hi), IND(win, R(SX, lo, hi)), AF.Copy)
-            elif lo < hi:
-                cp(R("G", 16 * lo, 16 * hi), IND(win, R(SX, lo, hi)))
+        nl, pad = WIDTH[u]
 
-        def minus_own(half):
-            if half == (u == 1):
-                c = (R("C", 1680, 1856), R("M0", 0, LE), R("C", 1856, 1856 + LE), R("CN2", 0, M))[u]
-                mm(R(pD, 0, c[2] - c[1]), R("NEG", 0, 128), c, True, False)
-            elif u == 2:
-                mm(R(pD, LE, L), R("NEG", 0, 128), R("land", 0, LP), False, False)
+        def span(ports, k, nk):
+            if ports:
+                return 16 * pad + k * PP, 16 * pad + (k + nk - 1) * PP + LP
+            return k * pad, (k + nk - 1) * pad + nl
 
-        gather("A", 0, n0 - h0)
-        gather("A", n0, L - h2 - h1)
+        def listing(ports, k, nk):
+            lo, hi = span(ports, k, nk)
+            return IND(win, R(LT, lo // 16, hi // 16))
+
+        def sums(b, k, lo, hi):
+            done[b] += 1
+            mm(R("pK%d" % b, k, 128, 16, hi - lo), R("MN", lo, hi), R("KEY8", 0, 8), False,
+               done[b] == (32 if u == 2 and b else 16))
+
+        def minima(k, gathers):
+            lo, hi = span(0, k, 1)
+            if gathers:
+                tt(R("MN", lo, hi), listing(0, k, 1), R(src, x, x + nl), O.min)
+            elif k >= 16 - AHEAD[u]:
+                tt(R("MN", lo + n0, hi), R("G", lo + n0, hi), R(pC, n0, nl), O.min)
+                return sums(1, k, lo + n0, hi)
+            else:
+                tt(R("MN", lo, hi), R("G", lo, hi), R(pC, 0, nl), O.min)
+            sums(1, k, lo + n0, hi)
+            sums(0, k, lo, lo + n0)
+
+        def port_minima(k, gathers):
+            at = 16 * pad + 128 * k
+            if gathers:
+                tt(R("MN", at + 128 - LP, at + 128), listing(1, k, 1), R("land", 0, LP), O.min)
+            else:
+                tt(R("MN", at + 128 - LP, at + 128), R("G", *span(1, k, 1)), R(pC, nl, nl + LP), O.min)
+            sums(1, k, at, at + 128)
+
+        def own(at, name, lo, hi):
+            mm(R(pC, at, at + hi - lo), IDN, R(name, lo, hi), True, True)
+
+        nf, npf, done = ORDER[u].count("F"), ORDER[u].count("f"), [0, 0]
+        theirs = [(0, nf + sum(CALLS[u][:i]), nk) for i, nk in enumerate(CALLS[u])]
+        theirs += [(1, npf + sum(PORT_CALLS[:i]), nk) for i, nk in enumerate(PORT_CALLS) if u == 2]
+        if u == 2:
+            keep(R("OW2", 0, nl), R("C", 1856, 1856 + nl), [[0, nl]], O.is_gt, 0.0, 1, 0)
+        for p, k, nk in theirs:
+            act(R("G", *span(p, k, nk)), listing(p, k, nk), AF.Copy)
         if u == 2:
             new_counts(1)
             send()
-            number(1)
         if u == 3:
             new_counts(2)
-        for b, nl in enumerate(CHUNKS[u]):
-            mm(R("pK%d" % b, 0, 128, 1, nl), R("ONEB", 0, nl, 1, 1), R("BIAS", 0, 128, 1, 1), True, False)
-        if u == 1:
-            mm(R("pC0", 0, L), R("IDN", 0, 128), R("CY0", 0, L), True, False)
-            mm(R("pC0", 0, L), R("NEG", 0, 128), R("RE0", 0, L), False, False)
-            for i in range(16):
-                mm(R("pC0", i, L, 16), R("RSEL", 128 * i, 128 * i + 128), R("KILL", 0, nt), False, i == 15)
-            spread_numbers(0)
-        else:
-            src, x = (("C", 1680), None, ("C", 1856), ("CN2", 0))[u]
-            for d in range(rep):
-                mm(R("pC0", d, rep * n0, rep), R("IDN", 0, 128), R(src, x, x + n0), True, True)
-            end = min(L, LE)
-            mm(R(own[1][0], own[1][1], own[1][1] + end - n0), R("IDN", 0, 128), R(src, x + n0, x + end), True, True)
-        if u == 2:
-            act(R("pC1", LE - n0, n1), R("land", 0, LP), AF.Copy)
-            spread_numbers(1)
-        gather("V", n0 - h0, n0)
-        gather("V", L - h2, L)
-        if u == 0:
-            act(R("BB1", 0, 128), R("BONES", 0, 128), AF.Copy)
-            act(R("BONB", 0, 128), R("BONES", 0, 128), AF.Copy, 0.5)
-            convert("C", 0, "CI", 0, 1680)
-            convert("C", 1856, "CI", 1856, B)
-        if u == 1:
-            sources(0)
-        if u == 2:
-            store("S", "yc", TOP, R("CN1", 0, M))
-            sources(1)
-            fetch(R("SN1", 0, M), "SY1", 1)
-            store("S", "ys", TOP - 1680, R("SN1", 0, M))
-        if u == 3:
             store("S", "yc", TOP + M, R("CN2", 0, M))
-
-        def keys(b, k):
-            nl, l0, r = CHUNKS[u][b], b * n0, (rep, 1)[b]
-            a = 16 * l0 + k * r * nl
-            tt(R("MN", a, a + r * nl), R("G", 16 * l0 + k, 16 * (l0 + nl), 16 // r), own[b], O.min)
-            for d in range(r):
-                mm(R("pK%d" % b, k + d * 16 // r, 128, 16, nl), R("MN", a + d, a + r * nl, r), R("KEY8", 0, 8),
-                   False, k == 16 // r - 1 and d == r - 1)
+        later("G")
+        for b, (lo, hi) in enumerate(((0, n0), (n0, L))):
+            K = R("pK%d" % b, 0, 128, 1, hi - lo)
+            if u == 1:
+                mm(K, R("FM", lo, hi), R("NBK", 0, 128), True, False)
+                mm(K, R("ONEB", 0, hi - lo, 1, 1), R("ROWS", 640, 768, 1, 1), False, False)
+            mm(K, R("ONEB", 0, hi - lo, 1, 1), R("BIAS", 0, 128, 1, 1), u != 1, False)
+        own(0, src, x, x + nl)
+        turn_of = {"F": 0, "m": nf, "f": 0, "p": npf}
+        for i, call in enumerate(ORDER[u]):
+            if call == "f" and turn_of["f"] == 0:
+                own(nl, "land", 0, LP)
+            (port_minima if call in "fp" else minima)(turn_of[call], call in "fF")
+            turn_of[call] += 1
+            if i == 1 and u == 1:
+                mm(R("pK1", 0, 128), R("CAP", n0, L), R("NBK", 0, 128), False, False)
+        for k in range(16 - AHEAD[u], 16):
+            tt(R("MN", k * pad, k * pad + n0), R("G", k * pad, k * pad + n0), R(pC, 0, n0), O.min)
+            sums(0, k, k * pad, k * pad + n0)
+        if u:
+            spread_numbers(u - 1)
 
         def best(b, part):
-            nl, l0 = CHUNKS[u][b], b * n0
+            nl = CHUNKS[u][b]
             K, X, H = "pK%d" % b, R("XB%d" % b, 0, 128, 1, nl), R("OH%d" % b, 0, 128, 1, nl)
             if part == 0:
                 scan(R(K, 128, 256, 1, nl), R("SEGK", 0, 128, 1, nl), R(K, 0, 128, 1, nl), big, O.min, O.max)
             elif part == 1:
-                scan(R(X[0], 0, 128, -1, nl), R("SEGK", 0, 128, 1, nl), R(K, 128, 256, -1, nl), big, O.min, O.max)
+                scan(R(X[0], 0, 128, -1, nl), R("SEGK", 128, 256, 1, nl), R(K, 0, 128, -1, nl), big, O.min, O.max)
             else:
-                tt(H, R(K, 0, 128, 1, nl), X, O.is_equal)
-
-        for k in range(16 // rep):
-            keys(0, k)
-            if k == MID[u]:
-                gather("V", L - h2 - h1, L - h2)
-
-        for k in range(16):
-            keys(1, k)
+                tt(H, R(K, 128, 256, 1, nl), X, O.is_equal)
 
         part = ((0, n0), (n0, L))
-        pO, pX, pY = ("pW", "pO"), ("pC0" if u == 1 else "pC1", "pX"), ("pW", "pK0")
+        pO, pX, pY = ("pW", "pO"), (pD, "pX"), ("pW", "pK0")
 
         def pick(b):
             lo, hi = part[b]
-            tt(R("PR", lo, hi), R(pO[b], lo, hi), R(SV, lo, hi), O.min)
-            mm(R(pX[b], lo, hi), R("BB1", 0, 128), R("PR", lo, hi), False, True)
+            tt(R("PR", lo, hi), R(pO[b], lo, hi), R(SV, lo, hi), O.max)
             mm(R(pY[b], 256 + lo, 256 + hi), R("BB1", 0, 128), R("PR", lo, hi), True, True)
-            act(R("YR", lo, hi), R(pY[b], 256 + lo, 256 + hi), AF.Identity, 1.0, 30720.0)
+            mm(R(pX[b], lo, hi), R("BB1", 0, 128), R("PR", lo, hi), False, True)
+            act(R("YR", lo, hi), R(pY[b], 256 + lo, 256 + hi), AF.Identity, 1.0, -30720.0)
 
         def listed(b):
             lo, hi = part[b]
-            scan(R("YX", lo, hi), R("SEGY", lo, hi), R(pX[b], lo, hi), big, O.min, O.max)
+            scan(R("YX", lo, hi), R("SEGY", lo, hi), R(pX[b], lo, hi), 0.0, O.max, O.min)
 
-        if u == 1:
-            act(R("M0", 0, L), R("pC0", 0, L), AF.Copy)
-        minus_own(0)
         for b, (lo, hi) in enumerate(part):
             row(pO[b], 0, lo, hi)
         for b in (1, 0):
             mm(R(pX[b], *part[b]), R("IDB", 0, 128), R("MASKC", *part[b]), True, False)
-        minus_own(1)
-        for i, place in enumerate("KFR"):
-            best(0, i)
-            later(place)
+        later("K")
+        lead, trail = (0, 1) if u == 2 else (1, 0)
+        for b, i in ((0, 0), (0, 1), (0, 2), (1, 0), (1, 1), (1, 2)) if u == 2 else ((1, 0), (1, 1), (0, 0), (0, 1), (1, 2), (0, 2)):
+            if u == 2 and (b, i) == (1, 2):
+                pick(0)
+            best(b, i)
             if i == 2:
-                turn(pO[0], u, 0, True)
-            best(1, i)
-        turn(pO[1], u, 1, True)
+                turn(pO[b], u, b, True, "NE4")
         later("O")
-        pick(0)
-        pick(1)
+        if u != 2:
+            pick(lead)
+        pick(trail)
         if u % 2 == 0:
             mm(R("pK1", 256, 272), R("ONEB", 0, 128, 1, 1), R("CU", 0, 16, 1, 1), True, False)
         later("P")
-        listed(0)
-        listed(1)
-        for b, (lo, hi) in enumerate(part):
-            act(R("DEAD", lo, hi), R(pY[b], 256 + lo, 256 + hi), AF.Relu, -big, -32767.0 * big)
-        later("Y")
-        act(R("YG", 0, nt), R("YX", 15, L, 16), AF.Relu, 1.0, HALF)
-        act(R("YF", 0, nt), R("YX", 15, L, 16), AF.Relu, 1.0, HALF)
-        act(R(CY, 0, L), IND(win, R("YG", 0, nt)), AF.Copy)
-        act(R(SY, 0, L), IND(R("SI", 0, wide), R("YG", 0, nt)), AF.Copy)
-        if u == 0:
-            act(R("SX1", 0, L), R(SY, 0, L), AF.Copy)
-            act(R("SV1", 0, L), R(SY, 0, L), AF.Identity, 1.0, -HALF)
-        if u == 1:
-            convert("SX2", 0, "SI", 1856, B)
+        listed(lead)
 
-        early = min(n0 // 16, EARLY)
-        apart = early == n0 // 16
-        pW, pW1 = "pO", "pW" if apart else "pO"
+        to = "pO"
+        mm(R(to, 0, L), R("IDF", 0, 128), R("OFFD", 0, L), True, False)
+        mm(R(to, 0, L), R("BB1", 0, 128), R("PR", 0, L), False, False)
 
-        def same(t, lo, hi, to, start, stop):
+        def same(t, lo, hi, stop=False):
             ts(R("EQ", 256 * t + lo, 256 * t + hi), R("YR", lo, hi), R("YX", 16 * t + 15, 16 * t + 16), O.is_equal,
-               R("WX", 16 * t + 15, 16 * t + 16), O.mult)
-            mm(R(to, lo, hi), R("BONB", 0, 128), R("EQ", 256 * t + lo, 256 * t + hi), start, stop)
+               4096.0, O.mult)
+            if lo == 16 * t:
+                mm(R(to, lo, lo + 16), R("L1N", 0, 128), R("EQ", 256 * t + lo, 256 * t + lo + 16), False, stop)
+                lo += 16
+            if lo < hi:
+                mm(R(to, lo, hi), R("BON1", 0, 128), R("EQ", 256 * t + lo, 256 * t + hi), False, stop)
 
-        def dead(to, lo, hi, stop):
-            mm(R(to, lo, hi), R("IDH", 0, 128), R("DEAD", lo, hi), False, stop)
+        def first():
+            ts(R("FM", 0, L), R(to, 0, L), float(SPARE), O.is_ge)
 
-        def first(to, lo, hi):
-            tt(R("FM", lo, hi), R(to, lo, hi), R("THR", lo, hi), O.is_ge)
+        def counted():
+            scan(R("RS", 16, 16 + L), R("ONEB", 0, L), R("FM", 0, L), 0.0, O.add, O.subtract)
 
-        def counted(lo, hi):
-            scan(R("RS", 16 + lo, 16 + hi), R("ONEB", lo, hi), R("FM", lo, hi), R("RS", 15 + lo, 16 + lo), O.add, O.subtract)
-            if u % 2:
-                scan(R("ZX", lo, hi), R("TS", lo, hi), R("FM", lo, hi), 0.0, O.max, O.mult)
+        def placed(lo=0, hi=L):
+            scan(R("ZX", lo, hi), R("TS", lo, hi), R(to, lo, hi), 0.0, O.max, O.min)
 
-        for t in range(early):
-            same(t, 16 * t, n0, pW, t == 0, False)
-        dead(pW, 0, n0, apart)
-        for t in range(nt):
-            same(t, max(16 * t, n0 if t < early else 0), L, pW1, apart and t == 0, t == nt - 1)
-            if t == 1:
-                dead(pW1, n0, L, False)
-        mm(R("pX", 0, 16), R("ONEB", 0, 128, 1, 1), R("CU", 16, 32, 1, 1), True, False)
-        mm(R(pD, 0, L), R("IDN", 0, 128), R(CY, 0, L), False, True)
-        act(R(RE, 0, L), R(pD, 0, L), AF.Relu)
-        if u == 1:
-            convert("SV2", 0, "SI", 1856, B, -HALF)
-        if apart:
-            first(pW, 0, n0)
+        def least_of_both():
+            tt(R(MU, 0, L), R(CY, 0, L), R(pC, 0, L), O.min)
+
+        if u == 2:
+            for t in range(n0 // 16):
+                same(t, 16 * t, n0)
+                if t == 1:
+                    listed(trail)
+            rest = [(t, max(16 * t, n0)) for t in range(nt)]
+        else:
+            listed(trail)
+            rest = [(t, 16 * t) for t in list(range(n0 // 16, nt - 1)) + list(range(n0 // 16)) + [nt - 1]]
+        act(R("YG", 0, nt), R("YX", 15, L, 16), AF.Identity, 1.0, HALF)
+        act(R(CY, 0, L), IND(win, R("YG", 0, nt)), AF.Copy)
+        if u == 0:
+            act(R("SV1", 0, L), IND(R("SI", 0, wide), R("YG", 0, nt)), AF.Identity, 1.0, -HALF)
+        later("Y")
+        if u:
+            act(R(SY, 0, L), IND(R("SI", 0, wide), R("YG", 0, nt)), AF.Copy)
+        for i, (t, lo) in enumerate(rest):
+            same(t, lo, L, i == len(rest) - 1)
+        if u:
+            mm(R("pX", 0, 16), R("ONEB", 0, 128, 1, 1), R("CU", 16, 32, 1, 1), True, False)
         later("E")
-        if apart:
-            counted(0, n0)
-        first(pW1, n0 if apart else 0, L)
-        later("L")
-        counted(n0 if apart else 0, L)
+        least_of_both()
+        if u == 0:
+            turned(1)
+            by_successor(1)
+            listed_successors(1)
         Z, U = R("pK1", 256, 256 + nt), R("pX", 0, nt)
         upto, before = R("RS", 31, 16 + L, 16), R("RS", 15, L, 16)
 
@@ -536,38 +568,65 @@ def rank_program(g, core, T, topo):
             for l1, l2 in (("L1N", "L2N"), ("NE4", "ID4")):
                 mm(U, R(l1, 0, 128), upto, False, False)
                 mm(U, R(l2, 0, 128), before, False, l2 == "ID4")
-        for call in ((ends, numbers), (numbers,), (numbers, ends), (numbers,))[u]:
-            call()
-        if u < 2:
-            mm(R("pO", 0, L), R("BONB", 0, 128), R("RS", 16, 16 + L), True, True)
-        later("S")
+
+        def along():
+            mm(R("pO", 0, L), R("BON1", 0, 128), R("RS", 16, 16 + L), True, True)
+            if u % 2 == 0:
+                act(R("CAP", n0, L), R("pO", n0, L), AF.Relu, 1.0, -float(M))
 
         def new_places():
             tt(R(LN, 0, nt), U, R("TR", 0, nt), O.min)
-        if u == 2:
-            new_places()
-        if u % 2:
-            Z = R("ZX", 15, L, 16)
-            tt(R("LY", 0, nt), Z, R("YF", 0, nt), O.max)
-        else:
-            tt(R("Z", 0, nt), Z, R("TR", 0, nt), O.min)
-        ts(R("KILL", 0, nt), Z, 0.5, O.is_gt, -65536.0, O.mult)
-        if u % 2 == 0:
-            tt(R("LY", 0, nt), R("YF", 0, nt), R("Z", 0, nt), O.max)
-        if u == 2:
-            new_links(2)
-            act(R("SX3", 0, M), R("SN2", 0, M), AF.Copy)
-            act(R("SV3", 0, M), R("SN2", 0, M), AF.Identity, 1.0, -HALF)
-            number(u)
-            spread_numbers(u)
-        if u == 0:
-            number(u)
-        if u % 2:
-            new_places()
-        cp(IND(R("C", 0, SPARE), R("LY", 0, nt)), R(RE, 0, L))
 
-    store("S", "yc", 0, R("C", 0, TOP))
-    number(3)
+        def what_stays(lo, hi):
+            tt(IND(R("C", 0, SPARE), R("LY", lo, hi)), R(CY, 16 * lo, 16 * hi), R(MU, 16 * lo, 16 * hi), O.subtract)
+
+        nm = M // 16
+
+        def places():
+            cp(R("LY", 0, min(nt, nm + u % 2)), R("ZX", 15, min(L, M + 16 * (u % 2)), 16))
+
+        if u == 2:
+            first()
+            placed(0, M)
+            counted()
+            places()
+            placed(M, L)
+            numbers()
+            ends()
+            along()
+            what_stays(0, 4)
+            new_places()
+            tt(R("Z", nm, nt), R("pK1", 256 + nm, 256 + nt), R("TR", nm, nt), O.min)
+            new_links(2)
+            act(R("SV3", 0, M), R("SN2", 0, M), AF.Identity, 1.0, -HALF)
+            tt(R("LY", nm, nt), R("ZX", M + 15, L, 16), R("Z", nm, nt), O.max)
+            what_stays(4, nm)
+            turned(3)
+            by_successor(3)
+            listed_successors(3)
+            what_stays(nm, nt)
+            continue
+        placed()
+        first()
+        places()
+        counted()
+        if u == 0:
+            ends()
+            along()
+            what_stays(0, nm)
+            ts(R("LY", nm, nt), R("pK1", 256 + nm, 256 + nt), R("ZX", L - 1, L), O.max, R("TR", nm, nt), O.min)
+            what_stays(nm, nt)
+        elif u == 1:
+            numbers()
+            along()
+            what_stays(0, nt)
+            new_places()
+        else:
+            numbers()
+            what_stays(0, nt)
+            store("S", "yc", 0, R("C", 0, TOP))
+            new_places()
+
     spread_numbers(3)
     new_counts(3)
     store("A", "yc", TOP + 2 * M, R("CN3", 0, M))

from concourse.mybir import AluOpType, ActivationFunctionType, AxisListType

B, LE, LP, M = 2112, 176, 80, 160
TOP = B + M
SPARE = TOP + 256
HALF = 1376.0
LOW = HALF + 15 * 2048
LANES = (176, 176, 256, 160)
WIDE = (B, B, B, TOP)
CHUNKS = ((48, 128), (48, 128), (128, 128), (32, 128))
WIDTH = ((176, 192), (176, 192), (176, 192), (160, 160))
PP = 96
ORDER = ("FFFFFmmmmFmmmmmm", "FFFFFmmmmFmmmmmm", "FFmmmmFFmmmFmmmm" + 4 * "f" + 12 * "p", "FFFFFmmmmFmmmmmm")
CALLS = ((4, 3, 2, 1), (4, 3, 2, 1), (4, 3, 2, 2), (4, 3, 2, 1))
PORT_CALLS = (6, 4, 2)
AHEAD = (4, 4, 0, 4)

SCRATCH = {}
PSUM = ("pK0", "pK1", "pC0", "pC1", "pO", "pX", "pW", "pN")
for _names, _w, _t in (
        ("CI", B, "int32"), ("SI", TOP, "int32"), ("PI PA PB", 1, "int32"), ("CE", 192, "int32"), ("OW0 OW2", 192, "float32"),
        ("C CN1 CN2 CN3", SPARE, "float32"), ("SN1", M, "float32"), ("SN2", M + SPARE, "float32"), ("SO", TOP - 1680, "float32"),
        ("G", 16 * (192 + PP), "float32"), ("MN", 16 * (192 + 128), "float32"), ("EQ", 4096, "bfloat16"), ("land", LP, "float32"),
        ("DEAD ONEB FM MASKC I256 CAP CNT", 256, "bfloat16"), ("JUNK", 10 * LE, "bfloat16"), ("RS", 272, "bfloat16"),
        ("CY0 CY1 CY2 CY3 SY0 SY1 SY2 SY3 M0 M1 M2 M3 YX SEGK SEGY TS ZX", 256, "float32"),
        ("PR YR OFFD SV0 SV1 SV2 SV3 XT0 XT1 XT2 XT3", 256, "float16"), ("LT0 LT1 LT2 LT3", 192 + PP, "uint16"), ("SW", 512, "float16"),
        ("OH0 OH1 NO0 NO1 IDB ID4 NE4 BON1 NB8 NBK BIAS L1A L2A L1N L2N", 128, "bfloat16"), ("BB1 IDF", 128, "float16"),
        ("ROWS", 768, "bfloat16"), ("CU", 32, "bfloat16"), ("IDW", 160, "float32"),
        ("XB0 XB1 BH BONES B4 LA LB", 128, "float32"), ("ONEF", 160, "float32"),
        ("YF Z TR JB SUMS FULL T16", 16, "float32"),
        ("YG LY LN1 LN2 LN3 FROM0 FROM1", 16, "uint16"),
        ("KEY8", 8, "float32"), ("PF H0 H1", 1, "float32")):
    for _n in _names.split():
        SCRATCH[_n] = ("sbuf", [128, _w], _t)
for _n in PSUM:
    SCRATCH[_n] = ("psum", [128, 512], "float32")
NDMA = 18
SEMAPHORES = ["qV", "qA", "qP", "qG", "snt", "arr"] + ["d%d" % _i for _i in range(NDMA)]


def R(name, lo, hi, step=1, p=128):
    return (name, lo, hi, step, p)


def IND(win, off):
    return ("@", win, off)


def machine(g, T):
    queue = {"V": g.vector, "A": g.scalar, "P": g.tensor, "G": g, "S": g.sync}
    count = {"V": 0, "A": 0, "P": 0, "G": 0}
    known = {"V": {}, "A": {}, "P": {}, "G": {}, "S": {}}
    clock = {}
    log = {}
    ndma = [0]

    def ap(r):
        if not isinstance(r, tuple):
            return r
        if r[0] == "@":
            return ap(r[1]).indirect(ap(r[2]))
        name, lo, hi, step, p = r
        if step == -1:
            return T[name][0:p, hi - 1::-1] if lo == 0 else T[name][0:p, hi - 1:lo - 1:-1]
        if step == 1:
            return T[name][0:p, lo:hi]
        return T[name][0:p, lo:hi:step]

    def spread(items):
        out = []
        for r in items:
            if not isinstance(r, tuple):
                continue
            if r[0] == "@":
                out.append(r[1])
                out.append(r[2])
            else:
                out.append(r)
        return out

    def needs(q, reads, writes, compute):
        need = {}
        for kind, items in (("r", reads), ("w", writes)):
            for r in items:
                name, lo, hi = r[0], r[1], r[2]
                psum = name in PSUM
                for (l2, h2, k2, ch, val, q2, c2) in log.get(name, []):
                    same = q2 == q and c2 and compute
                    over = lo < h2 and l2 < hi
                    if psum and not same:
                        hit = True
                    elif not over or (kind == "r" and k2 == "r"):
                        hit = False
                    elif same:
                        hit = q != "P" and k2 == "w"
                    else:
                        hit = True
                    if hit:
                        need[ch] = max(need.get(ch, 0), val)
        return need

    def wait(q, need):
        todo = {ch: v for ch, v in need.items() if known[q].get(ch, 0) < v}
        for ch, v in todo.items():
            if not any(c2 != ch and clock[(c2, v2)].get(ch, 0) >= v for c2, v2 in todo.items()):
                queue[q].wait_ge(T.sem[ch], v)
        for ch, v in todo.items():
            for c2, v2 in clock[(ch, v)].items():
                if known[q].get(c2, 0) < v2:
                    known[q][c2] = v2

    def record(q, ch, val, reads, writes, compute):
        snap = dict(known[q])
        if compute:
            for c2, v2 in clock.get((ch, val - 1), {}).items():
                if snap.get(c2, 0) < v2:
                    snap[c2] = v2
        snap[ch] = val
        clock[(ch, val)] = snap
        for kind, items in (("r", reads), ("w", writes)):
            for r in items:
                name, lo, hi, full = r[0], r[1], r[2], abs(r[3]) == 1 and r[4] == 128
                old = log.get(name, [])
                if name in PSUM:
                    old = [a for a in old if a[5] == q]
                if kind == "w" and full:
                    old = [a for a in old if not (lo <= a[0] and a[1] <= hi)]
                log[name] = old + [(lo, hi, kind, ch, val, q, compute)]

    def op(q, call, out, reads, also=()):
        rd = spread(reads)
        wr = [out] + list(also)
        if out[0] == "@":
            wr = [(out[1][0], out[1][1], out[1][2], 2, 128)]
            rd.append(out[2])
        wait(q, needs(q, rd, wr, True))
        count[q] += 1
        ch = "q" + q
        call(queue[q]).then_inc(T.sem[ch], 1)
        record(q, ch, count[q], rd, wr, True)

    def dma(q, out, in_, reads, writes):
        wait(q, needs(q, reads, writes, False))
        ch = "d%d" % ndma[0]
        ndma[0] += 1
        queue[q].dma_start(out, in_).then_inc(T.sem[ch], 16)
        record(q, ch, 16, reads, writes, False)

    m = {"ap": ap, "dma": dma}
    m["cp"] = lambda out, a: op("V", lambda e: e.tensor_copy(ap(out), ap(a)), out, [a])
    m["tt"] = lambda out, a, b, o: op("V", lambda e: e.tensor_tensor(ap(out), ap(a), ap(b), o), out, [a, b])
    m["blocks"] = lambda out, a: op("V", lambda e: e.transpose(ap(out), ap(a)), out, [a])

    def ts(out, a, s1, o0, s2=None, o1=None):
        if o1 is None:
            op("V", lambda e: e.tensor_scalar(ap(out), ap(a), ap(s1), None, o0), out, [a, s1])
        else:
            op("V", lambda e: e.tensor_scalar(ap(out), ap(a), ap(s1), ap(s2), o0, o1), out, [a, s1, s2])
    m["ts"] = ts
    m["fill"] = lambda out, c: op("V", lambda e: e.memset(ap(out), c), out, [])
    m["scan"] = lambda out, a, b, i, o0, o1: op(
        "V", lambda e: e.tensor_tensor_scan(ap(out), ap(a), ap(b), ap(i), o0, o1), out, [a, b, i])
    m["iota"] = lambda out, pat, base, cm, small: op(
        "G", (lambda e: e.iota(ap(out), pat, base, cm, allow_small_or_imprecise_dtypes=True)) if small else
        (lambda e: e.iota(ap(out), pat, base, cm)), out, [])
    m["keep"] = lambda out, a, pat, cond, other, base, cm: op(
        "G", lambda e: e.affine_select(ap(out), ap(a), pat, cond, other, base, cm), out, [a])
    m["mm"] = lambda out, l, r, start, stop: op(
        "P", lambda e: e.matmul(ap(out), ap(l), ap(r), start, stop), out, [l, r])
    m["act"] = lambda out, a, func, scale=1.0, bias=0.0: op(
        "A", lambda e: e.activation(ap(out), ap(a), func, bias=bias, scale=ap(scale)), out, [a, scale])
    m["signs"] = lambda total, out, a, bias: op(
        "A", lambda e: e.activation(ap(out), ap(a), ActivationFunctionType.Sign, bias=ap(bias), scale=-1.0,
                                    accum_out=ap(total)), out, [a, bias], [total])

    def remote(call, reads, local, n):
        wait("G", needs("G", reads, [], False))
        call()
        record("G", local, n, reads, [], False)
    m["remote"] = remote

    def landed(name, lo, hi, ch, n):
        clock[(ch, n)] = {ch: n}
        log[name] = [(lo, hi, "w", ch, n, "far", False)]
    m["landed"] = landed

    def finish(n):
        need = {"q" + q: count[q] for q in count}
        for i in range(ndma[0]):
            need["d%d" % i] = 16
        need["snt"] = n
        for ch, v in need.items():
            if known["G"].get(ch, 0) < v:
                g.wait_ge(T.sem[ch], v)
    m["finish"] = finish
    return m


def rank_program(g, core, T, topo):
    rank = T.rank_of(core)
    if rank is None:
        return
    O, AF = AluOpType, ActivationFunctionType
    m = machine(g, T)
    cp, tt, ts, fill, scan, mm, act, dma, iota, keep, blocks = (
        m["cp"], m["tt"], m["ts"], m["fill"], m["scan"], m["mm"], m["act"], m["dma"], m["iota"], m["keep"], m["blocks"])
    n = len(T.cores)
    nxt, prv = T.cores[(rank + 1) % n], T.cores[(rank - 1) % n]
    sent = len(topo.engines(core, nxt))
    m["landed"]("land", 0, LP, "arr", len(topo.engines(prv, core)))
    IDN = R("IDW", 16, 144)

    def load(q, to, src, lo, hi, after=()):
        dma(q, T[to][:, lo:hi], T[src][:, lo:hi], list(after), [R(to, lo, hi)])
    load("A", "SI", "s0", 1680, 1872)
    dma("S", T.CE[:, 0:192], T.c0[:, 1680:1872], [], [R("CE", 0, 192)])
    load("S", "CI", "c0", 0, B)
    load("S", "SI", "s0", 1872, B, [R("CI", 0, B)])
    load("S", "SI", "s0", 0, 1680)

    def turned(u):
        wide = max(WIDTH[u][1], LANES[u])
        blocks(R("XT%d" % u, 0, wide), R("SV%d" % u, 0, wide))

    def by_successor(u, lo=0, hi=None, ports=False):
        bank, nb, t0 = ("pN", PP // 16, LE // 16) if ports else ("pK0", WIDTH[u][1] // 16, 0)
        for i in range(nb)[lo:hi]:
            t = min(t0 + i, 15)
            for h in range(2):
                a, s = 32 * (t // 2) + 16 * h, 256 * (t % 2) + 128 * h
                mm(R(bank, i, 16 * nb, nb), R("SW", s, s + 128), R("XT%d" % u, a, a + 16), i == 0 and h == 0,
                   h == 1 and i == nb - 1)

    def listed_successors(u, ports=False):
        bank, at, wide = ("pN", WIDTH[u][1], PP) if ports else ("pK0", 0, WIDTH[u][1])
        act(R("LT%d" % u, at, at + wide), R(bank, 0, wide), AF.Identity, 1.0, HALF)

    big = float(2 ** 60)
    fill(R("ONEF", 0, 160), 1.0)
    iota(R("PI", 0, 1), [[0, 1]], 0, 1, False)
    keep(R("IDW", 0, 160), R("ONEF", 0, 160), [[-1, 160]], O.is_equal, 0.0, 16, 1)
    keep(R("BH", 0, 128), R("ONEF", 0, 128), [[-16, 8], [0, 16]], O.is_ge, 0.0, 0, 1)
    keep(R("BONES", 0, 128), R("BH", 0, 128), [[16, 8], [0, 16]], O.is_ge, 0.0, 15, -1)
    iota(R("BIAS", 0, 128), [[0, 8], [-1, 16]], 15, 0, True)
    iota(R("T16", 0, 16), [[16, 16]], 0, 0, True)
    iota(R("I256", 0, 256), [[0, 16], [1, 16]], 0, 0, True)
    fill(R("SEGK", 0, 256), big)
    ts(R("PB", 0, 1), R("PI", 0, 1), 4, O.arith_shift_right, 1, O.bitwise_and)
    fill(R("SEGY", 0, 256), -big)
    cp(R("H1", 0, 1), R("PB", 0, 1))
    fill(R("ONEB", 0, 256), 1.0)
    ts(R("H0", 0, 1), R("H1", 0, 1), -1.0, O.mult, 1.0, O.add)
    for tth, (lo, half) in enumerate(((16, "H0"), (0, "H0"), (32, "H1"), (16, "H1"))):
        act(R("SW", 128 * tth, 128 * tth + 128), R("IDW", lo, lo + 128), AF.Copy, R(half, 0, 1))
    ts(R("PA", 0, 1), R("PI", 0, 1), 15, O.bitwise_and)
    fill(R("SEGK", 0, 128, 16), 2 ** 20 - 0.5)
    fill(R("SEGK", 128, 256, 16), 2 ** 20 - 0.25)
    cp(R("PF", 0, 1), R("PA", 0, 1))
    ts(R("SV0", 0, 192), R("SI", 1680, 1872), -HALF, O.add)
    fill(R("SEGY", 0, 256, 16), B - 0.75 - HALF)
    turned(0)
    by_successor(0, 0, 12)
    fill(R("TS", 0, 256), 0.0)
    fill(R("RS", 0, 16), 0.0)
    fill(R("CU", 0, 16), 4096.0 * (255 - M + 1))
    fill(R("CU", 16, 32), 4096.0)
    fill(R("ROWS", 0, 128), 2048.0)
    fill(R("ROWS", 640, 768), 15.0 * 2 ** 25)
    cp(R("SV1", LE, LE + 16), R("ONEB", 0, 16))
    act(R("OW0", 0, 192), R("CE", 0, 192), AF.Copy)
    act(R("NE4", 0, 128), IDN, AF.Copy, -4096.0)
    act(R("IDB", 0, 128), IDN, AF.Copy)
    listed_successors(0)
    act(R("B4", 0, 128), R("BONES", 0, 128), AF.Copy, 4096.0)
    act(R("BB1", 0, 128), R("BONES", 0, 128), AF.Copy)
    act(R("BON1", 0, 128), R("BONES", 0, 128), AF.Copy)
    ts(R("KEY8", 0, 8), R("BONES", 0, 128, 16), 16.0, O.mult)
    ts(R("TR", 0, 16), R("T16", 0, 16), R("PF", 0, 1), O.add, float(TOP), O.add)
    ts(R("JB", 0, 16), R("T16", 0, 16), R("PF", 0, 1), O.add, 0.5, O.add)
    cp(R("TS", 0, 256, 16), R("TR", 0, 16))
    ts(R("MASKC", 0, 256), R("I256", 0, 256), R("PF", 0, 1), O.is_equal, -30720.0, O.mult)
    ts(R("CAP", 0, 256), R("I256", 0, 256), R("PF", 0, 1), O.not_equal, 4096.0, O.mult)
    act(R("OFFD", 0, 256), R("CAP", 0, 256), AF.Identity, 1.0, HALF - 30720.0)
    act(R("IDF", 0, 128), IDN, AF.Copy)
    keep(R("L1N", 0, 128), R("BONES", 0, 128), [[1, 128]], O.is_gt, 0.0, 0, -1)
    keep(R("LA", 0, 128), R("B4", 0, 128), [[1, 128]], O.is_gt, 0.0, 0, -1)
    keep(R("C", 0, B), R("CI", 0, B), [[0, B]], O.is_gt, 0.0, 1, 0)
    keep(R("LB", 0, 128), R("B4", 0, 128), [[-1, 128]], O.is_ge, 0.0, 0, 1)
    keep(R("L1A", 0, 128), R("LA", 0, 128), [[-1, 128]], O.not_equal, -255.0 * 4096, 0, 1)
    keep(R("L2A", 0, 128), R("LB", 0, 128), [[-1, 128]], O.not_equal, 256.0 * 4096, 0, 1)
    for name, lo, hi in (("M0", LE, LE + 16), ("SY0", LE, LE + 16), ("SY1", LE, LE + 16)):
        iota(R(name, lo, hi), [[0, hi - lo]], 0, 0, True)
    for u in range(4):
        iota(R("ROWS", 128 * u + 128, 128 * u + 256, 1, 2), [[0, 128]], B + M * u - 4096, 15 * 8192 - (B + M * u - 4096), True)
    keep(R("L2N", 0, 128), R("BONES", 0, 128), [[-1, 128]], O.is_ge, 0.0, 0, 1)
    for name, lo, hi in (("CN1", 0, M), ("MN", 16 * 192, 16 * (192 + 128)), ("CN2", 0, M), ("SN2", 0, 2 * M), ("CN3", 0, M)):
        iota(R(name, lo, hi), [[0, hi - lo]], 0, 0, True)

    NEWC = (None, R("CN1", 0, SPARE), R("CN2", 0, SPARE), R("CN3", 0, SPARE))
    NEWS = (None, None, R("SN2", 0, SPARE), R("SN2", M, M + SPARE))
    OLDS = (R("SI", 1680, 1856), R("SY0", 0, LE), R("SI", 1856, B), R("SN2", 0, M))
    OWN = (("OW0", 0), ("M0", 0), ("OW2", 0), ("CN2", 0))

    def new_counts(u):
        cp(IND(NEWC[u], R("LN%d" % u, 0, LANES[u] // 16)), R("M%d" % u, 0, LANES[u]))

    def new_links(u):
        cp(IND(NEWS[u], R("LN%d" % u, 0, LANES[u] // 16)), R("SY%d" % u, 0, LANES[u]))

    def sources():
        act(R("CNT", 0, LE), R("pO", 0, LE), AF.Copy)
        for t in range(M // 16):
            m["signs"](R("SUMS", t, t + 1), R("JUNK", LE * t + 16 * t, LE * t + LE), R("CNT", 16 * t, LE), R("JB", t, t + 1))

    def sources_below():
        tt(R("FULL", 0, M // 16), R("SUMS", 0, M // 16), R("T16", 0, M // 16), O.add)

    def sources_listed(u):
        act(R("FROM%d" % u, 0, M // 16), R("FULL", 0, M // 16), AF.Identity, 0.5, LE / 2.0)

    def fetch(to, src, u):
        act(to, IND(R(src, 0, LE + 16), R("FROM%d" % u, 0, M // 16)), AF.Copy)

    def turn(to, u, b, stop, by="ID4"):
        nl, l0 = CHUNKS[u][b], b * CHUNKS[u][0]
        mm(R(to, l0, l0 + nl), R("OH%d" % b, 0, 128, 1, nl), R(by, 0, nl, 1, nl), False, stop)

    def row(to, i, lo, hi, rows=1):
        mm(R(to, lo, hi), R("ROWS", 128 * i, 128 * i + 128, 1, rows), R("ONEB", lo, hi, 1, rows), True, False)

    def spread_numbers(u):
        L, n0 = LANES[u], CHUNKS[u][0]
        row("pN", u + 1, 0, L, 2)
        turn("pN", u, 0, False)
        turn("pN", u, 1, False)
        if u % 2 == 0:
            mm(R("pN", n0, L), R("NB8", 0, 128), R("CAP", n0, L), False, False)
        mm(R("pN", 0, L), R("NB8", 0, 128), R("FM", 0, L), False, False)
        mm(R("pN", 0, L), R("BON1", 0, 128), R("RS", 15, 15 + L), False, True)

    def change_links(u):
        tt(OLDS[u], OLDS[u], R("pN", 0, LANES[u]), O.max)

    def send():
        rid, pid = topo.addr(nxt)[:2]
        m["remote"](lambda: g.remote_dma(out_ap=T.land[:], in_ap=T.CN1[:, 0:LP], remote_sem=T.sem.arr,
                                         local_sem=T.sem.snt, pid=pid, routing_id=rid, dma_engine_mask=topo.mask(core, nxt)),
                    [R("CN1", 0, LP)], "snt", sent)

    def store(q, to, at, src, after=None):
        dma(q, T[to][:, at:at + src[2] - src[1]], T[src[0]][:, src[1]:src[2]], [src, after or src], [])

    def old_links_out(lo, hi):
        keep(R("SO", lo - 1680, hi - 1680), R("SI", lo, hi), [[0, hi - lo]], O.is_gt, 0.0, 1, 0)
        store("S", "ys", lo - 1680, R("SO", lo - 1680, hi - 1680))

    LATER = {
        0: {"G": [lambda: act(R("SV2", 0, 256), R("SI", 1856, B), AF.Identity, 1.0, -HALF),
                  lambda: act(R("NBK", 0, 128), R("BONES", 0, 128), AF.Copy, -float(2 ** 25)),
                  lambda: act(R("NB8", 0, 128), R("BONES", 0, 128), AF.Copy, -8192.0),
                  lambda: act(R("ID4", 0, 128), IDN, AF.Copy, 4096.0)],
            "K": [lambda: turned(2), lambda: by_successor(2, ports=True), lambda: listed_successors(2, True)]},
        1: {"G": [sources],
            "O": [lambda: change_links(0), lambda: old_links_out(1680, 1856)],
            "P": [sources_below],
            "Y": [lambda: sources_listed(0), lambda: fetch(R("C", B, TOP), "M0", 0)],
            "E": [lambda: by_successor(2), lambda: listed_successors(2)]},
        2: {"G": [lambda: act(R("SY0", 0, LE), R("SV1", 0, LE), AF.Identity, 1.0, HALF), sources], "O": [lambda: change_links(1)], "P": [sources_below],
            "E": [lambda: store("S", "yc", TOP, R("CN1", 0, M), R("YG", 0, 16))]},
        3: {"G": [lambda: fetch(R("SI", B, TOP), "SY0", 0), lambda: old_links_out(B, TOP),
                  lambda: sources_listed(1), lambda: fetch(R("SN1", 0, M), "SY1", 1),
                  lambda: store("S", "ys", TOP - 1680, R("SN1", 0, M))],
            "K": [lambda: fill(R("SN2", M, 256), 0.0), lambda: fill(R("SEGY", 0, M, 16), TOP - 0.75 - HALF)],
            "O": [lambda: change_links(2), lambda: old_links_out(1856, B)]},
    }

    for u in range(4):
        L, wide = LANES[u], WIDE[u]
        nt = L // 16
        n0, n1 = CHUNKS[u]
        win = R("C" if u else "CI", 0, wide)
        LT, SV, SY, CY, MU, LN = ("%s%d" % (a, u) for a in ("LT", "SV", "SY", "CY", "M", "LN"))
        pC, pD = "pC%d" % (u % 2), "pC%d" % (1 - u % 2)
        src, x = OWN[u]

        def later(place):
            for call in LATER[u].get(place, []):
                call()

        nl, pad = WIDTH[u]

        def span(ports, k, nk):
            if ports:
                return 16 * pad + k * PP, 16 * pad + (k + nk - 1) * PP + LP
            return k * pad, (k + nk - 1) * pad + nl

        def listing(ports, k, nk):
            lo, hi = span(ports, k, nk)
            return IND(win, R(LT, lo // 16, hi // 16))

        def sums(b, k, lo, hi):
            done[b] += 1
            mm(R("pK%d" % b, k, 128, 16, hi - lo), R("MN", lo, hi), R("KEY8", 0, 8), False,
               done[b] == (32 if u == 2 and b else 16))

        def minima(k, gathers):
            lo, hi = span(0, k, 1)
            if gathers:
                tt(R("MN", lo, hi), listing(0, k, 1), R(src, x, x + nl), O.min)
            elif k >= 16 - AHEAD[u]:
                tt(R("MN", lo + n0, hi), R("G", lo + n0, hi), R(pC, n0, nl), O.min)
                return sums(1, k, lo + n0, hi)
            else:
                tt(R("MN", lo, hi), R("G", lo, hi), R(pC, 0, nl), O.min)
            sums(1, k, lo + n0, hi)
            sums(0, k, lo, lo + n0)

        def port_minima(k, gathers):
            at = 16 * pad + 128 * k
            if gathers:
                tt(R("MN", at + 128 - LP, at + 128), listing(1, k, 1), R("land", 0, LP), O.min)
            else:
                tt(R("MN", at + 128 - LP, at + 128), R("G", *span(1, k, 1)), R(pC, nl, nl + LP), O.min)
            sums(1, k, at, at + 128)

        def own(at, name, lo, hi):
            mm(R(pC, at, at + hi - lo), IDN, R(name, lo, hi), True, True)

        nf, npf, done = ORDER[u].count("F"), ORDER[u].count("f"), [0, 0]
        theirs = [(0, nf + sum(CALLS[u][:i]), nk) for i, nk in enumerate(CALLS[u])]
        theirs += [(1, npf + sum(PORT_CALLS[:i]), nk) for i, nk in enumerate(PORT_CALLS) if u == 2]
        if u == 2:
            keep(R("OW2", 0, nl), R("C", 1856, 1856 + nl), [[0, nl]], O.is_gt, 0.0, 1, 0)
        for p, k, nk in theirs:
            act(R("G", *span(p, k, nk)), listing(p, k, nk), AF.Copy)
        if u == 2:
            new_counts(1)
            send()
        if u == 3:
            new_counts(2)
            store("S", "yc", TOP + M, R("CN2", 0, M))
        later("G")
        for b, (lo, hi) in enumerate(((0, n0), (n0, L))):
            K = R("pK%d" % b, 0, 128, 1, hi - lo)
            if u == 1:
                mm(K, R("FM", lo, hi), R("NBK", 0, 128), True, False)
                mm(K, R("ONEB", 0, hi - lo, 1, 1), R("ROWS", 640, 768, 1, 1), False, False)
            mm(K, R("ONEB", 0, hi - lo, 1, 1), R("BIAS", 0, 128, 1, 1), u != 1, False)
        own(0, src, x, x + nl)
        turn_of = {"F": 0, "m": nf, "f": 0, "p": npf}
        for i, call in enumerate(ORDER[u]):
            if call == "f" and turn_of["f"] == 0:
                own(nl, "land", 0, LP)
            (port_minima if call in "fp" else minima)(turn_of[call], call in "fF")
            turn_of[call] += 1
            if i == 1 and u == 1:
                mm(R("pK1", 0, 128), R("CAP", n0, L), R("NBK", 0, 128), False, False)
        for k in range(16 - AHEAD[u], 16):
            tt(R("MN", k * pad, k * pad + n0), R("G", k * pad, k * pad + n0), R(pC, 0, n0), O.min)
            sums(0, k, k * pad, k * pad + n0)
        if u:
            spread_numbers(u - 1)

        def best(b, part):
            nl = CHUNKS[u][b]
            K, X, H = "pK%d" % b, R("XB%d" % b, 0, 128, 1, nl), R("OH%d" % b, 0, 128, 1, nl)
            if part == 0:
                scan(R(K, 128, 256, 1, nl), R("SEGK", 0, 128, 1, nl), R(K, 0, 128, 1, nl), big, O.min, O.max)
            elif part == 1:
                scan(R(X[0], 0, 128, -1, nl), R("SEGK", 128, 256, 1, nl), R(K, 0, 128, -1, nl), big, O.min, O.max)
            else:
                tt(H, R(K, 128, 256, 1, nl), X, O.is_equal)

        part = ((0, n0), (n0, L))
        pO, pX, pY = ("pW", "pO"), (pD, "pX"), ("pW", "pK0")

        def pick(b):
            lo, hi = part[b]
            tt(R("PR", lo, hi), R(pO[b], lo, hi), R(SV, lo, hi), O.max)
            mm(R(pY[b], 256 + lo, 256 + hi), R("BB1", 0, 128), R("PR", lo, hi), True, True)
            mm(R(pX[b], lo, hi), R("BB1", 0, 128), R("PR", lo, hi), False, True)
            act(R("YR", lo, hi), R(pY[b], 256 + lo, 256 + hi), AF.Identity, 1.0, -30720.0)

        def listed(b):
            lo, hi = part[b]
            scan(R("YX", lo, hi), R("SEGY", lo, hi), R(pX[b], lo, hi), 0.0, O.max, O.min)

        for b, (lo, hi) in enumerate(part):
            row(pO[b], 0, lo, hi)
        for b in (1, 0):
            mm(R(pX[b], *part[b]), R("IDB", 0, 128), R("MASKC", *part[b]), True, False)
        later("K")
        lead, trail = (0, 1) if u == 2 else (1, 0)
        for b, i in ((0, 0), (0, 1), (0, 2), (1, 0), (1, 1), (1, 2)) if u == 2 else ((1, 0), (1, 1), (0, 0), (0, 1), (1, 2), (0, 2)):
            if u == 2 and (b, i) == (1, 2):
                pick(0)
            best(b, i)
            if i == 2:
                turn(pO[b], u, b, True, "NE4")
        later("O")
        if u != 2:
            pick(lead)
        pick(trail)
        if u % 2 == 0:
            mm(R("pK1", 256, 272), R("ONEB", 0, 128, 1, 1), R("CU", 0, 16, 1, 1), True, False)
        later("P")
        listed(lead)

        to = "pO"
        mm(R(to, 0, L), R("IDF", 0, 128), R("OFFD", 0, L), True, False)
        mm(R(to, 0, L), R("BB1", 0, 128), R("PR", 0, L), False, False)

        def same(t, lo, hi, stop=False):
            ts(R("EQ", 256 * t + lo, 256 * t + hi), R("YR", lo, hi), R("YX", 16 * t + 15, 16 * t + 16), O.is_equal,
               4096.0, O.mult)
            if lo == 16 * t:
                mm(R(to, lo, lo + 16), R("L1N", 0, 128), R("EQ", 256 * t + lo, 256 * t + lo + 16), False, stop)
                lo += 16
            if lo < hi:
                mm(R(to, lo, hi), R("BON1", 0, 128), R("EQ", 256 * t + lo, 256 * t + hi), False, stop)

        def first():
            ts(R("FM", 0, L), R(to, 0, L), float(SPARE), O.is_ge)

        def counted():
            scan(R("RS", 16, 16 + L), R("ONEB", 0, L), R("FM", 0, L), 0.0, O.add, O.subtract)

        def placed(lo=0, hi=L):
            scan(R("ZX", lo, hi), R("TS", lo, hi), R(to, lo, hi), 0.0, O.max, O.min)

        def least_of_both():
            tt(R(MU, 0, L), R(CY, 0, L), R(pC, 0, L), O.min)

        if u == 2:
            for t in range(n0 // 16):
                same(t, 16 * t, n0)
                if t == 1:
                    listed(trail)
            rest = [(t, max(16 * t, n0)) for t in range(nt)]
        else:
            listed(trail)
            rest = [(t, 16 * t) for t in list(range(n0 // 16, nt - 1)) + list(range(n0 // 16)) + [nt - 1]]
        act(R("YG", 0, nt), R("YX", 15, L, 16), AF.Identity, 1.0, HALF)
        act(R(CY, 0, L), IND(win, R("YG", 0, nt)), AF.Copy)
        if u == 0:
            act(R("SV1", 0, L), IND(R("SI", 0, wide), R("YG", 0, nt)), AF.Identity, 1.0, -HALF)
        later("Y")
        if u:
            act(R(SY, 0, L), IND(R("SI", 0, wide), R("YG", 0, nt)), AF.Copy)
        for i, (t, lo) in enumerate(rest):
            same(t, lo, L, i == len(rest) - 1)
        if u:
            mm(R("pX", 0, 16), R("ONEB", 0, 128, 1, 1), R("CU", 16, 32, 1, 1), True, False)
        later("E")
        least_of_both()
        if u == 0:
            turned(1)
            by_successor(1)
            listed_successors(1)
        Z, U = R("pK1", 256, 256 + nt), R("pX", 0, nt)
        upto, before = R("RS", 31, 16 + L, 16), R("RS", 15, L, 16)

        def ends():
            mm(Z, R("L1A", 0, 128), upto, False, False)
            mm(Z, R("L2A", 0, 128), before, False, True)

        def numbers():
            for l1, l2 in (("L1N", "L2N"), ("NE4", "ID4")):
                mm(U, R(l1, 0, 128), upto, False, False)
                mm(U, R(l2, 0, 128), before, False, l2 == "ID4")

        def along():
            mm(R("pO", 0, L), R("BON1", 0, 128), R("RS", 16, 16 + L), True, True)
            if u % 2 == 0:
                act(R("CAP", n0, L), R("pO", n0, L), AF.Relu, 1.0, -float(M))

        def new_places():
            tt(R(LN, 0, nt), U, R("TR", 0, nt), O.min)

        def what_stays(lo, hi):
            tt(IND(R("C", 0, SPARE), R("LY", lo, hi)), R(CY, 16 * lo, 16 * hi), R(MU, 16 * lo, 16 * hi), O.subtract)

        nm = M // 16

        def places():
            cp(R("LY", 0, min(nt, nm + u % 2)), R("ZX", 15, min(L, M + 16 * (u % 2)), 16))

        if u == 2:
            first()
            placed(0, M)
            counted()
            places()
            placed(M, L)
            numbers()
            ends()
            along()
            what_stays(0, 4)
            new_places()
            tt(R("Z", nm, nt), R("pK1", 256 + nm, 256 + nt), R("TR", nm, nt), O.min)
            new_links(2)
            act(R("SV3", 0, M), R("SN2", 0, M), AF.Identity, 1.0, -HALF)
            tt(R("LY", nm, nt), R("ZX", M + 15, L, 16), R("Z", nm, nt), O.max)
            what_stays(4, nm)
            turned(3)
            by_successor(3)
            listed_successors(3)
            what_stays(nm, nt)
            continue
        placed()
        first()
        places()
        counted()
        if u == 0:
            ends()
            along()
            what_stays(0, nm)
            ts(R("LY", nm, nt), R("pK1", 256 + nm, 256 + nt), R("ZX", L - 1, L), O.max, R("TR", nm, nt), O.min)
            what_stays(nm, nt)
        elif u == 1:
            numbers()
            along()
            what_stays(0, nt)
            new_places()
        else:
            numbers()
            what_stays(0, nt)
            store("S", "yc", 0, R("C", 0, TOP))
            new_places()

    spread_numbers(3)
    new_counts(3)
    store("A", "yc", TOP + 2 * M, R("CN3", 0, M))
    new_links(3)
    change_links(3)
    store("A", "ys", TOP + M - 1680, R("SN2", 0, 2 * M))
    m["finish"](sent)
